import numpy as np
import ml_dtypes


def mxq(x, axis, fmt="e4m3"):
    dtype, down = {"e4m3": (ml_dtypes.float8_e4m3fn, 7), "e5m2": (ml_dtypes.float8_e5m2, 14)}[fmt]
    v = np.moveaxis(np.asarray(x, np.float32).astype(ml_dtypes.bfloat16).astype(np.float64), axis, -1)
    blocks = v.reshape(v.shape[:-1] + (-1, 32))
    amax = np.abs(blocks).max(-1, keepdims=True)
    byte = np.maximum(np.where(amax > 0, np.frexp(amax)[1] - 1 + 127, 0) - down, 1)
    scale = np.exp2(byte - 127.0)
    codes = (blocks / scale).astype(np.float32).astype(dtype).astype(np.float64)
    return np.moveaxis((codes * scale).reshape(v.shape), -1, axis)


WIDE = False


def mx_kscale(k):
    if not WIDE:
        return np.ones(k)
    levels = np.array([10, -10, 5, -5, 0])
    if k % 512:
        return np.exp2(np.random.permutation(np.resize(levels, k // 32))).repeat(32)
    a = np.empty((k // 512, 16))
    for p in range(k // 512):
        a[p, :8] = np.random.permutation(np.resize(levels, 8))
        for g in range(8):
            far = levels[np.abs(levels - a[p, g]) >= 10]
            a[p, g + 8] = far[np.random.randint(len(far))]
    return np.exp2(a.ravel()).repeat(32)


def f64(x):
    return np.asarray(x).astype(np.float64)


def striped(idx):
    return np.tile(idx.reshape(-1, 16).T, (8, 1)).astype(np.uint16)


def unstriped(offs):
    return offs[:16].T.reshape(-1).astype(np.int64)


E2M1 = np.array([0.0, 0.5, 1.0, 1.5, 2.0, 3.0, 4.0, 6.0, -0.0, -0.5, -1.0, -1.5, -2.0, -3.0, -4.0, -6.0])


def pack_weight(w, fmt):
    k, n = w.shape
    w = f64(np.asarray(w, np.float32).astype(ml_dtypes.bfloat16)).reshape(k // 32, 32, n)
    amax = np.abs(w).max(1)
    if fmt == "e4m3":
        byte = np.frexp(amax)[1] - 1 + 127 - 7
    else:
        mant, ex = np.frexp(amax / 6.0)
        byte = np.where(mant > 0.5, ex, ex - 1) + 127
    byte = np.clip(np.where(amax > 0, byte, 1), 1, 254)
    scaled = (w * np.exp2(127.0 - byte)[:, None, :]).reshape(k, n).astype(np.float32)
    by_word = np.ascontiguousarray(scaled.reshape(k // 512, 128, 4, n).transpose(0, 1, 3, 2))
    if fmt == "e4m3":
        words = by_word.astype(ml_dtypes.float8_e4m3fn).view(np.uint8)
    else:
        c = by_word.astype(ml_dtypes.float4_e2m1fn).view(np.uint8) & 0xF
        words = (c[..., 0::2] | (c[..., 1::2] << 4)).reshape(k // 512, 128, 2 * n)
    return np.ascontiguousarray(words), np.ascontiguousarray(byte.astype(np.uint8).reshape(k // 512, 16, n))


def unpack_weight(words, scales, fmt):
    g, _, n = scales.shape
    words = np.ascontiguousarray(words).reshape(g, 128, n, -1)
    if fmt == "e4m3":
        vals = words.view(ml_dtypes.float8_e4m3fn).astype(np.float64)
    else:
        nib = np.empty((g, 128, n, 4), np.uint8)
        nib[..., 0::2] = words & 0xF
        nib[..., 1::2] = words >> 4
        vals = E2M1[nib]
    vals = vals * np.repeat(np.exp2(scales.astype(np.float64) - 127.0), 8, axis=1)[..., None]
    return vals.transpose(0, 1, 3, 2).reshape(g * 512, n)


def gelu(v):
    return 0.5 * v * (1.0 + np.tanh(np.sqrt(2.0 / np.pi) * (v + 0.044715 * v**3)))


def bf(x):
    return np.asarray(x, np.float32).astype(ml_dtypes.bfloat16)

def planes(Y):
    n, m = Y.shape
    b = f64(bf(Y)).reshape(n // 32, 32, m)
    amax = np.abs(b).max(1)
    byte = np.clip(np.where(amax > 0, np.frexp(amax)[1] - 1 + 127 - 7, 1), 1, 254)
    codes = (b * np.exp2(127.0 - byte)[:, None, :]).reshape(n, m).astype(np.float32).astype(ml_dtypes.float8_e4m3fn).view(np.uint8)
    words = codes.reshape(n // 512, 128, 4, m).transpose(0, 1, 3, 2)
    return np.ascontiguousarray(words), np.ascontiguousarray(byte.astype(np.uint8).reshape(n // 512, 16, m))


K, K2, H, N, T, T2, S = 1024, 512, 1024, 512, 4096, 2048, 1024

def setup_inputs():
    n = np.random.standard_normal
    s = mx_kscale(K)[:, None]
    s2 = mx_kscale(K2)[:, None]
    u = mx_kscale(H)[:, None]
    tab_words, tab_scales = pack_weight(n((K, T)) * s, "e4m3")
    tab2_words, tab2_scales = pack_weight(n((K2, T2)) * s2, "e4m3")
    wp = (n((K, H)) / np.sqrt(K) / s * u.T).astype(np.float32)
    wd_words, wd_scales = pack_weight(n((K2, H)) / np.sqrt(K2) / s2, "e2m1")
    wo_words, wo_scales = pack_weight(n((H, N)) / np.sqrt(H) / u, "e4m3")
    return {"tab_words": tab_words, "tab_scales": tab_scales,
            "tab2_words": tab2_words, "tab2_scales": tab2_scales,
            "offs": striped(np.random.permutation(T)[:S]),
            "offs2": striped(np.random.permutation(T2)[:S]),
            "wp": wp, "wd_words": wd_words, "wd_scales": wd_scales,
            "tv": np.exp(0.4 * n((H, S))).astype(np.float32),
            "wo_words": wo_words, "wo_scales": wo_scales,
            "bo": (0.5 * n(N)).astype(np.float32),
            "cost": np.exp(0.8 * n(N)).astype(np.float32)}

def reference(tab_words, tab_scales, tab2_words, tab2_scales, offs, offs2, wp, wd_words, wd_scales, tv, wo_words, wo_scales, bo, cost):
    v = unpack_weight(tab_words, tab_scales, "e4m3")[:, unstriped(offs)]
    v2 = unpack_weight(tab2_words, tab2_scales, "e4m3")[:, unstriped(offs2)]
    wd = unpack_weight(wd_words, wd_scales, "e2m1")
    wo = unpack_weight(wo_words, wo_scales, "e4m3")
    a = mxq(f64(wp), 0, "e4m3").T @ v
    b = wd.T @ v2
    h = a * b * f64(tv)
    z = (wo.T @ mxq(h, 0, "e4m3")) + f64(bo)[:, None]
    y = f64(cost)[:, None] * (1.0 / (1.0 + np.exp(-z)))
    words, scales = planes(y)
    return y, words, scales

@@ -1,0 +1,259 @@
+from contextlib import ExitStack
+
+import concourse.mybir as mybir
+
+K, K2, H, N, T, T2, S = 1024, 512, 1024, 512, 4096, 2048, 1024
+FLOPS = 2 * S * (K * H + K2 * H + H * N)
+
+F32 = mybir.dt.float32
+BF16 = mybir.dt.bfloat16
+I32 = mybir.dt.int32
+U32 = mybir.dt.uint32
+U16 = mybir.dt.uint16
+U8 = mybir.dt.uint8
+FP8X4 = mybir.dt.float8_e4m3fn_x4
+FP4X4 = mybir.dt.float4_e2m1fn_x4
+MULT = mybir.AluOpType.mult
+SIGMOID = mybir.ActivationFunctionType.Sigmoid
+COPY = mybir.ActivationFunctionType.Copy
+
+P = 128
+PACK = 4
+PASS = P * PACK
+HALF = 512
+NARROW = 128
+CHUNK = 256
+TAB_ROW = 8
+WO_ROW = 4
+
+
+def tile_list_visit_risk_burden_kernel(
+    tc, tab_words, tab_scales, tab2_words, tab2_scales, offs, offs2, wp, wd_words, wd_scales,
+    tv, wo_words, wo_scales, bo, cost, out_0, out_1, out_2,
+):
+    nc = tc.nc
+    with ExitStack() as ctx:
+        keep = ctx.enter_context(tc.tile_pool(name="keep", bufs=1))
+        ring = ctx.enter_context(tc.tile_pool(name="ring", bufs=3))
+        psum_b = ctx.enter_context(tc.psum_pool(name="psum_b", bufs=3))
+        psum_a = ctx.enter_context(tc.psum_pool(name="psum_a", bufs=3))
+        psum_z = ctx.enter_context(tc.psum_pool(name="psum_z", bufs=2))
+
+        def held(name, shape, dtype):
+            return keep.tile(shape, dtype, name=name, align_bytes=64)
+
+        list1 = held("list1", [P, S // 16], U16)
+        list2 = held("list2", [P, S // 16], U16)
+        tab_w = [held("tab_w%d" % a, [P, T], U32) for a in range(2)]
+        tab_s = held("tab_s", [P, T], U8)
+        tab2_w = held("tab2_w", [P, T2], U32)
+        tab2_s = held("tab2_s", [P, T2], U8)
+        v_w = [[held("v_w%d%d" % (a, f), [P, HALF], U32) for f in range(2)] for a in range(2)]
+        v_s = held("v_s", [P, S], U8)
+        v2_w = [held("v2_w%d" % f, [P, HALF], U32) for f in range(2)]
+        v2_s = held("v2_s", [P, S], U8)
+        wd_raw = held("wd_raw", [P, 2 * H], U8)
+        wd_w = held("wd_w", [P, 2 * H], U8)
+        wd_s_raw = held("wd_s_raw", [P, H], U8)
+        wd_s = held("wd_s", [P, H], U8)
+        wo_raw = held("wo_raw", [P, 2, N], I32)
+        wo_w = held("wo_w", [P, 2, N], I32)
+        wo_s_raw = held("wo_s_raw", [P, N], U8)
+        wo_s = held("wo_s", [P, N], U8)
+        wp_raw = [[held("wp_raw%d%d" % (g, a), [P, PACK, PASS], F32) for a in range(2)] for g in range(2)]
+        wp_w = [[held("wp_w%d%d" % (g, a), [P, PASS], U32) for a in range(2)] for g in range(2)]
+        wp_s = [[held("wp_s%d%d" % (g, a), [P, PASS], U8) for a in range(2)] for g in range(2)]
+        time_f = [[held("time_f%d%d" % (g, f), [P, PACK, HALF], F32) for f in range(2)] for g in range(2)]
+        h_w = [held("h_w%d" % g, [P, S], U32) for g in range(2)]
+        h_s = [held("h_s%d" % g, [P, S], U8) for g in range(2)]
+        h_bf = [held("h_bf%d" % g, [P, PACK * S], BF16) for g in range(2)]
+        y_bf = held("y_bf", [P, PACK * S], BF16)
+        y_w = held("y_w", [P, S], U32)
+        y_s = held("y_s", [P, S], U8)
+        bias = held("bias", [P, PACK], F32)
+        weight = held("weight", [P, PACK], F32)
+
+        for plane in (tab2_s, tab_s, wd_s_raw, wo_s_raw):
+            nc.vector.memset(plane[:].bitcast(I32), 0)
+
+        def words(dram):
+            return dram.rearrange("p n t -> p (n t)").bitcast(I32)
+
+        def load_scales(plane, scales, row):
+            passes = scales.shape[0]
+            for q in range(4):
+                first = 32 * q + row
+                nc.sync.dma_start(out=plane[first : first + 4 * passes, :].bitcast(I32),
+                                in_=scales[:, 4 * q : 4 * q + 4, :].bitcast(I32))
+
+        def load_time(g, f):
+            rows = tv[g * PASS : (g + 1) * PASS, f * HALF : (f + 1) * HALF]
+            nc.sync.dma_start(out=time_f[g][f][:], in_=rows.rearrange("(p t) j -> p t j", t=PACK))
+
+        def load_wp(g):
+            for a in range(2):
+                rows = wp[a * PASS : (a + 1) * PASS, g * PASS : (g + 1) * PASS]
+                nc.sync.dma_start(out=wp_raw[g][a][:], in_=rows.rearrange("(p i) c -> p i c", i=PACK))
+
+        nc.sync.dma_start(list2[:], offs2)
+        nc.sync.dma_start(out=tab2_w[:].bitcast(I32), in_=words(tab2_words[0]))
+        load_scales(tab2_s, tab2_scales, 0)
+        nc.sync.dma_start(list1[:], offs)
+        nc.sync.dma_start(out=tab_w[0][:].bitcast(I32), in_=words(tab_words[0]))
+        load_scales(tab_s, tab_scales, TAB_ROW)
+        load_time(0, 0)
+        nc.sync.dma_start(out=wd_raw[:].bitcast(I32), in_=wd_words[0].bitcast(I32))
+        load_scales(wd_s_raw, wd_scales, 0)
+        load_wp(0)
+        nc.sync.dma_start(out=tab_w[1][:].bitcast(I32), in_=words(tab_words[1]))
+        load_time(1, 0)
+        load_scales(wo_s_raw, wo_scales, WO_ROW)
+        load_wp(1)
+        nc.sync.dma_start(out=wo_raw[:], in_=wo_words.rearrange("a p n t -> p a (n t)").bitcast(I32))
+        nc.sync.dma_start(out=bias[:], in_=bo.rearrange("(p t) -> p t", t=PACK))
+        nc.sync.dma_start(out=weight[:], in_=cost.rearrange("(p t) -> p t", t=PACK))
+        load_time(0, 1)
+        load_time(1, 1)
+
+        def deal(dst, src, run):
+            nc.vector.tensor_copy(
+                out=dst.rearrange("p (g t b m) -> p g b t m", t=PACK, b=P // run, m=run),
+                in_=src.rearrange("p (g b m t) -> p g b t m", t=PACK, b=P // run, m=run),
+            )
+
+        def gather(dst, window, entries, first, count):
+            nc.vector.tensor_copy(dst, window[:].indirect(entries[:, first // 16 : (first + count) // 16]))
+
+        def quantize_wp(g, a):
+            rounded = ring.tile([P, PACK * PASS], BF16, name="wp_rounded", align_bytes=64)
+            nc.scalar.copy(
+                out=rounded[:].rearrange("p (t m i) -> p m i t", t=PACK, i=PACK),
+                in_=wp_raw[g][a][:].rearrange("p i (m t) -> p m i t", t=PACK),
+            )
+            nc.vector.quantize_mx(out=wp_w[g][a][:].bitcast(FP8X4), scales=wp_s[g][a][:], in_=rounded[:])
+
+        def times_b(g, f, t):
+            b = psum_b.tile([P, HALF], F32, name="b")
+            s = PACK * g + t
+            nc.tensor.matmul_mx(
+                out=b[:], lhsT=wd_w[:, 2 * P * s : 2 * P * (s + 1)].bitcast(FP4X4), lhsT_scale=wd_s[:, P * s : P * (s + 1)],
+                rhs=v2_w[f][:].bitcast(FP8X4), rhs_scale=v2_s[:, f * HALF : (f + 1) * HALF], start=True, stop=True,
+            )
+            nc.vector.tensor_tensor(time_f[g][f][:, t, :], b[:], time_f[g][f][:, t, :], MULT)
+
+        def times_a(g, j0):
+            f, c0 = divmod(j0, HALF)
+            acc = psum_a.tile([P, PACK, NARROW], F32, name="a")
+            for t in range(PACK):
+                for a in range(2):
+                    nc.tensor.matmul_mx(
+                        out=acc[:, t, :],
+                        lhsT=wp_w[g][a][:, P * t : P * (t + 1)].bitcast(FP8X4), lhsT_scale=wp_s[g][a][:, P * t : P * (t + 1)],
+                        rhs=v_w[a][f][:, c0 : c0 + NARROW].bitcast(FP8X4),
+                        rhs_scale=v_s[TAB_ROW + 4 * a : P, j0 : j0 + NARROW],
+                        start=(a == 0), stop=(a == 1),
+                    )
+            nc.vector.tensor_tensor(
+                h_bf[g][:, PACK * j0 : PACK * (j0 + NARROW)].rearrange("p (c e t) -> p c t e", e=2, t=PACK),
+                acc[:].rearrange("p t (c e) -> p c t e", e=2),
+                time_f[g][f][:, :, c0 : c0 + NARROW].rearrange("p t (c e) -> p c t e", e=2),
+                MULT,
+            )
+
+        def quantize_h(g, j0, width):
+            cols = slice(j0, j0 + width)
+            nc.vector.quantize_mx(out=h_w[g][:, cols].bitcast(FP8X4), scales=h_s[g][:, cols],
+                                  in_=h_bf[g][:, PACK * j0 : PACK * (j0 + width)])
+
+        def make_y(j0, width):
+            cols = slice(j0, j0 + width)
+            risk = ring.tile([P, PACK, width], F32, name="risk")
+            y = ring.tile([P, PACK, width], F32, name="y")
+            per_bank = HALF // width
+            for t0 in range(0, PACK, per_bank):
+                z = psum_z.tile([P, per_bank, width], F32, name="z")
+                for u in range(per_bank):
+                    t = t0 + u
+                    for g in range(2):
+                        nc.tensor.matmul_mx(
+                            out=z[:, u, :],
+                            lhsT=wo_w[:, g, P * t : P * (t + 1)].bitcast(FP8X4),
+                            lhsT_scale=wo_s[WO_ROW + 4 * g : P, P * t : P * (t + 1)],
+                            rhs=h_w[g][:, cols].bitcast(FP8X4), rhs_scale=h_s[g][:, cols],
+                            start=(g == 0), stop=(g == 1),
+                        )
+                for u in range(per_bank):
+                    t = t0 + u
+                    nc.scalar.activation(risk[:, t, :], z[:, u, :], SIGMOID, bias=bias[:, t : t + 1])
+            for t in range(PACK):
+                if j0 + width == S:
+                    nc.vector.tensor_scalar(y[:, t, :], risk[:, t, :], weight[:, t : t + 1], None, MULT)
+                else:
+                    nc.scalar.activation(y[:, t, :], risk[:, t, :], COPY, scale=weight[:, t : t + 1])
+            nc.sync.dma_start(out=out_0[:, cols].rearrange("(p t) j -> p t j", t=PACK), in_=y[:])
+            return y
+
+        def round_y(copy, y, j0, width):
+            copy(out=y_bf[:, PACK * j0 : PACK * (j0 + width)].rearrange("p (c e t) -> p c t e", e=2, t=PACK),
+                 in_=y[:].rearrange("p t (c e) -> p c t e", e=2))
+
+        def quantize_y(j0, width):
+            cols = slice(j0, j0 + width)
+            nc.vector.quantize_mx(out=y_w[:, cols].bitcast(FP8X4), scales=y_s[:, cols],
+                                  in_=y_bf[:, PACK * j0 : PACK * (j0 + width)])
+
+        def store_words(j0, width):
+            cols = slice(j0, j0 + width)
+            nc.sync.dma_start(out=words(out_1[0])[:, cols], in_=y_w[:, cols].bitcast(I32))
+
+        for f in range(2):
+            gather(v2_w[f][:], tab2_w, list2, f * HALF, HALF)
+        gather(v2_s[:], tab2_s, list2, 0, S)
+        for f in range(2):
+            gather(v_w[0][f][:], tab_w[0], list1, f * HALF, HALF)
+        gather(v_s[:], tab_s, list1, 0, S)
+        deal(wd_w[:].bitcast(U16), wd_raw[:].bitcast(U16), 8)
+        deal(wd_s[:], wd_s_raw[:], 16)
+        for t in range(PACK):
+            times_b(0, 0, t)
+        for a in range(2):
+            quantize_wp(0, a)
+        for f in range(2):
+            gather(v_w[1][f][:], tab_w[1], list1, f * HALF, HALF)
+
+        for t in range(PACK):
+            times_a(0, t * NARROW)
+            times_b(1, 0, t)
+            if t % 2:
+                quantize_h(0, (t - 1) * NARROW, CHUNK)
+        for a in range(2):
+            quantize_wp(1, a)
+        deal(wo_w[:].rearrange("p a n -> p (a n)"), wo_raw[:].rearrange("p a n -> p (a n)"), 4)
+        deal(wo_s[:], wo_s_raw[:], 16)
+        for t in range(PACK):
+            times_a(1, t * NARROW)
+            times_b(0, 1, t)
+            if t % 2:
+                j0 = (t - 1) * NARROW
+                quantize_h(1, j0, CHUNK)
+                round_y(nc.scalar.copy, make_y(j0, CHUNK), j0, CHUNK)
+        for t in range(PACK):
+            times_b(1, 1, t)
+        waiting = None
+        for j0 in range(HALF, S, NARROW):
+            times_a(0, j0)
+            times_a(1, j0)
+            quantize_h(0, j0, NARROW)
+            if waiting is not None:
+                round_y(nc.vector.tensor_copy, waiting, j0 - NARROW, NARROW)
+            quantize_h(1, j0, NARROW)
+            waiting = make_y(j0, NARROW)
+        quantize_y(0, HALF)
+        store_words(0, HALF)
+        quantize_y(HALF, CHUNK)
+        quantize_y(HALF + CHUNK, NARROW)
+        round_y(nc.vector.tensor_copy, waiting, S - NARROW, NARROW)
+        quantize_y(S - NARROW, NARROW)
+        store_words(HALF, HALF)
+        for q in range(4):
+            nc.scalar.dma_start(out=out_2[0, 4 * q : 4 * q + 4, :].bitcast(I32), in_=y_s[32 * q : 32 * q + 4, :].bitcast(I32))

@@ -79,11 +79,11 @@ def tile_list_visit_risk_burden_kernel(
         def words(dram):
             return dram.rearrange("p n t -> p (n t)").bitcast(I32)
 
-        def load_scales(plane, scales, row):
+        def load_scales(queue, plane, scales, row):
             passes = scales.shape[0]
             for q in range(4):
                 first = 32 * q + row
-                nc.sync.dma_start(out=plane[first : first + 4 * passes, :].bitcast(I32),
+                queue.dma_start(out=plane[first : first + 4 * passes, :].bitcast(I32),
                                 in_=scales[:, 4 * q : 4 * q + 4, :].bitcast(I32))
 
         def load_time(g, f):
@@ -97,23 +97,23 @@ def tile_list_visit_risk_burden_kernel(
 
         nc.sync.dma_start(list2[:], offs2)
         nc.sync.dma_start(out=tab2_w[:].bitcast(I32), in_=words(tab2_words[0]))
-        load_scales(tab2_s, tab2_scales, 0)
+        load_scales(nc.sync, tab2_s, tab2_scales, 0)
         nc.sync.dma_start(list1[:], offs)
         nc.sync.dma_start(out=tab_w[0][:].bitcast(I32), in_=words(tab_words[0]))
-        load_scales(tab_s, tab_scales, TAB_ROW)
-        load_time(0, 0)
         nc.sync.dma_start(out=wd_raw[:].bitcast(I32), in_=wd_words[0].bitcast(I32))
-        load_scales(wd_s_raw, wd_scales, 0)
+        load_time(0, 0)
+        load_scales(nc.sync, wd_s_raw, wd_scales, 0)
         load_wp(0)
         nc.sync.dma_start(out=tab_w[1][:].bitcast(I32), in_=words(tab_words[1]))
-        load_time(1, 0)
-        load_scales(wo_s_raw, wo_scales, WO_ROW)
-        load_wp(1)
-        nc.sync.dma_start(out=wo_raw[:], in_=wo_words.rearrange("a p n t -> p a (n t)").bitcast(I32))
-        nc.sync.dma_start(out=bias[:], in_=bo.rearrange("(p t) -> p t", t=PACK))
-        nc.sync.dma_start(out=weight[:], in_=cost.rearrange("(p t) -> p t", t=PACK))
         load_time(0, 1)
+        load_wp(1)
+        load_time(1, 0)
+        nc.sync.dma_start(out=wo_raw[:], in_=wo_words.rearrange("a p n t -> p a (n t)").bitcast(I32))
         load_time(1, 1)
+        load_scales(nc.gpsimd, tab_s, tab_scales, TAB_ROW)
+        load_scales(nc.gpsimd, wo_s_raw, wo_scales, WO_ROW)
+        nc.gpsimd.dma_start(out=bias[:], in_=bo.rearrange("(p t) -> p t", t=PACK))
+        nc.gpsimd.dma_start(out=weight[:], in_=cost.rearrange("(p t) -> p t", t=PACK))
 
         def deal(dst, src, run):
             nc.vector.tensor_copy(
@@ -223,36 +223,39 @@ def tile_list_visit_risk_burden_kernel(
 
         for t in range(PACK):
             times_a(0, t * NARROW)
-            times_b(1, 0, t)
+            times_b(0, 1, t)
             if t % 2:
                 quantize_h(0, (t - 1) * NARROW, CHUNK)
-        for a in range(2):
-            quantize_wp(1, a)
+        for t in range(PACK):
+            times_a(0, HALF + t * NARROW)
+            if t == 2:
+                quantize_wp(1, 0)
+                quantize_h(0, HALF, CHUNK)
+        quantize_wp(1, 1)
+        quantize_h(0, HALF + CHUNK, CHUNK)
+        for t in range(PACK):
+            times_b(1, 0, t)
         deal(wo_w[:].rearrange("p a n -> p (a n)"), wo_raw[:].rearrange("p a n -> p (a n)"), 4)
         deal(wo_s[:], wo_s_raw[:], 16)
         for t in range(PACK):
             times_a(1, t * NARROW)
-            times_b(0, 1, t)
+            times_b(1, 1, t)
             if t % 2:
                 j0 = (t - 1) * NARROW
                 quantize_h(1, j0, CHUNK)
-                round_y(nc.scalar.copy, make_y(j0, CHUNK), j0, CHUNK)
-        for t in range(PACK):
-            times_b(1, 1, t)
-        waiting = None
+                waiting = (make_y(j0, CHUNK), j0, CHUNK)
+                if t == 1:
+                    round_y(nc.scalar.copy, *waiting)
         for j0 in range(HALF, S, NARROW):
-            times_a(0, j0)
             times_a(1, j0)
-            quantize_h(0, j0, NARROW)
-            if waiting is not None:
-                round_y(nc.vector.tensor_copy, waiting, j0 - NARROW, NARROW)
+            round_y(nc.vector.tensor_copy, *waiting)
             quantize_h(1, j0, NARROW)
-            waiting = make_y(j0, NARROW)
+            waiting = (make_y(j0, NARROW), j0, NARROW)
         quantize_y(0, HALF)
         store_words(0, HALF)
         quantize_y(HALF, CHUNK)
         quantize_y(HALF + CHUNK, NARROW)
-        round_y(nc.vector.tensor_copy, waiting, S - NARROW, NARROW)
+        round_y(nc.vector.tensor_copy, *waiting)
         quantize_y(S - NARROW, NARROW)
         store_words(HALF, HALF)
         for q in range(4):

@@ -73,6 +73,8 @@ def tile_list_visit_risk_burden_kernel(
         bias = held("bias", [P, PACK], F32)
         weight = held("weight", [P, PACK], F32)
 
+        bt = {}
+
         for plane in (tab2_s, tab_s, wd_s_raw, wo_s_raw):
             nc.vector.memset(plane[:].bitcast(I32), 0)
 
@@ -125,21 +127,34 @@ def tile_list_visit_risk_burden_kernel(
             nc.vector.tensor_copy(dst, window[:].indirect(entries[:, first // 16 : (first + count) // 16]))
 
         def quantize_wp(g, a):
-            rounded = ring.tile([P, PACK * PASS], BF16, name="wp_rounded", align_bytes=64)
+            rounded = ring.tile([P, PACK * PASS], BF16, name="wp_rounded", align_bytes=64, bufs=2)
             nc.scalar.copy(
-                out=rounded[:].rearrange("p (t m i) -> p m i t", t=PACK, i=PACK),
-                in_=wp_raw[g][a][:].rearrange("p i (m t) -> p m i t", t=PACK),
+                out=rounded[:].rearrange("p (t m i) -> p m t i", t=PACK, i=PACK),
+                in_=wp_raw[g][a][:].rearrange("p i (m t) -> p m t i", t=PACK),
             )
             nc.vector.quantize_mx(out=wp_w[g][a][:].bitcast(FP8X4), scales=wp_s[g][a][:], in_=rounded[:])
 
-        def times_b(g, f, t):
-            b = psum_b.tile([P, HALF], F32, name="b")
-            s = PACK * g + t
-            nc.tensor.matmul_mx(
-                out=b[:], lhsT=wd_w[:, 2 * P * s : 2 * P * (s + 1)].bitcast(FP4X4), lhsT_scale=wd_s[:, P * s : P * (s + 1)],
-                rhs=v2_w[f][:].bitcast(FP8X4), rhs_scale=v2_s[:, f * HALF : (f + 1) * HALF], start=True, stop=True,
+        def times_b(g, f, step):
+            block, pair = divmod(step, 2)
+            j0 = f * HALF + block * CHUNK
+            if pair == 0:
+                bt[g, j0] = ring.tile([P, CHUNK // 2, PACK, 2], F32, name="bt", bufs=4)
+            b = psum_b.tile([P, 2, CHUNK], F32, name="b")
+            for u in range(2):
+                s = PACK * g + 2 * pair + u
+                nc.tensor.matmul_mx(
+                    out=b[:, u, :],
+                    lhsT=wd_w[:, 2 * P * s : 2 * P * (s + 1)].bitcast(FP4X4), lhsT_scale=wd_s[:, P * s : P * (s + 1)],
+                    rhs=v2_w[f][:, block * CHUNK : (block + 1) * CHUNK].bitcast(FP8X4), rhs_scale=v2_s[:, j0 : j0 + CHUNK],
+                    start=True, stop=True,
+                )
+            factors = time_f[g][f][:, 2 * pair : 2 * pair + 2, block * CHUNK : (block + 1) * CHUNK]
+            nc.vector.tensor_tensor(
+                bt[g, j0][:, :, 2 * pair : 2 * pair + 2, :],
+                b[:].rearrange("p t (n e) -> p n t e", e=2),
+                factors.rearrange("p t (n e) -> p n t e", e=2),
+                MULT,
             )
-            nc.vector.tensor_tensor(time_f[g][f][:, t, :], b[:], time_f[g][f][:, t, :], MULT)
 
         def times_a(g, j0):
             f, c0 = divmod(j0, HALF)
@@ -153,10 +168,12 @@ def tile_list_visit_risk_burden_kernel(
                         rhs_scale=v_s[TAB_ROW + 4 * a : P, j0 : j0 + NARROW],
                         start=(a == 0), stop=(a == 1),
                     )
+            block0 = j0 - j0 % CHUNK
+            n0 = (j0 - block0) // 2
             nc.vector.tensor_tensor(
-                h_bf[g][:, PACK * j0 : PACK * (j0 + NARROW)].rearrange("p (c e t) -> p c t e", e=2, t=PACK),
-                acc[:].rearrange("p t (c e) -> p c t e", e=2),
-                time_f[g][f][:, :, c0 : c0 + NARROW].rearrange("p t (c e) -> p c t e", e=2),
+                h_bf[g][:, PACK * j0 : PACK * (j0 + NARROW)].rearrange("p (n e t) -> p n e t", e=2, t=PACK),
+                acc[:].rearrange("p t (n e) -> p n e t", e=2),
+                bt[g, block0][:, n0 : n0 + NARROW // 2, :, :].rearrange("p n t e -> p n e t"),
                 MULT,
             )
 
@@ -167,7 +184,7 @@ def tile_list_visit_risk_burden_kernel(
 
         def make_y(j0, width):
             cols = slice(j0, j0 + width)
-            risk = ring.tile([P, PACK, width], F32, name="risk")
+            risk = ring.tile([P, PACK, width], F32, name="risk", bufs=2)
             y = ring.tile([P, PACK, width], F32, name="y")
             per_bank = HALF // width
             for t0 in range(0, PACK, per_bank):
@@ -194,8 +211,8 @@ def tile_list_visit_risk_burden_kernel(
             return y
 
         def round_y(copy, y, j0, width):
-            copy(out=y_bf[:, PACK * j0 : PACK * (j0 + width)].rearrange("p (c e t) -> p c t e", e=2, t=PACK),
-                 in_=y[:].rearrange("p t (c e) -> p c t e", e=2))
+            copy(out=y_bf[:, PACK * j0 : PACK * (j0 + width)].rearrange("p (n t) -> p n t", t=PACK),
+                 in_=y[:].rearrange("p t n -> p n t"))
 
         def quantize_y(j0, width):
             cols = slice(j0, j0 + width)

@@ -88,9 +88,9 @@ def tile_list_visit_risk_burden_kernel(
                 queue.dma_start(out=plane[first : first + 4 * passes, :].bitcast(I32),
                                 in_=scales[:, 4 * q : 4 * q + 4, :].bitcast(I32))
 
-        def load_time(g, f):
+        def load_time(g, f, slots=slice(0, PACK)):
             rows = tv[g * PASS : (g + 1) * PASS, f * HALF : (f + 1) * HALF]
-            nc.sync.dma_start(out=time_f[g][f][:], in_=rows.rearrange("(p t) j -> p t j", t=PACK))
+            nc.sync.dma_start(out=time_f[g][f][:, slots, :], in_=rows.rearrange("(p t) j -> p t j", t=PACK)[:, slots, :])
 
         def load_wp(g):
             for a in range(2):
@@ -107,10 +107,11 @@ def tile_list_visit_risk_burden_kernel(
         load_scales(nc.sync, wd_s_raw, wd_scales, 0)
         load_wp(0)
         nc.sync.dma_start(out=tab_w[1][:].bitcast(I32), in_=words(tab_words[1]))
-        load_time(0, 1)
         load_wp(1)
-        load_time(1, 0)
+        for pair in range(2):
+            load_time(1, 0, slice(2 * pair, 2 * pair + 2))
         nc.sync.dma_start(out=wo_raw[:], in_=wo_words.rearrange("a p n t -> p a (n t)").bitcast(I32))
+        load_time(0, 1)
         load_time(1, 1)
         load_scales(nc.gpsimd, tab_s, tab_scales, TAB_ROW)
         load_scales(nc.gpsimd, wo_s_raw, wo_scales, WO_ROW)
@@ -137,7 +138,7 @@ def tile_list_visit_risk_burden_kernel(
         def times_b(g, f, step):
             block, pair = divmod(step, 2)
             j0 = f * HALF + block * CHUNK
-            if pair == 0:
+            if (g, j0) not in bt:
                 bt[g, j0] = ring.tile([P, CHUNK // 2, PACK, 2], F32, name="bt", bufs=4)
             b = psum_b.tile([P, 2, CHUNK], F32, name="b")
             for u in range(2):
@@ -203,7 +204,7 @@ def tile_list_visit_risk_burden_kernel(
                     t = t0 + u
                     nc.scalar.activation(risk[:, t, :], z[:, u, :], SIGMOID, bias=bias[:, t : t + 1])
             for t in range(PACK):
-                if j0 + width == S:
+                if width == NARROW:
                     nc.vector.tensor_scalar(y[:, t, :], risk[:, t, :], weight[:, t : t + 1], None, MULT)
                 else:
                     nc.scalar.activation(y[:, t, :], risk[:, t, :], COPY, scale=weight[:, t : t + 1])
@@ -228,52 +229,66 @@ def tile_list_visit_risk_burden_kernel(
         gather(v2_s[:], tab2_s, list2, 0, S)
         for f in range(2):
             gather(v_w[0][f][:], tab_w[0], list1, f * HALF, HALF)
-        gather(v_s[:], tab_s, list1, 0, S)
         deal(wd_w[:].bitcast(U16), wd_raw[:].bitcast(U16), 8)
         deal(wd_s[:], wd_s_raw[:], 16)
         for t in range(PACK):
             times_b(0, 0, t)
+        gather(v_s[:], tab_s, list1, 0, S)
         for a in range(2):
             quantize_wp(0, a)
         for f in range(2):
             gather(v_w[1][f][:], tab_w[1], list1, f * HALF, HALF)
 
-        for t in range(PACK):
-            times_a(0, t * NARROW)
-            times_b(0, 1, t)
-            if t % 2:
-                quantize_h(0, (t - 1) * NARROW, CHUNK)
-        for t in range(PACK):
-            times_a(0, HALF + t * NARROW)
-            if t == 2:
-                quantize_wp(1, 0)
-                quantize_h(0, HALF, CHUNK)
+        for c in range(4):
+            times_a(0, c * NARROW)
+        quantize_wp(1, 0)
+        quantize_h(0, 0, HALF)
+        times_b(1, 0, 0)
+        times_b(1, 0, 2)
         quantize_wp(1, 1)
-        quantize_h(0, HALF + CHUNK, CHUNK)
-        for t in range(PACK):
-            times_b(1, 0, t)
+        times_b(1, 0, 1)
+        times_a(1, 0)
+        times_b(1, 0, 3)
+        times_a(1, NARROW)
         deal(wo_w[:].rearrange("p a n -> p (a n)"), wo_raw[:].rearrange("p a n -> p (a n)"), 4)
         deal(wo_s[:], wo_s_raw[:], 16)
-        for t in range(PACK):
-            times_a(1, t * NARROW)
-            times_b(1, 1, t)
-            if t % 2:
-                j0 = (t - 1) * NARROW
-                quantize_h(1, j0, CHUNK)
-                waiting = (make_y(j0, CHUNK), j0, CHUNK)
-                if t == 1:
-                    round_y(nc.scalar.copy, *waiting)
-        for j0 in range(HALF, S, NARROW):
-            times_a(1, j0)
-            round_y(nc.vector.tensor_copy, *waiting)
-            quantize_h(1, j0, NARROW)
-            waiting = (make_y(j0, NARROW), j0, NARROW)
+        quantize_h(1, 0, CHUNK)
+        round_y(nc.scalar.copy, make_y(0, CHUNK), 0, CHUNK)
+        times_a(1, CHUNK)
+        times_a(1, CHUNK + NARROW)
+        times_b(0, 1, 0)
+        quantize_h(1, CHUNK, CHUNK)
+        round_y(nc.scalar.copy, make_y(CHUNK, CHUNK), CHUNK, CHUNK)
+        times_b(0, 1, 1)
+        times_a(0, HALF)
+        times_b(1, 1, 0)
+        times_a(0, HALF + NARROW)
+        times_b(1, 1, 1)
+        quantize_h(0, HALF, CHUNK)
+        times_a(1, HALF)
+        times_b(0, 1, 2)
+        times_a(1, HALF + NARROW)
+        times_b(0, 1, 3)
+        quantize_h(1, HALF, CHUNK)
+        round_y(nc.scalar.copy, make_y(HALF, CHUNK), HALF, CHUNK)
+        first, last = S - 2 * NARROW, S - NARROW
+        times_b(1, 1, 2)
+        times_a(0, first)
+        times_b(1, 1, 3)
+        times_a(1, first)
+        quantize_h(0, first, NARROW)
+        times_a(0, last)
+        quantize_h(1, first, NARROW)
+        times_a(1, last)
+        quantize_h(0, last, NARROW)
+        quantize_h(1, last, NARROW)
         quantize_y(0, HALF)
         store_words(0, HALF)
+        round_y(nc.vector.tensor_copy, make_y(first, NARROW), first, NARROW)
         quantize_y(HALF, CHUNK)
-        quantize_y(HALF + CHUNK, NARROW)
-        round_y(nc.vector.tensor_copy, *waiting)
-        quantize_y(S - NARROW, NARROW)
-        store_words(HALF, HALF)
+        store_words(HALF, CHUNK)
+        round_y(nc.vector.tensor_copy, make_y(last, NARROW), last, NARROW)
+        quantize_y(first, CHUNK)
+        store_words(first, CHUNK)
         for q in range(4):
             nc.scalar.dma_start(out=out_2[0, 4 * q : 4 * q + 4, :].bitcast(I32), in_=y_s[32 * q : 32 * q + 4, :].bitcast(I32))

@@ -97,8 +97,8 @@ def tile_list_visit_risk_burden_kernel(
                 rows = wp[a * PASS : (a + 1) * PASS, g * PASS : (g + 1) * PASS]
                 nc.sync.dma_start(out=wp_raw[g][a][:], in_=rows.rearrange("(p i) c -> p i c", i=PACK))
 
-        nc.sync.dma_start(list2[:], offs2)
         nc.sync.dma_start(out=tab2_w[:].bitcast(I32), in_=words(tab2_words[0]))
+        nc.sync.dma_start(list2[:], offs2)
         load_scales(nc.sync, tab2_s, tab2_scales, 0)
         nc.sync.dma_start(list1[:], offs)
         nc.sync.dma_start(out=tab_w[0][:].bitcast(I32), in_=words(tab_words[0]))
@@ -160,14 +160,14 @@ def tile_list_visit_risk_burden_kernel(
         def times_a(g, j0):
             f, c0 = divmod(j0, HALF)
             acc = psum_a.tile([P, PACK, NARROW], F32, name="a")
-            for t in range(PACK):
-                for a in range(2):
+            for a in range(2):
+                for t in range(PACK):
                     nc.tensor.matmul_mx(
                         out=acc[:, t, :],
                         lhsT=wp_w[g][a][:, P * t : P * (t + 1)].bitcast(FP8X4), lhsT_scale=wp_s[g][a][:, P * t : P * (t + 1)],
                         rhs=v_w[a][f][:, c0 : c0 + NARROW].bitcast(FP8X4),
                         rhs_scale=v_s[TAB_ROW + 4 * a : P, j0 : j0 + NARROW],
-                        start=(a == 0), stop=(a == 1),
+                        start=(a == 0 and t == 0), stop=(a == 1 and t == PACK - 1),
                     )
             block0 = j0 - j0 % CHUNK
             n0 = (j0 - block0) // 2
@@ -190,15 +190,15 @@ def tile_list_visit_risk_burden_kernel(
             per_bank = HALF // width
             for t0 in range(0, PACK, per_bank):
                 z = psum_z.tile([P, per_bank, width], F32, name="z")
-                for u in range(per_bank):
-                    t = t0 + u
-                    for g in range(2):
+                for g in range(2):
+                    for u in range(per_bank):
+                        t = t0 + u
                         nc.tensor.matmul_mx(
                             out=z[:, u, :],
                             lhsT=wo_w[:, g, P * t : P * (t + 1)].bitcast(FP8X4),
                             lhsT_scale=wo_s[WO_ROW + 4 * g : P, P * t : P * (t + 1)],
                             rhs=h_w[g][:, cols].bitcast(FP8X4), rhs_scale=h_s[g][:, cols],
-                            start=(g == 0), stop=(g == 1),
+                            start=(g == 0 and u == 0), stop=(g == 1 and u == per_bank - 1),
                         )
                 for u in range(per_bank):
                     t = t0 + u
@@ -275,20 +275,21 @@ def tile_list_visit_risk_burden_kernel(
         times_b(1, 1, 2)
         times_a(0, first)
         times_b(1, 1, 3)
-        times_a(1, first)
-        quantize_h(0, first, NARROW)
         times_a(0, last)
+        times_a(1, first)
+        quantize_h(0, first, CHUNK)
         quantize_h(1, first, NARROW)
         times_a(1, last)
-        quantize_h(0, last, NARROW)
+        quantize_y(0, CHUNK)
         quantize_h(1, last, NARROW)
-        quantize_y(0, HALF)
+        quantize_y(CHUNK, CHUNK)
         store_words(0, HALF)
         round_y(nc.vector.tensor_copy, make_y(first, NARROW), first, NARROW)
         quantize_y(HALF, CHUNK)
-        store_words(HALF, CHUNK)
+        quantize_y(first, NARROW)
+        store_words(HALF, CHUNK + NARROW)
         round_y(nc.vector.tensor_copy, make_y(last, NARROW), last, NARROW)
-        quantize_y(first, CHUNK)
-        store_words(first, CHUNK)
+        quantize_y(last, NARROW)
+        store_words(last, NARROW)
         for q in range(4):
             nc.scalar.dma_start(out=out_2[0, 4 * q : 4 * q + 4, :].bitcast(I32), in_=y_s[32 * q : 32 * q + 4, :].bitcast(I32))

@@ -14,6 +14,7 @@ U8 = mybir.dt.uint8
 FP8X4 = mybir.dt.float8_e4m3fn_x4
 FP4X4 = mybir.dt.float4_e2m1fn_x4
 MULT = mybir.AluOpType.mult
+ADD = mybir.AluOpType.add
 SIGMOID = mybir.ActivationFunctionType.Sigmoid
 COPY = mybir.ActivationFunctionType.Copy
 
@@ -54,28 +55,26 @@ def tile_list_visit_risk_burden_kernel(
         v2_s = held("v2_s", [P, S], U8)
         wd_raw = held("wd_raw", [P, 2 * H], U8)
         wd_w = held("wd_w", [P, 2 * H], U8)
-        wd_s_raw = held("wd_s_raw", [P, H], U8)
-        wd_s = held("wd_s", [P, H], U8)
+        w_s_raw = held("w_s_raw", [P, H], U8)
+        w_s = held("w_s", [P, H], U8)
         wo_raw = held("wo_raw", [P, 2, N], I32)
         wo_w = held("wo_w", [P, 2, N], I32)
-        wo_s_raw = held("wo_s_raw", [P, N], U8)
-        wo_s = held("wo_s", [P, N], U8)
         wp_raw = [[held("wp_raw%d%d" % (g, a), [P, PACK, PASS], F32) for a in range(2)] for g in range(2)]
         wp_w = [[held("wp_w%d%d" % (g, a), [P, PASS], U32) for a in range(2)] for g in range(2)]
         wp_s = [[held("wp_s%d%d" % (g, a), [P, PASS], U8) for a in range(2)] for g in range(2)]
-        time_f = [[held("time_f%d%d" % (g, f), [P, PACK, HALF], F32) for f in range(2)] for g in range(2)]
         h_w = [held("h_w%d" % g, [P, S], U32) for g in range(2)]
         h_s = [held("h_s%d" % g, [P, S], U8) for g in range(2)]
-        h_bf = [held("h_bf%d" % g, [P, PACK * S], BF16) for g in range(2)]
         y_bf = held("y_bf", [P, PACK * S], BF16)
         y_w = held("y_w", [P, S], U32)
         y_s = held("y_s", [P, S], U8)
         bias = held("bias", [P, PACK], F32)
         weight = held("weight", [P, PACK], F32)
 
+        time_f = {}
         bt = {}
+        h_bf = {}
 
-        for plane in (tab2_s, tab_s, wd_s_raw, wo_s_raw):
+        for plane in (tab2_s, w_s_raw, tab_s):
             nc.vector.memset(plane[:].bitcast(I32), 0)
 
         def words(dram):
@@ -85,36 +84,43 @@ def tile_list_visit_risk_burden_kernel(
             passes = scales.shape[0]
             for q in range(4):
                 first = 32 * q + row
-                queue.dma_start(out=plane[first : first + 4 * passes, :].bitcast(I32),
+                queue.dma_start(out=plane[first : first + 4 * passes, 0 : scales.shape[2]].bitcast(I32),
                                 in_=scales[:, 4 * q : 4 * q + 4, :].bitcast(I32))
 
-        def load_time(g, f, slots=slice(0, PACK)):
-            rows = tv[g * PASS : (g + 1) * PASS, f * HALF : (f + 1) * HALF]
-            nc.sync.dma_start(out=time_f[g][f][:, slots, :], in_=rows.rearrange("(p t) j -> p t j", t=PACK)[:, slots, :])
+        def load_time(g, j0, width):
+            tile = held("time%d_%d" % (g, j0), [P, PACK, width], F32)
+            rows = tv[g * PASS : (g + 1) * PASS, j0 : j0 + width]
+            nc.sync.dma_start(out=tile[:], in_=rows.rearrange("(p t) j -> p t j", t=PACK))
+            for c0 in range(0, width, CHUNK):
+                time_f[g, j0 + c0] = tile[:, :, c0 : c0 + CHUNK]
 
-        def load_wp(g):
-            for a in range(2):
-                rows = wp[a * PASS : (a + 1) * PASS, g * PASS : (g + 1) * PASS]
-                nc.sync.dma_start(out=wp_raw[g][a][:], in_=rows.rearrange("(p i) c -> p i c", i=PACK))
+        def load_wp(g, a):
+            rows = wp[a * PASS : (a + 1) * PASS, g * PASS : (g + 1) * PASS]
+            nc.sync.dma_start(out=wp_raw[g][a][:], in_=rows.rearrange("(p i) c -> p i c", i=PACK))
 
-        nc.sync.dma_start(out=tab2_w[:].bitcast(I32), in_=words(tab2_words[0]))
+        def load_table(tile, dram):
+            nc.sync.dma_start(out=tile[:].bitcast(I32), in_=words(dram))
+
+        load_table(tab2_w, tab2_words[0])
         nc.sync.dma_start(list2[:], offs2)
         load_scales(nc.sync, tab2_s, tab2_scales, 0)
         nc.sync.dma_start(list1[:], offs)
-        nc.sync.dma_start(out=tab_w[0][:].bitcast(I32), in_=words(tab_words[0]))
+        load_table(tab_w[0], tab_words[0])
         nc.sync.dma_start(out=wd_raw[:].bitcast(I32), in_=wd_words[0].bitcast(I32))
-        load_time(0, 0)
-        load_scales(nc.sync, wd_s_raw, wd_scales, 0)
-        load_wp(0)
-        nc.sync.dma_start(out=tab_w[1][:].bitcast(I32), in_=words(tab_words[1]))
-        load_wp(1)
-        for pair in range(2):
-            load_time(1, 0, slice(2 * pair, 2 * pair + 2))
+        load_scales(nc.sync, w_s_raw, wd_scales, 0)
+        load_time(0, 0, HALF)
+        load_wp(0, 0)
+        load_wp(0, 1)
+        load_table(tab_w[1], tab_words[1])
+        load_wp(1, 0)
+        load_wp(1, 1)
+        load_time(1, 0, CHUNK)
         nc.sync.dma_start(out=wo_raw[:], in_=wo_words.rearrange("a p n t -> p a (n t)").bitcast(I32))
-        load_time(0, 1)
-        load_time(1, 1)
+        load_time(1, CHUNK, CHUNK)
+        load_time(0, HALF, HALF)
+        load_time(1, HALF, HALF)
+        load_scales(nc.gpsimd, w_s_raw, wo_scales, WO_ROW)
         load_scales(nc.gpsimd, tab_s, tab_scales, TAB_ROW)
-        load_scales(nc.gpsimd, wo_s_raw, wo_scales, WO_ROW)
         nc.gpsimd.dma_start(out=bias[:], in_=bo.rearrange("(p t) -> p t", t=PACK))
         nc.gpsimd.dma_start(out=weight[:], in_=cost.rearrange("(p t) -> p t", t=PACK))
 
@@ -135,30 +141,32 @@ def tile_list_visit_risk_burden_kernel(
             )
             nc.vector.quantize_mx(out=wp_w[g][a][:].bitcast(FP8X4), scales=wp_s[g][a][:], in_=rounded[:])
 
-        def times_b(g, f, step):
-            block, pair = divmod(step, 2)
-            j0 = f * HALF + block * CHUNK
-            if (g, j0) not in bt:
-                bt[g, j0] = ring.tile([P, CHUNK // 2, PACK, 2], F32, name="bt", bufs=4)
-            b = psum_b.tile([P, 2, CHUNK], F32, name="b")
+        def product_b(g, j0, pair, pool, tag):
+            f, c0 = divmod(j0, HALF)
+            b = pool.tile([P, 2, CHUNK], F32, name=tag)
             for u in range(2):
                 s = PACK * g + 2 * pair + u
                 nc.tensor.matmul_mx(
                     out=b[:, u, :],
-                    lhsT=wd_w[:, 2 * P * s : 2 * P * (s + 1)].bitcast(FP4X4), lhsT_scale=wd_s[:, P * s : P * (s + 1)],
-                    rhs=v2_w[f][:, block * CHUNK : (block + 1) * CHUNK].bitcast(FP8X4), rhs_scale=v2_s[:, j0 : j0 + CHUNK],
+                    lhsT=wd_w[:, 2 * P * s : 2 * P * (s + 1)].bitcast(FP4X4), lhsT_scale=w_s[:, P * s : P * (s + 1)],
+                    rhs=v2_w[f][:, c0 : c0 + CHUNK].bitcast(FP8X4), rhs_scale=v2_s[:, j0 : j0 + CHUNK],
                     start=True, stop=True,
                 )
-            factors = time_f[g][f][:, 2 * pair : 2 * pair + 2, block * CHUNK : (block + 1) * CHUNK]
-            nc.vector.tensor_tensor(
-                bt[g, j0][:, :, 2 * pair : 2 * pair + 2, :],
-                b[:].rearrange("p t (n e) -> p n t e", e=2),
-                factors.rearrange("p t (n e) -> p n t e", e=2),
-                MULT,
-            )
+            return b
+
+        def factors(g, j0, pair):
+            return time_f[g, j0][:, 2 * pair : 2 * pair + 2, :]
+
+        def times_b(g, j0, pair):
+            if (g, j0) not in bt:
+                bt[g, j0] = ring.tile([P, PACK, CHUNK], F32, name="bt", bufs=4)
+            b = product_b(g, j0, pair, psum_b, "b")
+            nc.vector.tensor_tensor(bt[g, j0][:, 2 * pair : 2 * pair + 2, :], b[:], factors(g, j0, pair), MULT)
 
         def times_a(g, j0):
             f, c0 = divmod(j0, HALF)
+            if (g, f) not in h_bf:
+                h_bf[g, f] = ring.tile([P, PACK * HALF], BF16, name="h_bf", align_bytes=64)
             acc = psum_a.tile([P, PACK, NARROW], F32, name="a")
             for a in range(2):
                 for t in range(PACK):
@@ -170,20 +178,27 @@ def tile_list_visit_risk_burden_kernel(
                         start=(a == 0 and t == 0), stop=(a == 1 and t == PACK - 1),
                     )
             block0 = j0 - j0 % CHUNK
-            n0 = (j0 - block0) // 2
+            n0 = j0 - block0
             nc.vector.tensor_tensor(
-                h_bf[g][:, PACK * j0 : PACK * (j0 + NARROW)].rearrange("p (n e t) -> p n e t", e=2, t=PACK),
-                acc[:].rearrange("p t (n e) -> p n e t", e=2),
-                bt[g, block0][:, n0 : n0 + NARROW // 2, :, :].rearrange("p n t e -> p n e t"),
+                h_bf[g, f][:, PACK * c0 : PACK * (c0 + NARROW)].rearrange("p (n e t) -> p n t e", e=2, t=PACK),
+                acc[:].rearrange("p t (n e) -> p n t e", e=2),
+                bt[g, block0][:, :, n0 : n0 + NARROW].rearrange("p t (n e) -> p n t e", e=2),
                 MULT,
             )
 
         def quantize_h(g, j0, width):
+            f, c0 = divmod(j0, HALF)
             cols = slice(j0, j0 + width)
             nc.vector.quantize_mx(out=h_w[g][:, cols].bitcast(FP8X4), scales=h_s[g][:, cols],
-                                  in_=h_bf[g][:, PACK * j0 : PACK * (j0 + width)])
+                                  in_=h_bf[g, f][:, PACK * c0 : PACK * (c0 + width)])
 
-        def make_y(j0, width):
+        def weigh_on_scalar(y, risk, t):
+            nc.scalar.activation(y, risk, COPY, scale=weight[:, t : t + 1])
+
+        def weigh_on_vector(y, risk, t):
+            nc.vector.tensor_scalar(y, risk, weight[:, t : t + 1], None, MULT)
+
+        def make_y(j0, width, weigh, round_copy):
             cols = slice(j0, j0 + width)
             risk = ring.tile([P, PACK, width], F32, name="risk", bufs=2)
             y = ring.tile([P, PACK, width], F32, name="y")
@@ -196,7 +211,7 @@ def tile_list_visit_risk_burden_kernel(
                         nc.tensor.matmul_mx(
                             out=z[:, u, :],
                             lhsT=wo_w[:, g, P * t : P * (t + 1)].bitcast(FP8X4),
-                            lhsT_scale=wo_s[WO_ROW + 4 * g : P, P * t : P * (t + 1)],
+                            lhsT_scale=w_s[WO_ROW + 4 * g : P, P * t : P * (t + 1)],
                             rhs=h_w[g][:, cols].bitcast(FP8X4), rhs_scale=h_s[g][:, cols],
                             start=(g == 0 and u == 0), stop=(g == 1 and u == per_bank - 1),
                         )
@@ -204,16 +219,10 @@ def tile_list_visit_risk_burden_kernel(
                     t = t0 + u
                     nc.scalar.activation(risk[:, t, :], z[:, u, :], SIGMOID, bias=bias[:, t : t + 1])
             for t in range(PACK):
-                if width == NARROW:
-                    nc.vector.tensor_scalar(y[:, t, :], risk[:, t, :], weight[:, t : t + 1], None, MULT)
-                else:
-                    nc.scalar.activation(y[:, t, :], risk[:, t, :], COPY, scale=weight[:, t : t + 1])
+                weigh(y[:, t, :], risk[:, t, :], t)
             nc.sync.dma_start(out=out_0[:, cols].rearrange("(p t) j -> p t j", t=PACK), in_=y[:])
-            return y
-
-        def round_y(copy, y, j0, width):
-            copy(out=y_bf[:, PACK * j0 : PACK * (j0 + width)].rearrange("p (n t) -> p n t", t=PACK),
-                 in_=y[:].rearrange("p t n -> p n t"))
+            round_copy(out=y_bf[:, PACK * j0 : PACK * (j0 + width)].rearrange("p (n t) -> p n t", t=PACK),
+                       in_=y[:].rearrange("p t n -> p n t"))
 
         def quantize_y(j0, width):
             cols = slice(j0, j0 + width)
@@ -230,65 +239,68 @@ def tile_list_visit_risk_burden_kernel(
         for f in range(2):
             gather(v_w[0][f][:], tab_w[0], list1, f * HALF, HALF)
         deal(wd_w[:].bitcast(U16), wd_raw[:].bitcast(U16), 8)
-        deal(wd_s[:], wd_s_raw[:], 16)
-        for t in range(PACK):
-            times_b(0, 0, t)
+        deal(w_s[:], w_s_raw[:], 16)
+        second, third, fourth = CHUNK, 2 * CHUNK, 3 * CHUNK
+        first, last = S - 2 * NARROW, S - NARROW
+
+        for j0 in (0, second):
+            for pair in range(2):
+                times_b(0, j0, pair)
         gather(v_s[:], tab_s, list1, 0, S)
         for a in range(2):
             quantize_wp(0, a)
-        for f in range(2):
-            gather(v_w[1][f][:], tab_w[1], list1, f * HALF, HALF)
+        gather(v_w[1][0][:], tab_w[1], list1, 0, HALF)
 
         for c in range(4):
             times_a(0, c * NARROW)
-        quantize_wp(1, 0)
+        gather(v_w[1][1][:], tab_w[1], list1, HALF, HALF)
         quantize_h(0, 0, HALF)
+        quantize_wp(1, 0)
         times_b(1, 0, 0)
-        times_b(1, 0, 2)
-        quantize_wp(1, 1)
         times_b(1, 0, 1)
-        times_a(1, 0)
-        times_b(1, 0, 3)
-        times_a(1, NARROW)
         deal(wo_w[:].rearrange("p a n -> p (a n)"), wo_raw[:].rearrange("p a n -> p (a n)"), 4)
-        deal(wo_s[:], wo_s_raw[:], 16)
+        quantize_wp(1, 1)
+        times_a(1, 0)
+        times_a(1, NARROW)
+        times_b(1, second, 0)
         quantize_h(1, 0, CHUNK)
-        round_y(nc.scalar.copy, make_y(0, CHUNK), 0, CHUNK)
-        times_a(1, CHUNK)
-        times_a(1, CHUNK + NARROW)
-        times_b(0, 1, 0)
-        quantize_h(1, CHUNK, CHUNK)
-        round_y(nc.scalar.copy, make_y(CHUNK, CHUNK), CHUNK, CHUNK)
-        times_b(0, 1, 1)
-        times_a(0, HALF)
-        times_b(1, 1, 0)
-        times_a(0, HALF + NARROW)
-        times_b(1, 1, 1)
-        quantize_h(0, HALF, CHUNK)
-        times_a(1, HALF)
-        times_b(0, 1, 2)
-        times_a(1, HALF + NARROW)
-        times_b(0, 1, 3)
-        quantize_h(1, HALF, CHUNK)
-        round_y(nc.scalar.copy, make_y(HALF, CHUNK), HALF, CHUNK)
-        first, last = S - 2 * NARROW, S - NARROW
-        times_b(1, 1, 2)
+        make_y(0, CHUNK, weigh_on_scalar, nc.scalar.copy)
+        times_b(1, second, 1)
+        times_a(1, second)
+        times_a(1, second + NARROW)
+        times_b(0, third, 0)
+        quantize_h(1, second, CHUNK)
+        make_y(second, CHUNK, weigh_on_scalar, nc.scalar.copy)
+        times_b(0, third, 1)
+        times_a(0, third)
+        times_b(1, third, 0)
+        times_a(0, third + NARROW)
+        times_b(1, third, 1)
+        quantize_h(0, third, CHUNK)
+        times_a(1, third)
+        times_b(0, fourth, 0)
+        times_a(1, third + NARROW)
+        times_b(0, fourth, 1)
+        quantize_h(1, third, CHUNK)
+        make_y(third, CHUNK, weigh_on_scalar, nc.scalar.copy)
+        times_b(1, fourth, 0)
         times_a(0, first)
-        times_b(1, 1, 3)
+        times_b(1, fourth, 1)
         times_a(0, last)
         times_a(1, first)
         quantize_h(0, first, CHUNK)
         quantize_h(1, first, NARROW)
         times_a(1, last)
+
         quantize_y(0, CHUNK)
         quantize_h(1, last, NARROW)
-        quantize_y(CHUNK, CHUNK)
+        quantize_y(second, CHUNK)
         store_words(0, HALF)
-        round_y(nc.vector.tensor_copy, make_y(first, NARROW), first, NARROW)
-        quantize_y(HALF, CHUNK)
+        make_y(first, NARROW, weigh_on_vector, nc.vector.tensor_copy)
+        quantize_y(third, CHUNK)
         quantize_y(first, NARROW)
         store_words(HALF, CHUNK + NARROW)
-        round_y(nc.vector.tensor_copy, make_y(last, NARROW), last, NARROW)
+        make_y(last, NARROW, weigh_on_vector, nc.vector.tensor_copy)
         quantize_y(last, NARROW)
         store_words(last, NARROW)
         for q in range(4):

@@ -14,7 +14,6 @@ U8 = mybir.dt.uint8
 FP8X4 = mybir.dt.float8_e4m3fn_x4
 FP4X4 = mybir.dt.float4_e2m1fn_x4
 MULT = mybir.AluOpType.mult
-ADD = mybir.AluOpType.add
 SIGMOID = mybir.ActivationFunctionType.Sigmoid
 COPY = mybir.ActivationFunctionType.Copy
 
@@ -35,10 +34,7 @@ def tile_list_visit_risk_burden_kernel(
     nc = tc.nc
     with ExitStack() as ctx:
         keep = ctx.enter_context(tc.tile_pool(name="keep", bufs=1))
-        ring = ctx.enter_context(tc.tile_pool(name="ring", bufs=3))
-        psum_b = ctx.enter_context(tc.psum_pool(name="psum_b", bufs=3))
-        psum_a = ctx.enter_context(tc.psum_pool(name="psum_a", bufs=3))
-        psum_z = ctx.enter_context(tc.psum_pool(name="psum_z", bufs=2))
+        psum = ctx.enter_context(tc.psum_pool(name="psum", bufs=1))
 
         def held(name, shape, dtype):
             return keep.tile(shape, dtype, name=name, align_bytes=64)
@@ -55,8 +51,10 @@ def tile_list_visit_risk_burden_kernel(
         v2_s = held("v2_s", [P, S], U8)
         wd_raw = held("wd_raw", [P, 2 * H], U8)
         wd_w = held("wd_w", [P, 2 * H], U8)
-        w_s_raw = held("w_s_raw", [P, H], U8)
-        w_s = held("w_s", [P, H], U8)
+        wd_s_raw = held("wd_s_raw", [P, H], U8)
+        wd_s = held("wd_s", [P, H], U8)
+        wo_s_raw = held("wo_s_raw", [P, N], U8)
+        wo_s = held("wo_s", [P, N], U8)
         wo_raw = held("wo_raw", [P, 2, N], I32)
         wo_w = held("wo_w", [P, 2, N], I32)
         wp_raw = [[held("wp_raw%d%d" % (g, a), [P, PACK, PASS], F32) for a in range(2)] for g in range(2)]
@@ -70,11 +68,26 @@ def tile_list_visit_risk_burden_kernel(
         bias = held("bias", [P, PACK], F32)
         weight = held("weight", [P, PACK], F32)
 
+        banks = [psum.tile([P, HALF], F32, name="bank%d" % i) for i in range(8)]
+        rings = {
+            "a": banks[0:3], "b": banks[3:6], "z": banks[6:8],
+            "rounded": [held("rounded%d" % i, [P, PACK * PASS], BF16) for i in range(2)],
+            "bt": [held("bt%d" % i, [P, PACK * CHUNK], F32) for i in range(4)],
+            "h_bf": [held("h_bf%d" % i, [P, PACK * HALF], BF16) for i in range(3)],
+            "risk": [held("risk%d" % i, [P, PACK * CHUNK], F32) for i in range(2)],
+            "y": [held("y%d" % i, [P, PACK * CHUNK], F32) for i in range(3)],
+        }
+
+        def take(name):
+            ring = rings[name]
+            ring.append(ring.pop(0))
+            return ring[-1]
+
         time_f = {}
         bt = {}
         h_bf = {}
 
-        for plane in (tab2_s, w_s_raw, tab_s):
+        for plane in (tab2_s, tab_s, wd_s_raw, wo_s_raw):
             nc.vector.memset(plane[:].bitcast(I32), 0)
 
         def words(dram):
@@ -107,7 +120,7 @@ def tile_list_visit_risk_burden_kernel(
         nc.sync.dma_start(list1[:], offs)
         load_table(tab_w[0], tab_words[0])
         nc.sync.dma_start(out=wd_raw[:].bitcast(I32), in_=wd_words[0].bitcast(I32))
-        load_scales(nc.sync, w_s_raw, wd_scales, 0)
+        load_scales(nc.sync, wd_s_raw, wd_scales, 0)
         load_time(0, 0, HALF)
         load_wp(0, 0)
         load_wp(0, 1)
@@ -119,8 +132,8 @@ def tile_list_visit_risk_burden_kernel(
         load_time(1, CHUNK, CHUNK)
         load_time(0, HALF, HALF)
         load_time(1, HALF, HALF)
-        load_scales(nc.gpsimd, w_s_raw, wo_scales, WO_ROW)
         load_scales(nc.gpsimd, tab_s, tab_scales, TAB_ROW)
+        load_scales(nc.gpsimd, wo_s_raw, wo_scales, WO_ROW)
         nc.gpsimd.dma_start(out=bias[:], in_=bo.rearrange("(p t) -> p t", t=PACK))
         nc.gpsimd.dma_start(out=weight[:], in_=cost.rearrange("(p t) -> p t", t=PACK))
 
@@ -134,21 +147,21 @@ def tile_list_visit_risk_burden_kernel(
             nc.vector.tensor_copy(dst, window[:].indirect(entries[:, first // 16 : (first + count) // 16]))
 
         def quantize_wp(g, a):
-            rounded = ring.tile([P, PACK * PASS], BF16, name="wp_rounded", align_bytes=64, bufs=2)
+            rounded = take("rounded")
             nc.scalar.copy(
                 out=rounded[:].rearrange("p (t m i) -> p m t i", t=PACK, i=PACK),
                 in_=wp_raw[g][a][:].rearrange("p i (m t) -> p m t i", t=PACK),
             )
             nc.vector.quantize_mx(out=wp_w[g][a][:].bitcast(FP8X4), scales=wp_s[g][a][:], in_=rounded[:])
 
-        def product_b(g, j0, pair, pool, tag):
+        def product_b(g, j0, pair, ring):
             f, c0 = divmod(j0, HALF)
-            b = pool.tile([P, 2, CHUNK], F32, name=tag)
+            b = take(ring)[:].rearrange("p (u n) -> p u n", u=2)
             for u in range(2):
                 s = PACK * g + 2 * pair + u
                 nc.tensor.matmul_mx(
                     out=b[:, u, :],
-                    lhsT=wd_w[:, 2 * P * s : 2 * P * (s + 1)].bitcast(FP4X4), lhsT_scale=w_s[:, P * s : P * (s + 1)],
+                    lhsT=wd_w[:, 2 * P * s : 2 * P * (s + 1)].bitcast(FP4X4), lhsT_scale=wd_s[:, P * s : P * (s + 1)],
                     rhs=v2_w[f][:, c0 : c0 + CHUNK].bitcast(FP8X4), rhs_scale=v2_s[:, j0 : j0 + CHUNK],
                     start=True, stop=True,
                 )
@@ -157,17 +170,23 @@ def tile_list_visit_risk_burden_kernel(
         def factors(g, j0, pair):
             return time_f[g, j0][:, 2 * pair : 2 * pair + 2, :]
 
+        def paired(flat):
+            return flat.rearrange("p (n t e) -> p n t e", t=PACK, e=2)
+
+        def in_pairs(rows):
+            return rows.rearrange("p t (n e) -> p n t e", e=2)
+
         def times_b(g, j0, pair):
             if (g, j0) not in bt:
-                bt[g, j0] = ring.tile([P, PACK, CHUNK], F32, name="bt", bufs=4)
-            b = product_b(g, j0, pair, psum_b, "b")
-            nc.vector.tensor_tensor(bt[g, j0][:, 2 * pair : 2 * pair + 2, :], b[:], factors(g, j0, pair), MULT)
+                bt[g, j0] = paired(take("bt")[:])
+            b = product_b(g, j0, pair, "b")
+            nc.vector.tensor_tensor(bt[g, j0][:, :, 2 * pair : 2 * pair + 2, :], in_pairs(b), in_pairs(factors(g, j0, pair)), MULT)
 
         def times_a(g, j0):
             f, c0 = divmod(j0, HALF)
             if (g, f) not in h_bf:
-                h_bf[g, f] = ring.tile([P, PACK * HALF], BF16, name="h_bf", align_bytes=64)
-            acc = psum_a.tile([P, PACK, NARROW], F32, name="a")
+                h_bf[g, f] = take("h_bf")
+            acc = take("a")[:].rearrange("p (t n) -> p t n", t=PACK)
             for a in range(2):
                 for t in range(PACK):
                     nc.tensor.matmul_mx(
@@ -178,11 +197,11 @@ def tile_list_visit_risk_burden_kernel(
                         start=(a == 0 and t == 0), stop=(a == 1 and t == PACK - 1),
                     )
             block0 = j0 - j0 % CHUNK
-            n0 = j0 - block0
+            n0 = (j0 - block0) // 2
             nc.vector.tensor_tensor(
-                h_bf[g, f][:, PACK * c0 : PACK * (c0 + NARROW)].rearrange("p (n e t) -> p n t e", e=2, t=PACK),
-                acc[:].rearrange("p t (n e) -> p n t e", e=2),
-                bt[g, block0][:, :, n0 : n0 + NARROW].rearrange("p t (n e) -> p n t e", e=2),
+                h_bf[g, f][:, PACK * c0 : PACK * (c0 + NARROW)].rearrange("p (n e t) -> p n e t", e=2, t=PACK),
+                acc.rearrange("p t (n e) -> p n e t", e=2),
+                bt[g, block0][:, n0 : n0 + NARROW // 2, :, :].rearrange("p n t e -> p n e t"),
                 MULT,
             )
 
@@ -200,18 +219,18 @@ def tile_list_visit_risk_burden_kernel(
 
         def make_y(j0, width, weigh, round_copy):
             cols = slice(j0, j0 + width)
-            risk = ring.tile([P, PACK, width], F32, name="risk", bufs=2)
-            y = ring.tile([P, PACK, width], F32, name="y")
+            risk = take("risk")[:, 0 : PACK * width].rearrange("p (t n) -> p t n", t=PACK)
+            y = take("y")[:, 0 : PACK * width].rearrange("p (t n) -> p t n", t=PACK)
             per_bank = HALF // width
             for t0 in range(0, PACK, per_bank):
-                z = psum_z.tile([P, per_bank, width], F32, name="z")
+                z = take("z")[:].rearrange("p (u n) -> p u n", u=per_bank)
                 for g in range(2):
                     for u in range(per_bank):
                         t = t0 + u
                         nc.tensor.matmul_mx(
                             out=z[:, u, :],
                             lhsT=wo_w[:, g, P * t : P * (t + 1)].bitcast(FP8X4),
-                            lhsT_scale=w_s[WO_ROW + 4 * g : P, P * t : P * (t + 1)],
+                            lhsT_scale=wo_s[WO_ROW + 4 * g : P, P * t : P * (t + 1)],
                             rhs=h_w[g][:, cols].bitcast(FP8X4), rhs_scale=h_s[g][:, cols],
                             start=(g == 0 and u == 0), stop=(g == 1 and u == per_bank - 1),
                         )
@@ -220,9 +239,9 @@ def tile_list_visit_risk_burden_kernel(
                     nc.scalar.activation(risk[:, t, :], z[:, u, :], SIGMOID, bias=bias[:, t : t + 1])
             for t in range(PACK):
                 weigh(y[:, t, :], risk[:, t, :], t)
-            nc.sync.dma_start(out=out_0[:, cols].rearrange("(p t) j -> p t j", t=PACK), in_=y[:])
+            nc.sync.dma_start(out=out_0[:, cols].rearrange("(p t) j -> p t j", t=PACK), in_=y)
             round_copy(out=y_bf[:, PACK * j0 : PACK * (j0 + width)].rearrange("p (n t) -> p n t", t=PACK),
-                       in_=y[:].rearrange("p t n -> p n t"))
+                       in_=y.rearrange("p t n -> p n t"))
 
         def quantize_y(j0, width):
             cols = slice(j0, j0 + width)
@@ -239,16 +258,16 @@ def tile_list_visit_risk_burden_kernel(
         for f in range(2):
             gather(v_w[0][f][:], tab_w[0], list1, f * HALF, HALF)
         deal(wd_w[:].bitcast(U16), wd_raw[:].bitcast(U16), 8)
-        deal(w_s[:], w_s_raw[:], 16)
+        deal(wd_s[:], wd_s_raw[:], 16)
         second, third, fourth = CHUNK, 2 * CHUNK, 3 * CHUNK
         first, last = S - 2 * NARROW, S - NARROW
-
         for j0 in (0, second):
             for pair in range(2):
                 times_b(0, j0, pair)
         gather(v_s[:], tab_s, list1, 0, S)
         for a in range(2):
             quantize_wp(0, a)
+
         gather(v_w[1][0][:], tab_w[1], list1, 0, HALF)
 
         for c in range(4):
@@ -259,6 +278,7 @@ def tile_list_visit_risk_burden_kernel(
         times_b(1, 0, 0)
         times_b(1, 0, 1)
         deal(wo_w[:].rearrange("p a n -> p (a n)"), wo_raw[:].rearrange("p a n -> p (a n)"), 4)
+        deal(wo_s[:], wo_s_raw[:], 16)
         quantize_wp(1, 1)
         times_a(1, 0)
         times_a(1, NARROW)

@@ -23,6 +23,7 @@ PASS = P * PACK
 HALF = 512
 NARROW = 128
 CHUNK = 256
+SLIM = 64
 TAB_ROW = 8
 WO_ROW = 4
 
@@ -127,9 +128,8 @@ def tile_list_visit_risk_burden_kernel(
         load_table(tab_w[1], tab_words[1])
         load_wp(1, 0)
         load_wp(1, 1)
-        load_time(1, 0, CHUNK)
+        load_time(1, 0, HALF)
         nc.sync.dma_start(out=wo_raw[:], in_=wo_words.rearrange("a p n t -> p a (n t)").bitcast(I32))
-        load_time(1, CHUNK, CHUNK)
         load_time(0, HALF, HALF)
         load_time(1, HALF, HALF)
         load_scales(nc.gpsimd, tab_s, tab_scales, TAB_ROW)
@@ -149,8 +149,8 @@ def tile_list_visit_risk_burden_kernel(
         def quantize_wp(g, a):
             rounded = take("rounded")
             nc.scalar.copy(
-                out=rounded[:].rearrange("p (t m i) -> p m t i", t=PACK, i=PACK),
-                in_=wp_raw[g][a][:].rearrange("p i (m t) -> p m t i", t=PACK),
+                out=rounded[:].rearrange("p (t m i) -> p m i t", t=PACK, i=PACK),
+                in_=wp_raw[g][a][:].rearrange("p i (m t) -> p m i t", t=PACK),
             )
             nc.vector.quantize_mx(out=wp_w[g][a][:].bitcast(FP8X4), scales=wp_s[g][a][:], in_=rounded[:])
 
@@ -180,13 +180,23 @@ def tile_list_visit_risk_burden_kernel(
             if (g, j0) not in bt:
                 bt[g, j0] = paired(take("bt")[:])
             b = product_b(g, j0, pair, "b")
-            nc.vector.tensor_tensor(bt[g, j0][:, :, 2 * pair : 2 * pair + 2, :], in_pairs(b), in_pairs(factors(g, j0, pair)), MULT)
+            nc.vector.tensor_tensor(bt[g, j0][:, :, 2 * pair : 2 * pair + 2, :], in_pairs(factors(g, j0, pair)), in_pairs(b), MULT)
 
-        def times_a(g, j0):
+        def park_b(g, j0, room):
+            bt[g, j0] = paired(room)
+            for pair in range(2):
+                nc.scalar.copy(out=bt[g, j0][:, :, 2 * pair : 2 * pair + 2, :], in_=in_pairs(product_b(g, j0, pair, "z")))
+
+        def times_parked_b(g, j0):
+            for c0 in range(0, CHUNK, SLIM):
+                rows = bt[g, j0][:, c0 // 2 : (c0 + SLIM) // 2, :, :]
+                nc.gpsimd.tensor_tensor(rows, rows, in_pairs(time_f[g, j0][:, :, c0 : c0 + SLIM]), MULT)
+
+        def times_a(g, j0, ring="a"):
             f, c0 = divmod(j0, HALF)
             if (g, f) not in h_bf:
                 h_bf[g, f] = take("h_bf")
-            acc = take("a")[:].rearrange("p (t n) -> p t n", t=PACK)
+            acc = take(ring)[:].rearrange("p (t n) -> p t n", t=PACK)
             for a in range(2):
                 for t in range(PACK):
                     nc.tensor.matmul_mx(
@@ -200,8 +210,8 @@ def tile_list_visit_risk_burden_kernel(
             n0 = (j0 - block0) // 2
             nc.vector.tensor_tensor(
                 h_bf[g, f][:, PACK * c0 : PACK * (c0 + NARROW)].rearrange("p (n e t) -> p n e t", e=2, t=PACK),
-                acc.rearrange("p t (n e) -> p n e t", e=2),
                 bt[g, block0][:, n0 : n0 + NARROW // 2, :, :].rearrange("p n t e -> p n e t"),
+                acc.rearrange("p t (n e) -> p n e t", e=2),
                 MULT,
             )
 
@@ -217,13 +227,12 @@ def tile_list_visit_risk_burden_kernel(
         def weigh_on_vector(y, risk, t):
             nc.vector.tensor_scalar(y, risk, weight[:, t : t + 1], None, MULT)
 
-        def make_y(j0, width, weigh, round_copy):
+        def make_y(j0, width, weigh, round_copy, ring="z", per_bank=2):
             cols = slice(j0, j0 + width)
             risk = take("risk")[:, 0 : PACK * width].rearrange("p (t n) -> p t n", t=PACK)
             y = take("y")[:, 0 : PACK * width].rearrange("p (t n) -> p t n", t=PACK)
-            per_bank = HALF // width
             for t0 in range(0, PACK, per_bank):
-                z = take("z")[:].rearrange("p (u n) -> p u n", u=per_bank)
+                z = take(ring)[:, 0 : per_bank * width].rearrange("p (u n) -> p u n", u=per_bank)
                 for g in range(2):
                     for u in range(per_bank):
                         t = t0 + u
@@ -240,17 +249,17 @@ def tile_list_visit_risk_burden_kernel(
             for t in range(PACK):
                 weigh(y[:, t, :], risk[:, t, :], t)
             nc.sync.dma_start(out=out_0[:, cols].rearrange("(p t) j -> p t j", t=PACK), in_=y)
-            round_copy(out=y_bf[:, PACK * j0 : PACK * (j0 + width)].rearrange("p (n t) -> p n t", t=PACK),
-                       in_=y.rearrange("p t n -> p n t"))
+            round_copy(out=y_bf[:, PACK * j0 : PACK * (j0 + width)].rearrange("p (n e t) -> p n t e", e=4, t=PACK),
+                       in_=y.rearrange("p t (n e) -> p n t e", e=4))
 
         def quantize_y(j0, width):
             cols = slice(j0, j0 + width)
             nc.vector.quantize_mx(out=y_w[:, cols].bitcast(FP8X4), scales=y_s[:, cols],
                                   in_=y_bf[:, PACK * j0 : PACK * (j0 + width)])
 
-        def store_words(j0, width):
+        def store_words(j0, width, queue):
             cols = slice(j0, j0 + width)
-            nc.sync.dma_start(out=words(out_1[0])[:, cols], in_=y_w[:, cols].bitcast(I32))
+            queue.dma_start(out=words(out_1[0])[:, cols], in_=y_w[:, cols].bitcast(I32))
 
         for f in range(2):
             gather(v2_w[f][:], tab2_w, list2, f * HALF, HALF)
@@ -267,11 +276,15 @@ def tile_list_visit_risk_burden_kernel(
         gather(v_s[:], tab_s, list1, 0, S)
         for a in range(2):
             quantize_wp(0, a)
+        room = wp_raw[0][1][:].rearrange("p i c -> p (i c)")
+        park_b(0, fourth, room[:, 0 : PACK * CHUNK])
+        park_b(1, fourth, room[:, PACK * CHUNK :])
 
         gather(v_w[1][0][:], tab_w[1], list1, 0, HALF)
 
-        for c in range(4):
+        for c in range(3):
             times_a(0, c * NARROW)
+        times_a(0, 3 * NARROW, "z")
         gather(v_w[1][1][:], tab_w[1], list1, HALF, HALF)
         quantize_h(0, 0, HALF)
         quantize_wp(1, 0)
@@ -289,6 +302,8 @@ def tile_list_visit_risk_burden_kernel(
         times_a(1, second)
         times_a(1, second + NARROW)
         times_b(0, third, 0)
+        times_parked_b(0, fourth)
+        times_parked_b(1, fourth)
         quantize_h(1, second, CHUNK)
         make_y(second, CHUNK, weigh_on_scalar, nc.scalar.copy)
         times_b(0, third, 1)
@@ -298,14 +313,10 @@ def tile_list_visit_risk_burden_kernel(
         times_b(1, third, 1)
         quantize_h(0, third, CHUNK)
         times_a(1, third)
-        times_b(0, fourth, 0)
         times_a(1, third + NARROW)
-        times_b(0, fourth, 1)
-        quantize_h(1, third, CHUNK)
-        make_y(third, CHUNK, weigh_on_scalar, nc.scalar.copy)
-        times_b(1, fourth, 0)
         times_a(0, first)
-        times_b(1, fourth, 1)
+        quantize_h(1, third, CHUNK)
+        make_y(third, CHUNK, weigh_on_scalar, nc.vector.tensor_copy)
         times_a(0, last)
         times_a(1, first)
         quantize_h(0, first, CHUNK)
@@ -315,13 +326,14 @@ def tile_list_visit_risk_burden_kernel(
         quantize_y(0, CHUNK)
         quantize_h(1, last, NARROW)
         quantize_y(second, CHUNK)
-        store_words(0, HALF)
+        store_words(0, HALF, nc.sync)
         make_y(first, NARROW, weigh_on_vector, nc.vector.tensor_copy)
         quantize_y(third, CHUNK)
         quantize_y(first, NARROW)
-        store_words(HALF, CHUNK + NARROW)
-        make_y(last, NARROW, weigh_on_vector, nc.vector.tensor_copy)
+        store_words(HALF, CHUNK + NARROW, nc.sync)
+        make_y(last, NARROW, weigh_on_vector, nc.vector.tensor_copy, "b")
         quantize_y(last, NARROW)
-        store_words(last, NARROW)
+        store_words(last, NARROW, nc.scalar)
         for q in range(4):
-            nc.scalar.dma_start(out=out_2[0, 4 * q : 4 * q + 4, :].bitcast(I32), in_=y_s[32 * q : 32 * q + 4, :].bitcast(I32))
+            queue = nc.sync if q < 3 else nc.scalar
+            queue.dma_start(out=out_2[0, 4 * q : 4 * q + 4, :].bitcast(I32), in_=y_s[32 * q : 32 * q + 4, :].bitcast(I32))

@@ -23,7 +23,6 @@ PASS = P * PACK
 HALF = 512
 NARROW = 128
 CHUNK = 256
-SLIM = 64
 TAB_ROW = 8
 WO_ROW = 4
 
@@ -46,9 +45,9 @@ def tile_list_visit_risk_burden_kernel(
         tab_s = held("tab_s", [P, T], U8)
         tab2_w = held("tab2_w", [P, T2], U32)
         tab2_s = held("tab2_s", [P, T2], U8)
-        v_w = [[held("v_w%d%d" % (a, f), [P, HALF], U32) for f in range(2)] for a in range(2)]
+        v_w = [held("v_w%d" % a, [P, S], U32) for a in range(2)]
         v_s = held("v_s", [P, S], U8)
-        v2_w = [held("v2_w%d" % f, [P, HALF], U32) for f in range(2)]
+        v2_w = held("v2_w", [P, S], U32)
         v2_s = held("v2_s", [P, S], U8)
         wd_raw = held("wd_raw", [P, 2 * H], U8)
         wd_w = held("wd_w", [P, 2 * H], U8)
@@ -58,26 +57,26 @@ def tile_list_visit_risk_burden_kernel(
         wo_s = held("wo_s", [P, N], U8)
         wo_raw = held("wo_raw", [P, 2, N], I32)
         wo_w = held("wo_w", [P, 2, N], I32)
-        wp_raw = [[held("wp_raw%d%d" % (g, a), [P, PACK, PASS], F32) for a in range(2)] for g in range(2)]
+        wp_raw = [[held("wp_raw%d%d" % (g, a), [P, PACK * PASS], F32) for a in range(2)] for g in range(2)]
         wp_w = [[held("wp_w%d%d" % (g, a), [P, PASS], U32) for a in range(2)] for g in range(2)]
         wp_s = [[held("wp_s%d%d" % (g, a), [P, PASS], U8) for a in range(2)] for g in range(2)]
-        h_w = [held("h_w%d" % g, [P, S], U32) for g in range(2)]
-        h_s = [held("h_s%d" % g, [P, S], U8) for g in range(2)]
+        h_w = held("h_w", [P, 2 * S], U32)
+        h_s = held("h_s", [P, 2 * S], U8)
         y_bf = held("y_bf", [P, PACK * S], BF16)
         y_w = held("y_w", [P, S], U32)
         y_s = held("y_s", [P, S], U8)
         bias = held("bias", [P, PACK], F32)
         weight = held("weight", [P, PACK], F32)
+        h_half = [wp_raw[1][1][:, i * PACK * CHUNK : (i + 1) * PACK * CHUNK].bitcast(BF16) for i in range(2)]
+        h_half.append(held("h_half2", [P, PACK * HALF], BF16))
 
         banks = [psum.tile([P, HALF], F32, name="bank%d" % i) for i in range(8)]
-        rings = {
-            "a": banks[0:3], "b": banks[3:6], "z": banks[6:8],
-            "rounded": [held("rounded%d" % i, [P, PACK * PASS], BF16) for i in range(2)],
-            "bt": [held("bt%d" % i, [P, PACK * CHUNK], F32) for i in range(4)],
-            "h_bf": [held("h_bf%d" % i, [P, PACK * HALF], BF16) for i in range(3)],
-            "risk": [held("risk%d" % i, [P, PACK * CHUNK], F32) for i in range(2)],
-            "y": [held("y%d" % i, [P, PACK * CHUNK], F32) for i in range(3)],
-        }
+        rings = {"a": banks[0:3], "b": banks[3:6], "z": banks[6:8]}
+        rings["rounded"] = [held("rounded%d" % i, [P, PACK * PASS], BF16) for i in range(2)]
+        bt_half = [held("bt_half%d" % i, [P, PACK * HALF], F32) for i in range(1)]
+        rings["bt"] = [bt_half[i][:, PACK * c0 : PACK * (c0 + CHUNK)] for i in range(1) for c0 in (0, CHUNK)]
+        rings["risk"] = [held("risk%d" % i, [P, PACK * CHUNK], F32) for i in range(3)]
+        rings["y"] = [held("y%d" % i, [P, PACK * CHUNK], F32) for i in range(4)]
 
         def take(name):
             ring = rings[name]
@@ -86,7 +85,20 @@ def tile_list_visit_risk_burden_kernel(
 
         time_f = {}
         bt = {}
-        h_bf = {}
+        parked = {}
+        rounded = {}
+        opened = {}
+        plain = {}
+        z_open = {}
+        risk = {}
+        y = {}
+
+        h_at = {}
+        for g in range(2):
+            for c in range(2):
+                for k in range(3):
+                    h_at[g, k * CHUNK + c * NARROW] = (k, g * CHUNK + c * NARROW, k * HALF + g * CHUNK + c * NARROW)
+                h_at[g, 3 * CHUNK + c * NARROW] = (0, c * CHUNK + g * NARROW, 3 * HALF + c * CHUNK + g * NARROW)
 
         for plane in (tab2_s, tab_s, wd_s_raw, wo_s_raw):
             nc.vector.memset(plane[:].bitcast(I32), 0)
@@ -101,41 +113,37 @@ def tile_list_visit_risk_burden_kernel(
                 queue.dma_start(out=plane[first : first + 4 * passes, 0 : scales.shape[2]].bitcast(I32),
                                 in_=scales[:, 4 * q : 4 * q + 4, :].bitcast(I32))
 
+        def load_scales_by_row(queue, plane, scales):
+            for r in range(4):
+                queue.dma_start(out=plane[r:P:32, :].bitcast(I32), in_=scales[0, r:16:4, :].bitcast(I32))
+
         def load_time(g, j0, width):
             tile = held("time%d_%d" % (g, j0), [P, PACK, width], F32)
             rows = tv[g * PASS : (g + 1) * PASS, j0 : j0 + width]
             nc.sync.dma_start(out=tile[:], in_=rows.rearrange("(p t) j -> p t j", t=PACK))
-            for c0 in range(0, width, CHUNK):
-                time_f[g, j0 + c0] = tile[:, :, c0 : c0 + CHUNK]
+            for c0 in range(0, width, NARROW):
+                time_f[g, j0 + c0] = (tile, c0)
+
+        def factors(g, j0, width):
+            tile, c0 = time_f[g, j0]
+            return tile[:, :, c0 : c0 + width]
 
         def load_wp(g, a):
             rows = wp[a * PASS : (a + 1) * PASS, g * PASS : (g + 1) * PASS]
-            nc.sync.dma_start(out=wp_raw[g][a][:], in_=rows.rearrange("(p i) c -> p i c", i=PACK))
+            nc.sync.dma_start(out=wp_raw[g][a][:].rearrange("p (i c) -> p i c", i=PACK), in_=rows.rearrange("(p i) c -> p i c", i=PACK))
 
         def load_table(tile, dram):
             nc.sync.dma_start(out=tile[:].bitcast(I32), in_=words(dram))
 
-        load_table(tab2_w, tab2_words[0])
-        nc.sync.dma_start(list2[:], offs2)
-        load_scales(nc.sync, tab2_s, tab2_scales, 0)
-        nc.sync.dma_start(list1[:], offs)
-        load_table(tab_w[0], tab_words[0])
-        nc.sync.dma_start(out=wd_raw[:].bitcast(I32), in_=wd_words[0].bitcast(I32))
-        load_scales(nc.sync, wd_s_raw, wd_scales, 0)
-        load_time(0, 0, HALF)
-        load_wp(0, 0)
-        load_wp(0, 1)
-        load_table(tab_w[1], tab_words[1])
-        load_wp(1, 0)
-        load_wp(1, 1)
-        load_time(1, 0, HALF)
-        nc.sync.dma_start(out=wo_raw[:], in_=wo_words.rearrange("a p n t -> p a (n t)").bitcast(I32))
-        load_time(0, HALF, HALF)
-        load_time(1, HALF, HALF)
-        load_scales(nc.gpsimd, tab_s, tab_scales, TAB_ROW)
-        load_scales(nc.gpsimd, wo_s_raw, wo_scales, WO_ROW)
-        nc.gpsimd.dma_start(out=bias[:], in_=bo.rearrange("(p t) -> p t", t=PACK))
-        nc.gpsimd.dma_start(out=weight[:], in_=cost.rearrange("(p t) -> p t", t=PACK))
+        def load_wd():
+            nc.sync.dma_start(out=wd_raw[:].bitcast(I32), in_=wd_words[0].bitcast(I32))
+
+        def load_wo():
+            nc.sync.dma_start(out=wo_raw[:], in_=wo_words.rearrange("a p n t -> p a (n t)").bitcast(I32))
+
+        def load_bias(queue):
+            queue.dma_start(out=bias[:], in_=bo.rearrange("(p t) -> p t", t=PACK))
+            queue.dma_start(out=weight[:], in_=cost.rearrange("(p t) -> p t", t=PACK))
 
         def deal(dst, src, run):
             nc.vector.tensor_copy(
@@ -143,32 +151,35 @@ def tile_list_visit_risk_burden_kernel(
                 in_=src.rearrange("p (g b m t) -> p g b t m", t=PACK, b=P // run, m=run),
             )
 
+        def deal_wd():
+            deal(wd_w[:].bitcast(U16), wd_raw[:].bitcast(U16), 8)
+            deal(wd_s[:], wd_s_raw[:], 16)
+
+        def deal_wo():
+            deal(wo_w[:].rearrange("p a n -> p (a n)"), wo_raw[:].rearrange("p a n -> p (a n)"), 4)
+
         def gather(dst, window, entries, first, count):
-            nc.vector.tensor_copy(dst, window[:].indirect(entries[:, first // 16 : (first + count) // 16]))
+            nc.vector.tensor_copy(dst[:, first : first + count], window[:].indirect(entries[:, first // 16 : (first + count) // 16]))
+
+        def round_wp(g, a, copy, m0=0, m1=P):
+            if (g, a) not in rounded:
+                rounded[g, a] = take("rounded")
+            copy(
+                out=rounded[g, a][:].rearrange("p (t m i) -> p m i t", t=PACK, i=PACK)[:, m0:m1, :, :],
+                in_=wp_raw[g][a][:].rearrange("p (i m t) -> p m i t", i=PACK, t=PACK)[:, m0:m1, :, :],
+            )
 
         def quantize_wp(g, a):
-            rounded = take("rounded")
-            nc.scalar.copy(
-                out=rounded[:].rearrange("p (t m i) -> p m i t", t=PACK, i=PACK),
-                in_=wp_raw[g][a][:].rearrange("p i (m t) -> p m i t", t=PACK),
+            nc.vector.quantize_mx(out=wp_w[g][a][:].bitcast(FP8X4), scales=wp_s[g][a][:], in_=rounded[g, a][:])
+
+        def product_b(out, g, t, j0, width):
+            s = PACK * g + t
+            nc.tensor.matmul_mx(
+                out=out,
+                lhsT=wd_w[:, 2 * P * s : 2 * P * (s + 1)].bitcast(FP4X4), lhsT_scale=wd_s[:, P * s : P * (s + 1)],
+                rhs=v2_w[:, j0 : j0 + width].bitcast(FP8X4), rhs_scale=v2_s[:, j0 : j0 + width],
+                start=True, stop=True,
             )
-            nc.vector.quantize_mx(out=wp_w[g][a][:].bitcast(FP8X4), scales=wp_s[g][a][:], in_=rounded[:])
-
-        def product_b(g, j0, pair, ring):
-            f, c0 = divmod(j0, HALF)
-            b = take(ring)[:].rearrange("p (u n) -> p u n", u=2)
-            for u in range(2):
-                s = PACK * g + 2 * pair + u
-                nc.tensor.matmul_mx(
-                    out=b[:, u, :],
-                    lhsT=wd_w[:, 2 * P * s : 2 * P * (s + 1)].bitcast(FP4X4), lhsT_scale=wd_s[:, P * s : P * (s + 1)],
-                    rhs=v2_w[f][:, c0 : c0 + CHUNK].bitcast(FP8X4), rhs_scale=v2_s[:, j0 : j0 + CHUNK],
-                    start=True, stop=True,
-                )
-            return b
-
-        def factors(g, j0, pair):
-            return time_f[g, j0][:, 2 * pair : 2 * pair + 2, :]
 
         def paired(flat):
             return flat.rearrange("p (n t e) -> p n t e", t=PACK, e=2)
@@ -176,81 +187,223 @@ def tile_list_visit_risk_burden_kernel(
         def in_pairs(rows):
             return rows.rearrange("p t (n e) -> p n t e", e=2)
 
-        def times_b(g, j0, pair):
+        def note_bt(g, j0, width, view):
+            for c0 in range(0, width, NARROW):
+                bt[g, j0 + c0] = (view, c0 // 2)
+
+        def pair_of_b(g, j0, pair, ring):
+            b = take(ring)[:, 0 : 2 * CHUNK].rearrange("p (u n) -> p u n", u=2)
+            for u in range(2):
+                product_b(b[:, u, :], g, 2 * pair + u, j0, CHUNK)
+            return b
+
+        def times_b(g, j0, pair, ring="b"):
             if (g, j0) not in bt:
-                bt[g, j0] = paired(take("bt")[:])
-            b = product_b(g, j0, pair, "b")
-            nc.vector.tensor_tensor(bt[g, j0][:, :, 2 * pair : 2 * pair + 2, :], in_pairs(factors(g, j0, pair)), in_pairs(b), MULT)
+                note_bt(g, j0, CHUNK, paired(take("bt")))
+            rows = slice(2 * pair, 2 * pair + 2)
+            nc.vector.tensor_tensor(bt[g, j0][0][:, :, rows, :], in_pairs(factors(g, j0, CHUNK)[:, rows, :]),
+                                    in_pairs(pair_of_b(g, j0, pair, ring)), MULT)
 
-        def park_b(g, j0, room):
-            bt[g, j0] = paired(room)
+        def times_wide_b(g, j0, ring="b"):
+            note_bt(g, j0, CHUNK, paired(take("bt")))
+            b = take(ring)[:].rearrange("p (t n) -> p t n", t=PACK)
+            for t in range(PACK):
+                product_b(b[:, t, :], g, t, j0, CHUNK)
+            nc.vector.tensor_tensor(bt[g, j0][0], in_pairs(factors(g, j0, CHUNK)), in_pairs(b), MULT)
+
+        def park_b(g, j0, room, ring="z"):
+            view = paired(room)
+            for c0 in range(0, CHUNK, NARROW):
+                parked[g, j0 + c0] = (view, c0 // 2)
             for pair in range(2):
-                nc.scalar.copy(out=bt[g, j0][:, :, 2 * pair : 2 * pair + 2, :], in_=in_pairs(product_b(g, j0, pair, "z")))
+                nc.scalar.copy(out=view[:, :, 2 * pair : 2 * pair + 2, :], in_=in_pairs(pair_of_b(g, j0, pair, ring)))
 
-        def times_parked_b(g, j0):
-            for c0 in range(0, CHUNK, SLIM):
-                rows = bt[g, j0][:, c0 // 2 : (c0 + SLIM) // 2, :, :]
-                nc.gpsimd.tensor_tensor(rows, rows, in_pairs(time_f[g, j0][:, :, c0 : c0 + SLIM]), MULT)
+        def times_half(g):
+            note_bt(g, 0, HALF, paired(bt_half[g][:]))
+            nc.vector.tensor_tensor(bt[g, 0][0], bt[g, 0][0], in_pairs(factors(g, 0, HALF)), MULT)
 
-        def times_a(g, j0, ring="a"):
-            f, c0 = divmod(j0, HALF)
-            if (g, f) not in h_bf:
-                h_bf[g, f] = take("h_bf")
-            acc = take(ring)[:].rearrange("p (t n) -> p t n", t=PACK)
-            for a in range(2):
-                for t in range(PACK):
-                    nc.tensor.matmul_mx(
-                        out=acc[:, t, :],
-                        lhsT=wp_w[g][a][:, P * t : P * (t + 1)].bitcast(FP8X4), lhsT_scale=wp_s[g][a][:, P * t : P * (t + 1)],
-                        rhs=v_w[a][f][:, c0 : c0 + NARROW].bitcast(FP8X4),
-                        rhs_scale=v_s[TAB_ROW + 4 * a : P, j0 : j0 + NARROW],
-                        start=(a == 0 and t == 0), stop=(a == 1 and t == PACK - 1),
-                    )
-            block0 = j0 - j0 % CHUNK
-            n0 = (j0 - block0) // 2
+        def times_parked(g, j0, width, engine, step, room=None):
+            view, n0 = parked[g, j0]
+            src = view[:, n0 : n0 + width // 2, :, :]
+            dst = src if room is None else paired(room)
+            note_bt(g, j0, width, dst)
+            for c0 in range(0, width, step):
+                cols = slice(c0 // 2, (c0 + step) // 2)
+                engine.tensor_tensor(dst[:, cols, :, :], src[:, cols, :, :], in_pairs(factors(g, j0 + c0 - c0 % NARROW, NARROW if step <= NARROW else step)[:, :, c0 % NARROW : c0 % NARROW + step]), MULT)
+
+        def pass_a(g, j0, a, width=NARROW):
+            if a == 0:
+                opened[g, j0] = take("a")[:, 0 : PACK * width].rearrange("p (t n) -> p t n", t=PACK)
+            per_bank = HALF // width
+            for t in range(PACK):
+                nc.tensor.matmul_mx(
+                    out=opened[g, j0][:, t, :],
+                    lhsT=wp_w[g][a][:, P * t : P * (t + 1)].bitcast(FP8X4), lhsT_scale=wp_s[g][a][:, P * t : P * (t + 1)],
+                    rhs=v_w[a][:, j0 : j0 + width].bitcast(FP8X4),
+                    rhs_scale=v_s[TAB_ROW + 4 * a : P, j0 : j0 + width],
+                    start=(a == 0 and t % per_bank == 0), stop=(a == 1 and t % per_bank == per_bank - 1),
+                )
+
+        def times_a(g, j0, width=NARROW):
+            if (g, j0) not in opened:
+                pass_a(g, j0, 0, width)
+            pass_a(g, j0, 1, width)
+            view, n0 = bt[g, j0]
+            i, c0, w0 = h_at[g, j0]
             nc.vector.tensor_tensor(
-                h_bf[g, f][:, PACK * c0 : PACK * (c0 + NARROW)].rearrange("p (n e t) -> p n e t", e=2, t=PACK),
-                bt[g, block0][:, n0 : n0 + NARROW // 2, :, :].rearrange("p n t e -> p n e t"),
-                acc.rearrange("p t (n e) -> p n e t", e=2),
+                h_half[i][:, PACK * c0 : PACK * (c0 + width)].rearrange("p (n e t) -> p n e t", e=2, t=PACK),
+                view[:, n0 : n0 + width // 2, :, :].rearrange("p n t e -> p n e t"),
+                opened[g, j0].rearrange("p t (n e) -> p n e t", e=2),
                 MULT,
             )
 
+        def a_times_parked(g, j0):
+            if (g, j0) not in opened:
+                pass_a(g, j0, 0)
+            pass_a(g, j0, 1)
+            view, n0 = parked[g, j0]
+            rows = view[:, n0 : n0 + NARROW // 2, :, :]
+            nc.vector.tensor_tensor(rows, rows, in_pairs(opened[g, j0]), MULT)
+
+        def finish_h(g, j0, engine, step):
+            view, n0 = parked[g, j0]
+            i, c0, w0 = h_at[g, j0]
+            for k in range(0, NARROW, step):
+                engine.tensor_tensor(
+                    h_half[i][:, PACK * (c0 + k) : PACK * (c0 + k + step)].rearrange("p (n e t) -> p n t e", e=2, t=PACK),
+                    view[:, n0 + k // 2 : n0 + (k + step) // 2, :, :],
+                    in_pairs(factors(g, j0, NARROW)[:, :, k : k + step]),
+                    MULT,
+                )
+
+        def park_plain(j0, room):
+            plain[j0] = room.rearrange("p (t n) -> p t n", t=PACK)
+            for pair in range(2):
+                nc.scalar.copy(out=plain[j0][:, 2 * pair : 2 * pair + 2, :], in_=pair_of_b(0, j0, pair, "b"))
+
+        def a_times_plain(j0):
+            if (0, j0) not in opened:
+                pass_a(0, j0, 0)
+            pass_a(0, j0, 1)
+            rows = plain[j0 - j0 % CHUNK][:, :, j0 % CHUNK : j0 % CHUNK + NARROW]
+            nc.vector.tensor_tensor(rows, rows, opened[0, j0], MULT)
+
+        def plain_times_time(j0, slices):
+            for t0 in range(0, PACK, slices):
+                rows = plain[j0][:, t0 : t0 + slices, :]
+                nc.gpsimd.tensor_tensor(rows, rows, factors(0, j0, CHUNK)[:, t0 : t0 + slices, :], MULT)
+
+        def round_h(j0, copy):
+            i, c0, w0 = h_at[0, j0]
+            copy(out=h_half[i][:, PACK * c0 : PACK * (c0 + CHUNK)].rearrange("p (n e t) -> p n t e", e=4, t=PACK),
+                 in_=plain[j0].rearrange("p t (n e) -> p n t e", e=4))
+
+        def finish_wide(j0):
+            view, n0 = parked[0, j0]
+            i, c0, w0 = h_at[0, j0]
+            nc.vector.tensor_tensor(
+                h_half[i][:, PACK * c0 : PACK * (c0 + CHUNK)].rearrange("p (n e t) -> p n t e", e=2, t=PACK),
+                view, in_pairs(factors(0, j0, CHUNK)), MULT)
+
         def quantize_h(g, j0, width):
-            f, c0 = divmod(j0, HALF)
-            cols = slice(j0, j0 + width)
-            nc.vector.quantize_mx(out=h_w[g][:, cols].bitcast(FP8X4), scales=h_s[g][:, cols],
-                                  in_=h_bf[g, f][:, PACK * c0 : PACK * (c0 + width)])
+            i, c0, w0 = h_at[g, j0]
+            nc.vector.quantize_mx(out=h_w[:, w0 : w0 + width].bitcast(FP8X4), scales=h_s[:, w0 : w0 + width],
+                                  in_=h_half[i][:, PACK * c0 : PACK * (c0 + width)])
 
-        def weigh_on_scalar(y, risk, t):
-            nc.scalar.activation(y, risk, COPY, scale=weight[:, t : t + 1])
+        def spent_h(g, j0):
+            i, c0, w0 = h_at[g, j0]
+            return h_half[i][:, PACK * c0 : PACK * (c0 + CHUNK)].bitcast(F32)
 
-        def weigh_on_vector(y, risk, t):
-            nc.vector.tensor_scalar(y, risk, weight[:, t : t + 1], None, MULT)
-
-        def make_y(j0, width, weigh, round_copy, ring="z", per_bank=2):
-            cols = slice(j0, j0 + width)
-            risk = take("risk")[:, 0 : PACK * width].rearrange("p (t n) -> p t n", t=PACK)
-            y = take("y")[:, 0 : PACK * width].rearrange("p (t n) -> p t n", t=PACK)
-            for t0 in range(0, PACK, per_bank):
-                z = take(ring)[:, 0 : per_bank * width].rearrange("p (u n) -> p u n", u=per_bank)
+        def make_risk(j0, width, ring="z"):
+            risk[j0] = take("risk")[:, 0 : PACK * width].rearrange("p (t n) -> p t n", t=PACK)
+            for t0 in range(0, PACK, 2):
+                z = take(ring)[:, 0 : 2 * width].rearrange("p (u n) -> p u n", u=2)
                 for g in range(2):
-                    for u in range(per_bank):
+                    w0 = h_at[g, j0][2]
+                    for u in range(2):
                         t = t0 + u
                         nc.tensor.matmul_mx(
                             out=z[:, u, :],
                             lhsT=wo_w[:, g, P * t : P * (t + 1)].bitcast(FP8X4),
                             lhsT_scale=wo_s[WO_ROW + 4 * g : P, P * t : P * (t + 1)],
-                            rhs=h_w[g][:, cols].bitcast(FP8X4), rhs_scale=h_s[g][:, cols],
-                            start=(g == 0 and u == 0), stop=(g == 1 and u == per_bank - 1),
+                            rhs=h_w[:, w0 : w0 + width].bitcast(FP8X4), rhs_scale=h_s[:, w0 : w0 + width],
+                            start=(g == 0 and u == 0), stop=(g == 1 and u == 1),
                         )
-                for u in range(per_bank):
+                for u in range(2):
                     t = t0 + u
-                    nc.scalar.activation(risk[:, t, :], z[:, u, :], SIGMOID, bias=bias[:, t : t + 1])
+                    nc.scalar.activation(risk[j0][:, t, :], z[:, u, :], SIGMOID, bias=bias[:, t : t + 1])
+
+        def make_y_by_pairs(j0):
+            risk[j0] = take("risk")[:].rearrange("p (t n) -> p t n", t=PACK)
+            y[j0] = take("y")[:].rearrange("p (t n) -> p t n", t=PACK)
+            for t0 in range(0, PACK, 2):
+                z = take("z")[:].rearrange("p (u n) -> p u n", u=2)
+                for g in range(2):
+                    w0 = h_at[g, j0][2]
+                    for u in range(2):
+                        t = t0 + u
+                        nc.tensor.matmul_mx(
+                            out=z[:, u, :],
+                            lhsT=wo_w[:, g, P * t : P * (t + 1)].bitcast(FP8X4),
+                            lhsT_scale=wo_s[WO_ROW + 4 * g : P, P * t : P * (t + 1)],
+                            rhs=h_w[:, w0 : w0 + CHUNK].bitcast(FP8X4), rhs_scale=h_s[:, w0 : w0 + CHUNK],
+                            start=(g == 0 and u == 0), stop=(g == 1 and u == 1),
+                        )
+                for u in range(2):
+                    nc.scalar.activation(risk[j0][:, t0 + u, :], z[:, u, :], SIGMOID, bias=bias[:, t0 + u : t0 + u + 1])
+                for u in range(2):
+                    weigh_on_scalar(y[j0][:, t0 + u, :], risk[j0][:, t0 + u, :], t0 + u)
+                rows = out_0[:, j0 : j0 + CHUNK].rearrange("(p t) j -> p t j", t=PACK)
+                nc.sync.dma_start(out=rows[:, t0 : t0 + 2, :], in_=y[j0][:, t0 : t0 + 2, :])
+
+        def pass_z(j0, width, g):
+            if g == 0:
+                z_open[j0] = [take("z")[:, 0 : 2 * width].rearrange("p (u n) -> p u n", u=2) for half in range(2)]
+            w0 = h_at[g, j0][2]
             for t in range(PACK):
-                weigh(y[:, t, :], risk[:, t, :], t)
-            nc.sync.dma_start(out=out_0[:, cols].rearrange("(p t) j -> p t j", t=PACK), in_=y)
-            round_copy(out=y_bf[:, PACK * j0 : PACK * (j0 + width)].rearrange("p (n e t) -> p n t e", e=4, t=PACK),
-                       in_=y.rearrange("p t (n e) -> p n t e", e=4))
+                nc.tensor.matmul_mx(
+                    out=z_open[j0][t // 2][:, t % 2, :],
+                    lhsT=wo_w[:, g, P * t : P * (t + 1)].bitcast(FP8X4),
+                    lhsT_scale=wo_s[WO_ROW + 4 * g : P, P * t : P * (t + 1)],
+                    rhs=h_w[:, w0 : w0 + width].bitcast(FP8X4), rhs_scale=h_s[:, w0 : w0 + width],
+                    start=(g == 0 and t % 2 == 0), stop=(g == 1 and t % 2 == 1),
+                )
+
+        def close_risk(j0, width):
+            pass_z(j0, width, 1)
+            risk[j0] = take("risk")[:, 0 : PACK * width].rearrange("p (t n) -> p t n", t=PACK)
+            for t in range(PACK):
+                nc.scalar.activation(risk[j0][:, t, :], z_open[j0][t // 2][:, t % 2, :], SIGMOID, bias=bias[:, t : t + 1])
+
+        def weigh_on_scalar(dst, src, t):
+            nc.scalar.activation(dst, src, COPY, scale=weight[:, t : t + 1])
+
+        def weigh_on_vector(dst, src, t):
+            nc.vector.tensor_scalar(dst, src, weight[:, t : t + 1], None, MULT)
+
+        def make_y(j0, weigh, queue=nc.sync):
+            width = risk[j0].shape[2]
+            y[j0] = take("y")[:, 0 : PACK * width].rearrange("p (t n) -> p t n", t=PACK)
+            for t in range(PACK):
+                weigh(y[j0][:, t, :], risk[j0][:, t, :], t)
+            queue.dma_start(out=out_0[:, j0 : j0 + width].rearrange("(p t) j -> p t j", t=PACK), in_=y[j0])
+
+        def round_y(j0, copy):
+            width = y[j0].shape[2]
+            copy(out=y_bf[:, PACK * j0 : PACK * (j0 + width)].rearrange("p (n e t) -> p n t e", e=4, t=PACK),
+                 in_=y[j0].rearrange("p t (n e) -> p n t e", e=4))
+
+        def weigh_and_round(j0):
+            width = risk[j0].shape[2]
+            nc.vector.tensor_tensor(
+                y_bf[:, PACK * j0 : PACK * (j0 + width)].rearrange("p (n e t) -> p n t e", e=2, t=PACK),
+                risk[j0].rearrange("p t (n e) -> p n t e", e=2),
+                weight[:].unsqueeze(1).unsqueeze(3).to_broadcast([P, width // 2, PACK, 2]),
+                MULT,
+            )
+
+        def on_gpsimd(out, in_):
+            nc.gpsimd.tensor_scalar(out, in_, 1.0, 0.0, MULT, mybir.AluOpType.add)
 
         def quantize_y(j0, width):
             cols = slice(j0, j0 + width)
@@ -261,79 +414,114 @@ def tile_list_visit_risk_burden_kernel(
             cols = slice(j0, j0 + width)
             queue.dma_start(out=words(out_1[0])[:, cols], in_=y_w[:, cols].bitcast(I32))
 
-        for f in range(2):
-            gather(v2_w[f][:], tab2_w, list2, f * HALF, HALF)
-        gather(v2_s[:], tab2_s, list2, 0, S)
-        for f in range(2):
-            gather(v_w[0][f][:], tab_w[0], list1, f * HALF, HALF)
-        deal(wd_w[:].bitcast(U16), wd_raw[:].bitcast(U16), 8)
-        deal(wd_s[:], wd_s_raw[:], 16)
+        def store_scales(queues):
+            for r in range(4):
+                queues[r].dma_start(out=out_2[0, r:16:4, :].bitcast(I32), in_=y_s[r:P:32, :].bitcast(I32))
+
+        on_scalar, on_vector = nc.scalar.copy, nc.vector.tensor_copy
         second, third, fourth = CHUNK, 2 * CHUNK, 3 * CHUNK
         first, last = S - 2 * NARROW, S - NARROW
-        for j0 in (0, second):
-            for pair in range(2):
-                times_b(0, j0, pair)
-        gather(v_s[:], tab_s, list1, 0, S)
-        for a in range(2):
-            quantize_wp(0, a)
-        room = wp_raw[0][1][:].rearrange("p i c -> p (i c)")
-        park_b(0, fourth, room[:, 0 : PACK * CHUNK])
-        park_b(1, fourth, room[:, PACK * CHUNK :])
 
-        gather(v_w[1][0][:], tab_w[1], list1, 0, HALF)
-
+        load_table(tab2_w, tab2_words[0])
+        nc.sync.dma_start(list2[:], offs2)
+        load_scales_by_row(nc.sync, tab2_s, tab2_scales)
+        nc.sync.dma_start(list1[:], offs)
+        load_table(tab_w[0], tab_words[0])
+        load_wd()
+        load_scales_by_row(nc.sync, wd_s_raw, wd_scales)
+        load_wp(0, 0)
+        load_wp(0, 1)
+        load_table(tab_w[1], tab_words[1])
+        load_time(0, 0, HALF)
+        load_wp(1, 0)
+        load_wp(1, 1)
+        load_time(1, 0, CHUNK)
+        load_wo()
+        load_time(1, CHUNK, CHUNK)
+        load_time(0, HALF, HALF)
+        load_time(1, HALF, HALF)
+        load_scales(nc.gpsimd, tab_s, tab_scales, TAB_ROW)
+        load_scales(nc.gpsimd, wo_s_raw, wo_scales, WO_ROW)
+        load_bias(nc.gpsimd)
+        gather(v2_w, tab2_w, list2, 0, S)
+        gather(v2_s, tab2_s, list2, 0, S)
+        deal_wd()
+        gather(v_w[0], tab_w[0], list1, 0, S)
+        gather(v_s, tab_s, list1, 0, S)
+        deal(wo_s[:], wo_s_raw[:], 16)
+        round_wp(0, 0, on_scalar)
+        quantize_wp(0, 0)
+        round_wp(0, 1, on_scalar)
+        quantize_wp(0, 1)
+        park_plain(0, wp_raw[0][1][:, 0 : PACK * CHUNK])
+        park_plain(second, wp_raw[0][1][:, PACK * CHUNK :])
+        park_b(0, third, wp_raw[0][0][:, 0 : PACK * CHUNK], "b")
+        park_b(0, fourth, wp_raw[0][0][:, PACK * CHUNK :], "b")
         for c in range(3):
-            times_a(0, c * NARROW)
-        times_a(0, 3 * NARROW, "z")
-        gather(v_w[1][1][:], tab_w[1], list1, HALF, HALF)
-        quantize_h(0, 0, HALF)
+            pass_a(0, c * NARROW, 0)
+        gather(v_w[1], tab_w[1], list1, 0, HALF)
+        gather(v_w[1], tab_w[1], list1, HALF, HALF)
+        for j0 in range(0, HALF, NARROW):
+            a_times_plain(j0)
+        for j0 in range(HALF, S, NARROW):
+            a_times_parked(0, j0)
+        plain_times_time(0, 2)
+        plain_times_time(second, 2)
+        round_wp(1, 0, on_scalar)
+        round_wp(1, 1, on_scalar)
+        round_h(0, on_scalar)
+        round_h(second, on_scalar)
         quantize_wp(1, 0)
         times_b(1, 0, 0)
         times_b(1, 0, 1)
-        deal(wo_w[:].rearrange("p a n -> p (a n)"), wo_raw[:].rearrange("p a n -> p (a n)"), 4)
-        deal(wo_s[:], wo_s_raw[:], 16)
+        for c in range(3):
+            pass_a(1, c * NARROW, 0)
         quantize_wp(1, 1)
+        deal_wo()
         times_a(1, 0)
         times_a(1, NARROW)
         times_b(1, second, 0)
-        quantize_h(1, 0, CHUNK)
-        make_y(0, CHUNK, weigh_on_scalar, nc.scalar.copy)
+        quantize_h(0, 0, HALF)
+        make_risk(0, CHUNK)
+        make_y(0, weigh_on_scalar)
+        round_y(0, on_scalar)
         times_b(1, second, 1)
         times_a(1, second)
         times_a(1, second + NARROW)
-        times_b(0, third, 0)
-        times_parked_b(0, fourth)
-        times_parked_b(1, fourth)
-        quantize_h(1, second, CHUNK)
-        make_y(second, CHUNK, weigh_on_scalar, nc.scalar.copy)
-        times_b(0, third, 1)
-        times_a(0, third)
+        finish_wide(third)
+        quantize_h(0, second, HALF)
+        make_risk(second, CHUNK)
+        make_y(second, weigh_on_scalar)
         times_b(1, third, 0)
-        times_a(0, third + NARROW)
         times_b(1, third, 1)
-        quantize_h(0, third, CHUNK)
         times_a(1, third)
         times_a(1, third + NARROW)
-        times_a(0, first)
-        quantize_h(1, third, CHUNK)
-        make_y(third, CHUNK, weigh_on_scalar, nc.vector.tensor_copy)
-        times_a(0, last)
-        times_a(1, first)
-        quantize_h(0, first, CHUNK)
-        quantize_h(1, first, NARROW)
-        times_a(1, last)
-
+        times_b(1, fourth, 0)
         quantize_y(0, CHUNK)
-        quantize_h(1, last, NARROW)
+        store_words(0, CHUNK, nc.sync)
+        quantize_h(0, third, HALF)
+        make_y_by_pairs(third)
+        times_b(1, fourth, 1)
+        rings["z"] = rings["z"] + rings["b"][0:2]
+        finish_h(0, first, nc.vector, NARROW)
+        times_a(1, first)
+        finish_h(0, last, nc.vector, NARROW)
+        quantize_h(0, first, CHUNK)
+        make_risk(first, NARROW)
+        times_a(1, last)
+        quantize_h(0, last, CHUNK)
+        make_risk(last, NARROW)
+        round_y(second, on_vector)
         quantize_y(second, CHUNK)
-        store_words(0, HALF, nc.sync)
-        make_y(first, NARROW, weigh_on_vector, nc.vector.tensor_copy)
+        store_words(second, CHUNK, nc.sync)
+        round_y(third, on_vector)
+        make_y(first, weigh_on_vector)
+        round_y(first, on_vector)
+        make_y(last, weigh_on_scalar)
         quantize_y(third, CHUNK)
+        store_words(third, CHUNK, nc.sync)
+        weigh_and_round(last)
         quantize_y(first, NARROW)
-        store_words(HALF, CHUNK + NARROW, nc.sync)
-        make_y(last, NARROW, weigh_on_vector, nc.vector.tensor_copy, "b")
         quantize_y(last, NARROW)
-        store_words(last, NARROW, nc.scalar)
-        for q in range(4):
-            queue = nc.sync if q < 3 else nc.scalar
-            queue.dma_start(out=out_2[0, 4 * q : 4 * q + 4, :].bitcast(I32), in_=y_s[32 * q : 32 * q + 4, :].bitcast(I32))
+        store_words(first, CHUNK, nc.sync)
+        store_scales([nc.scalar] * 4)

@@ -14,6 +14,7 @@ U8 = mybir.dt.uint8
 FP8X4 = mybir.dt.float8_e4m3fn_x4
 FP4X4 = mybir.dt.float4_e2m1fn_x4
 MULT = mybir.AluOpType.mult
+ADD = mybir.AluOpType.add
 SIGMOID = mybir.ActivationFunctionType.Sigmoid
 COPY = mybir.ActivationFunctionType.Copy
 
@@ -67,14 +68,13 @@ def tile_list_visit_risk_burden_kernel(
         y_s = held("y_s", [P, S], U8)
         bias = held("bias", [P, PACK], F32)
         weight = held("weight", [P, PACK], F32)
-        h_half = [wp_raw[1][1][:, i * PACK * CHUNK : (i + 1) * PACK * CHUNK].bitcast(BF16) for i in range(2)]
+        h_half = [wp_raw[0][0][:, i * PACK * CHUNK : (i + 1) * PACK * CHUNK].bitcast(BF16) for i in range(2)]
         h_half.append(held("h_half2", [P, PACK * HALF], BF16))
+        rooms = [held("room%d" % i, [P, PACK * CHUNK], F32) for i in range(4)]
 
-        banks = [psum.tile([P, HALF], F32, name="bank%d" % i) for i in range(8)]
-        rings = {"a": banks[0:3], "b": banks[3:6], "z": banks[6:8]}
+        bank = [psum.tile([P, HALF], F32, name="bank%d" % i) for i in range(8)]
+        rings = {}
         rings["rounded"] = [held("rounded%d" % i, [P, PACK * PASS], BF16) for i in range(2)]
-        bt_half = [held("bt_half%d" % i, [P, PACK * HALF], F32) for i in range(1)]
-        rings["bt"] = [bt_half[i][:, PACK * c0 : PACK * (c0 + CHUNK)] for i in range(1) for c0 in (0, CHUNK)]
         rings["risk"] = [held("risk%d" % i, [P, PACK * CHUNK], F32) for i in range(3)]
         rings["y"] = [held("y%d" % i, [P, PACK * CHUNK], F32) for i in range(4)]
 
@@ -84,14 +84,12 @@ def tile_list_visit_risk_burden_kernel(
             return ring[-1]
 
         time_f = {}
-        bt = {}
-        parked = {}
-        rounded = {}
-        opened = {}
+        partial = {}
         plain = {}
-        z_open = {}
+        rounded = {}
         risk = {}
         y = {}
+        opened = set()
 
         h_at = {}
         for g in range(2):
@@ -100,18 +98,16 @@ def tile_list_visit_risk_burden_kernel(
                     h_at[g, k * CHUNK + c * NARROW] = (k, g * CHUNK + c * NARROW, k * HALF + g * CHUNK + c * NARROW)
                 h_at[g, 3 * CHUNK + c * NARROW] = (0, c * CHUNK + g * NARROW, 3 * HALF + c * CHUNK + g * NARROW)
 
-        for plane in (tab2_s, tab_s, wd_s_raw, wo_s_raw):
+        for plane in (tab_s, tab2_s, wd_s_raw, wo_s_raw):
             nc.vector.memset(plane[:].bitcast(I32), 0)
 
         def words(dram):
             return dram.rearrange("p n t -> p (n t)").bitcast(I32)
 
-        def load_scales(queue, plane, scales, row):
-            passes = scales.shape[0]
-            for q in range(4):
-                first = 32 * q + row
-                queue.dma_start(out=plane[first : first + 4 * passes, 0 : scales.shape[2]].bitcast(I32),
-                                in_=scales[:, 4 * q : 4 * q + 4, :].bitcast(I32))
+        def load_scales(queue, plane, scales, row, q):
+            first = 32 * q + row
+            queue.dma_start(out=plane[first : first + 4 * scales.shape[0], :].bitcast(I32),
+                            in_=scales[:, 4 * q : 4 * q + 4, :].bitcast(I32))
 
         def load_scales_by_row(queue, plane, scales):
             for r in range(4):
@@ -125,7 +121,8 @@ def tile_list_visit_risk_burden_kernel(
                 time_f[g, j0 + c0] = (tile, c0)
 
         def factors(g, j0, width):
-            tile, c0 = time_f[g, j0]
+            tile, c0 = time_f[g, j0 - j0 % NARROW]
+            c0 = c0 + j0 % NARROW
             return tile[:, :, c0 : c0 + width]
 
         def load_wp(g, a):
@@ -141,22 +138,17 @@ def tile_list_visit_risk_burden_kernel(
         def load_wo():
             nc.sync.dma_start(out=wo_raw[:], in_=wo_words.rearrange("a p n t -> p a (n t)").bitcast(I32))
 
-        def load_bias(queue):
-            queue.dma_start(out=bias[:], in_=bo.rearrange("(p t) -> p t", t=PACK))
-            queue.dma_start(out=weight[:], in_=cost.rearrange("(p t) -> p t", t=PACK))
+        def load_by_slices(tile, vector):
+            nc.sync.dma_start(out=tile[:], in_=vector.rearrange("(p t) -> p t", t=PACK))
 
-        def deal(dst, src, run):
-            nc.vector.tensor_copy(
+        def deal(engine, dst, src, run):
+            engine.tensor_copy(
                 out=dst.rearrange("p (g t b m) -> p g b t m", t=PACK, b=P // run, m=run),
                 in_=src.rearrange("p (g b m t) -> p g b t m", t=PACK, b=P // run, m=run),
             )
 
-        def deal_wd():
-            deal(wd_w[:].bitcast(U16), wd_raw[:].bitcast(U16), 8)
-            deal(wd_s[:], wd_s_raw[:], 16)
-
-        def deal_wo():
-            deal(wo_w[:].rearrange("p a n -> p (a n)"), wo_raw[:].rearrange("p a n -> p (a n)"), 4)
+        def deal_wo(engine):
+            deal(engine, wo_w[:].rearrange("p a n -> p (a n)"), wo_raw[:].rearrange("p a n -> p (a n)"), 4)
 
         def gather(dst, window, entries, first, count):
             nc.vector.tensor_copy(dst[:, first : first + count], window[:].indirect(entries[:, first // 16 : (first + count) // 16]))
@@ -172,208 +164,134 @@ def tile_list_visit_risk_burden_kernel(
         def quantize_wp(g, a):
             nc.vector.quantize_mx(out=wp_w[g][a][:].bitcast(FP8X4), scales=wp_s[g][a][:], in_=rounded[g, a][:])
 
-        def product_b(out, g, t, j0, width):
-            s = PACK * g + t
-            nc.tensor.matmul_mx(
-                out=out,
-                lhsT=wd_w[:, 2 * P * s : 2 * P * (s + 1)].bitcast(FP4X4), lhsT_scale=wd_s[:, P * s : P * (s + 1)],
-                rhs=v2_w[:, j0 : j0 + width].bitcast(FP8X4), rhs_scale=v2_s[:, j0 : j0 + width],
-                start=True, stop=True,
-            )
-
         def paired(flat):
             return flat.rearrange("p (n t e) -> p n t e", t=PACK, e=2)
 
         def in_pairs(rows):
             return rows.rearrange("p t (n e) -> p n t e", e=2)
 
-        def note_bt(g, j0, width, view):
-            for c0 in range(0, width, NARROW):
-                bt[g, j0 + c0] = (view, c0 // 2)
+        def slices(b, count):
+            return bank[b][:].rearrange("p (t n) -> p t n", t=count)
 
-        def pair_of_b(g, j0, pair, ring):
-            b = take(ring)[:, 0 : 2 * CHUNK].rearrange("p (u n) -> p u n", u=2)
+        def part(g, j0, width):
+            c0 = j0 % CHUNK
+            return partial[g, j0 - c0][:, c0 // 2 : (c0 + width) // 2, :, :]
+
+        def product_b(g, j0, pair, b):
             for u in range(2):
-                product_b(b[:, u, :], g, 2 * pair + u, j0, CHUNK)
-            return b
-
-        def times_b(g, j0, pair, ring="b"):
-            if (g, j0) not in bt:
-                note_bt(g, j0, CHUNK, paired(take("bt")))
-            rows = slice(2 * pair, 2 * pair + 2)
-            nc.vector.tensor_tensor(bt[g, j0][0][:, :, rows, :], in_pairs(factors(g, j0, CHUNK)[:, rows, :]),
-                                    in_pairs(pair_of_b(g, j0, pair, ring)), MULT)
-
-        def times_wide_b(g, j0, ring="b"):
-            note_bt(g, j0, CHUNK, paired(take("bt")))
-            b = take(ring)[:].rearrange("p (t n) -> p t n", t=PACK)
-            for t in range(PACK):
-                product_b(b[:, t, :], g, t, j0, CHUNK)
-            nc.vector.tensor_tensor(bt[g, j0][0], in_pairs(factors(g, j0, CHUNK)), in_pairs(b), MULT)
-
-        def park_b(g, j0, room, ring="z"):
-            view = paired(room)
-            for c0 in range(0, CHUNK, NARROW):
-                parked[g, j0 + c0] = (view, c0 // 2)
-            for pair in range(2):
-                nc.scalar.copy(out=view[:, :, 2 * pair : 2 * pair + 2, :], in_=in_pairs(pair_of_b(g, j0, pair, ring)))
-
-        def times_half(g):
-            note_bt(g, 0, HALF, paired(bt_half[g][:]))
-            nc.vector.tensor_tensor(bt[g, 0][0], bt[g, 0][0], in_pairs(factors(g, 0, HALF)), MULT)
-
-        def times_parked(g, j0, width, engine, step, room=None):
-            view, n0 = parked[g, j0]
-            src = view[:, n0 : n0 + width // 2, :, :]
-            dst = src if room is None else paired(room)
-            note_bt(g, j0, width, dst)
-            for c0 in range(0, width, step):
-                cols = slice(c0 // 2, (c0 + step) // 2)
-                engine.tensor_tensor(dst[:, cols, :, :], src[:, cols, :, :], in_pairs(factors(g, j0 + c0 - c0 % NARROW, NARROW if step <= NARROW else step)[:, :, c0 % NARROW : c0 % NARROW + step]), MULT)
-
-        def pass_a(g, j0, a, width=NARROW):
-            if a == 0:
-                opened[g, j0] = take("a")[:, 0 : PACK * width].rearrange("p (t n) -> p t n", t=PACK)
-            per_bank = HALF // width
-            for t in range(PACK):
+                s = PACK * g + 2 * pair + u
                 nc.tensor.matmul_mx(
-                    out=opened[g, j0][:, t, :],
+                    out=slices(b, 2)[:, u, :],
+                    lhsT=wd_w[:, 2 * P * s : 2 * P * (s + 1)].bitcast(FP4X4), lhsT_scale=wd_s[:, P * s : P * (s + 1)],
+                    rhs=v2_w[:, j0 : j0 + CHUNK].bitcast(FP8X4), rhs_scale=v2_s[:, j0 : j0 + CHUNK],
+                    start=True, stop=True,
+                )
+            return in_pairs(slices(b, 2))
+
+        def park_b(g, j0, room, banks):
+            partial[g, j0] = paired(room)
+            for pair in range(2):
+                nc.scalar.copy(out=partial[g, j0][:, :, 2 * pair : 2 * pair + 2, :], in_=product_b(g, j0, pair, banks[pair]))
+
+        def b_times_time(g, j0, pair, room, b):
+            partial[g, j0] = paired(room)
+            rows = slice(2 * pair, 2 * pair + 2)
+            nc.vector.tensor_tensor(partial[g, j0][:, :, rows, :], in_pairs(factors(g, j0, CHUNK)[:, rows, :]),
+                                    product_b(g, j0, pair, b), MULT)
+
+        def parked_times_time(g, j0, step):
+            for c0 in range(j0, j0 + CHUNK, step):
+                nc.gpsimd.tensor_tensor(part(g, c0, step), part(g, c0, step), in_pairs(factors(g, c0, step)), MULT)
+
+        def park_plain(g, j0, room, banks):
+            plain[g, j0] = room.rearrange("p (t n) -> p t n", t=PACK)
+            partial[g, j0] = in_pairs(plain[g, j0])
+            for pair in range(2):
+                product_b(g, j0, pair, banks[pair])
+                nc.scalar.copy(out=plain[g, j0][:, 2 * pair : 2 * pair + 2, :], in_=slices(banks[pair], 2))
+
+        def plain_times_time(g, j0, step):
+            for t0 in range(0, PACK, step):
+                rows = plain[g, j0][:, t0 : t0 + step, :]
+                nc.gpsimd.tensor_tensor(rows, rows, factors(g, j0, CHUNK)[:, t0 : t0 + step, :], MULT)
+
+        def h_by_a_plain(g, j0, b):
+            pass_a(g, j0, 1, b, 0, PACK)
+            nc.vector.tensor_tensor(
+                h_of(g, j0, NARROW).rearrange("p (n e t) -> p n t e", e=2, t=PACK),
+                part(g, j0, NARROW), in_pairs(slices(b, PACK)), MULT)
+
+        def pass_a(g, j0, a, b, t0, count):
+            width = HALF // count
+            for u in range(count):
+                t = t0 + u
+                nc.tensor.matmul_mx(
+                    out=slices(b, count)[:, u, :],
                     lhsT=wp_w[g][a][:, P * t : P * (t + 1)].bitcast(FP8X4), lhsT_scale=wp_s[g][a][:, P * t : P * (t + 1)],
                     rhs=v_w[a][:, j0 : j0 + width].bitcast(FP8X4),
                     rhs_scale=v_s[TAB_ROW + 4 * a : P, j0 : j0 + width],
-                    start=(a == 0 and t % per_bank == 0), stop=(a == 1 and t % per_bank == per_bank - 1),
+                    start=(a == 0 and u == 0), stop=(a == 1 and u == count - 1),
                 )
 
-        def times_a(g, j0, width=NARROW):
-            if (g, j0) not in opened:
-                pass_a(g, j0, 0, width)
-            pass_a(g, j0, 1, width)
-            view, n0 = bt[g, j0]
+        def h_of(g, j0, width):
             i, c0, w0 = h_at[g, j0]
+            return h_half[i][:, PACK * c0 : PACK * (c0 + width)]
+
+        def a_times_parked(g, j0, pair, b):
+            pass_a(g, j0, 1, b, 2 * pair, 2)
+            rows = partial[g, j0][:, :, 2 * pair : 2 * pair + 2, :]
+            nc.vector.tensor_tensor(rows, rows, in_pairs(slices(b, 2)), MULT)
+
+        def h_by_a(g, j0, b):
+            pass_a(g, j0, 1, b, 0, PACK)
             nc.vector.tensor_tensor(
-                h_half[i][:, PACK * c0 : PACK * (c0 + width)].rearrange("p (n e t) -> p n e t", e=2, t=PACK),
-                view[:, n0 : n0 + width // 2, :, :].rearrange("p n t e -> p n e t"),
-                opened[g, j0].rearrange("p t (n e) -> p n e t", e=2),
+                h_of(g, j0, NARROW).rearrange("p (n e t) -> p n e t", e=2, t=PACK),
+                part(g, j0, NARROW).rearrange("p n t e -> p n e t"),
+                slices(b, PACK).rearrange("p t (n e) -> p n e t", e=2),
                 MULT,
             )
 
-        def a_times_parked(g, j0):
-            if (g, j0) not in opened:
-                pass_a(g, j0, 0)
-            pass_a(g, j0, 1)
-            view, n0 = parked[g, j0]
-            rows = view[:, n0 : n0 + NARROW // 2, :, :]
-            nc.vector.tensor_tensor(rows, rows, in_pairs(opened[g, j0]), MULT)
-
-        def finish_h(g, j0, engine, step):
-            view, n0 = parked[g, j0]
-            i, c0, w0 = h_at[g, j0]
-            for k in range(0, NARROW, step):
-                engine.tensor_tensor(
-                    h_half[i][:, PACK * (c0 + k) : PACK * (c0 + k + step)].rearrange("p (n e t) -> p n t e", e=2, t=PACK),
-                    view[:, n0 + k // 2 : n0 + (k + step) // 2, :, :],
-                    in_pairs(factors(g, j0, NARROW)[:, :, k : k + step]),
-                    MULT,
-                )
-
-        def park_plain(j0, room):
-            plain[j0] = room.rearrange("p (t n) -> p t n", t=PACK)
-            for pair in range(2):
-                nc.scalar.copy(out=plain[j0][:, 2 * pair : 2 * pair + 2, :], in_=pair_of_b(0, j0, pair, "b"))
-
-        def a_times_plain(j0):
-            if (0, j0) not in opened:
-                pass_a(0, j0, 0)
-            pass_a(0, j0, 1)
-            rows = plain[j0 - j0 % CHUNK][:, :, j0 % CHUNK : j0 % CHUNK + NARROW]
-            nc.vector.tensor_tensor(rows, rows, opened[0, j0], MULT)
-
-        def plain_times_time(j0, slices):
-            for t0 in range(0, PACK, slices):
-                rows = plain[j0][:, t0 : t0 + slices, :]
-                nc.gpsimd.tensor_tensor(rows, rows, factors(0, j0, CHUNK)[:, t0 : t0 + slices, :], MULT)
-
-        def round_h(j0, copy):
-            i, c0, w0 = h_at[0, j0]
-            copy(out=h_half[i][:, PACK * c0 : PACK * (c0 + CHUNK)].rearrange("p (n e t) -> p n t e", e=4, t=PACK),
-                 in_=plain[j0].rearrange("p t (n e) -> p n t e", e=4))
-
-        def finish_wide(j0):
-            view, n0 = parked[0, j0]
-            i, c0, w0 = h_at[0, j0]
+        def h_by_time(g, j0, width):
             nc.vector.tensor_tensor(
-                h_half[i][:, PACK * c0 : PACK * (c0 + CHUNK)].rearrange("p (n e t) -> p n t e", e=2, t=PACK),
-                view, in_pairs(factors(0, j0, CHUNK)), MULT)
+                h_of(g, j0, width).rearrange("p (n e t) -> p n t e", e=2, t=PACK),
+                part(g, j0, width), in_pairs(factors(g, j0, width)), MULT)
 
-        def quantize_h(g, j0, width):
-            i, c0, w0 = h_at[g, j0]
-            nc.vector.quantize_mx(out=h_w[:, w0 : w0 + width].bitcast(FP8X4), scales=h_s[:, w0 : w0 + width],
-                                  in_=h_half[i][:, PACK * c0 : PACK * (c0 + width)])
-
-        def spent_h(g, j0):
-            i, c0, w0 = h_at[g, j0]
-            return h_half[i][:, PACK * c0 : PACK * (c0 + CHUNK)].bitcast(F32)
-
-        def make_risk(j0, width, ring="z"):
-            risk[j0] = take("risk")[:, 0 : PACK * width].rearrange("p (t n) -> p t n", t=PACK)
-            for t0 in range(0, PACK, 2):
-                z = take(ring)[:, 0 : 2 * width].rearrange("p (u n) -> p u n", u=2)
-                for g in range(2):
-                    w0 = h_at[g, j0][2]
-                    for u in range(2):
-                        t = t0 + u
-                        nc.tensor.matmul_mx(
-                            out=z[:, u, :],
-                            lhsT=wo_w[:, g, P * t : P * (t + 1)].bitcast(FP8X4),
-                            lhsT_scale=wo_s[WO_ROW + 4 * g : P, P * t : P * (t + 1)],
-                            rhs=h_w[:, w0 : w0 + width].bitcast(FP8X4), rhs_scale=h_s[:, w0 : w0 + width],
-                            start=(g == 0 and u == 0), stop=(g == 1 and u == 1),
-                        )
-                for u in range(2):
-                    t = t0 + u
-                    nc.scalar.activation(risk[j0][:, t, :], z[:, u, :], SIGMOID, bias=bias[:, t : t + 1])
-
-        def make_y_by_pairs(j0):
-            risk[j0] = take("risk")[:].rearrange("p (t n) -> p t n", t=PACK)
-            y[j0] = take("y")[:].rearrange("p (t n) -> p t n", t=PACK)
-            for t0 in range(0, PACK, 2):
-                z = take("z")[:].rearrange("p (u n) -> p u n", u=2)
-                for g in range(2):
-                    w0 = h_at[g, j0][2]
-                    for u in range(2):
-                        t = t0 + u
-                        nc.tensor.matmul_mx(
-                            out=z[:, u, :],
-                            lhsT=wo_w[:, g, P * t : P * (t + 1)].bitcast(FP8X4),
-                            lhsT_scale=wo_s[WO_ROW + 4 * g : P, P * t : P * (t + 1)],
-                            rhs=h_w[:, w0 : w0 + CHUNK].bitcast(FP8X4), rhs_scale=h_s[:, w0 : w0 + CHUNK],
-                            start=(g == 0 and u == 0), stop=(g == 1 and u == 1),
-                        )
-                for u in range(2):
-                    nc.scalar.activation(risk[j0][:, t0 + u, :], z[:, u, :], SIGMOID, bias=bias[:, t0 + u : t0 + u + 1])
-                for u in range(2):
-                    weigh_on_scalar(y[j0][:, t0 + u, :], risk[j0][:, t0 + u, :], t0 + u)
-                rows = out_0[:, j0 : j0 + CHUNK].rearrange("(p t) j -> p t j", t=PACK)
-                nc.sync.dma_start(out=rows[:, t0 : t0 + 2, :], in_=y[j0][:, t0 : t0 + 2, :])
-
-        def pass_z(j0, width, g):
-            if g == 0:
-                z_open[j0] = [take("z")[:, 0 : 2 * width].rearrange("p (u n) -> p u n", u=2) for half in range(2)]
+        def quantize_h(j0, width, g=0):
             w0 = h_at[g, j0][2]
-            for t in range(PACK):
+            nc.vector.quantize_mx(out=h_w[:, w0 : w0 + width].bitcast(FP8X4), scales=h_s[:, w0 : w0 + width],
+                                  in_=h_of(g, j0, width))
+
+        def pass_z(j0, width, t0, b, g):
+            z = bank[b][:, 0 : 2 * width].rearrange("p (u n) -> p u n", u=2)
+            w0 = h_at[g, j0][2]
+            for u in range(2):
+                t = t0 + u
                 nc.tensor.matmul_mx(
-                    out=z_open[j0][t // 2][:, t % 2, :],
+                    out=z[:, u, :],
                     lhsT=wo_w[:, g, P * t : P * (t + 1)].bitcast(FP8X4),
                     lhsT_scale=wo_s[WO_ROW + 4 * g : P, P * t : P * (t + 1)],
                     rhs=h_w[:, w0 : w0 + width].bitcast(FP8X4), rhs_scale=h_s[:, w0 : w0 + width],
-                    start=(g == 0 and t % 2 == 0), stop=(g == 1 and t % 2 == 1),
+                    start=(g == 0 and u == 0), stop=(g == 1 and u == 1),
                 )
+            return z
 
-        def close_risk(j0, width):
-            pass_z(j0, width, 1)
+        def open_z(j0, width, banks):
+            for pair in range(2):
+                pass_z(j0, width, 2 * pair, banks[pair], 0)
+            opened.add(j0)
+
+        def product_z(j0, width, t0, b):
+            if j0 not in opened:
+                pass_z(j0, width, t0, b, 0)
+            z = pass_z(j0, width, t0, b, 1)
+            for u in range(2):
+                t = t0 + u
+                nc.scalar.activation(risk[j0][:, t, :], z[:, u, :], SIGMOID, bias=bias[:, t : t + 1])
+
+        def make_risk(j0, width, banks):
             risk[j0] = take("risk")[:, 0 : PACK * width].rearrange("p (t n) -> p t n", t=PACK)
-            for t in range(PACK):
-                nc.scalar.activation(risk[j0][:, t, :], z_open[j0][t // 2][:, t % 2, :], SIGMOID, bias=bias[:, t : t + 1])
+            for pair in range(2):
+                product_z(j0, width, 2 * pair, banks[pair])
 
         def weigh_on_scalar(dst, src, t):
             nc.scalar.activation(dst, src, COPY, scale=weight[:, t : t + 1])
@@ -381,12 +299,25 @@ def tile_list_visit_risk_burden_kernel(
         def weigh_on_vector(dst, src, t):
             nc.vector.tensor_scalar(dst, src, weight[:, t : t + 1], None, MULT)
 
-        def make_y(j0, weigh, queue=nc.sync):
+        def rows_of_out(j0, width):
+            return out_0[:, j0 : j0 + width].rearrange("(p t) j -> p t j", t=PACK)
+
+        def make_y_by_pairs(j0, banks):
+            risk[j0] = take("risk")[:].rearrange("p (t n) -> p t n", t=PACK)
+            y[j0] = take("y")[:].rearrange("p (t n) -> p t n", t=PACK)
+            for pair in range(2):
+                t0 = 2 * pair
+                product_z(j0, CHUNK, t0, banks[pair])
+                for t in range(t0, t0 + 2):
+                    weigh_on_scalar(y[j0][:, t, :], risk[j0][:, t, :], t)
+                nc.sync.dma_start(out=rows_of_out(j0, CHUNK)[:, t0 : t0 + 2, :], in_=y[j0][:, t0 : t0 + 2, :])
+
+        def make_y(j0, weigh):
             width = risk[j0].shape[2]
             y[j0] = take("y")[:, 0 : PACK * width].rearrange("p (t n) -> p t n", t=PACK)
             for t in range(PACK):
                 weigh(y[j0][:, t, :], risk[j0][:, t, :], t)
-            queue.dma_start(out=out_0[:, j0 : j0 + width].rearrange("(p t) j -> p t j", t=PACK), in_=y[j0])
+            nc.sync.dma_start(out=rows_of_out(j0, width), in_=y[j0])
 
         def round_y(j0, copy):
             width = y[j0].shape[2]
@@ -402,9 +333,6 @@ def tile_list_visit_risk_burden_kernel(
                 MULT,
             )
 
-        def on_gpsimd(out, in_):
-            nc.gpsimd.tensor_scalar(out, in_, 1.0, 0.0, MULT, mybir.AluOpType.add)
-
         def quantize_y(j0, width):
             cols = slice(j0, j0 + width)
             nc.vector.quantize_mx(out=y_w[:, cols].bitcast(FP8X4), scales=y_s[:, cols],
@@ -414,9 +342,9 @@ def tile_list_visit_risk_burden_kernel(
             cols = slice(j0, j0 + width)
             queue.dma_start(out=words(out_1[0])[:, cols], in_=y_w[:, cols].bitcast(I32))
 
-        def store_scales(queues):
+        def store_scales(queue):
             for r in range(4):
-                queues[r].dma_start(out=out_2[0, r:16:4, :].bitcast(I32), in_=y_s[r:P:32, :].bitcast(I32))
+                queue.dma_start(out=out_2[0, r:16:4, :].bitcast(I32), in_=y_s[r:P:32, :].bitcast(I32))
 
         on_scalar, on_vector = nc.scalar.copy, nc.vector.tensor_copy
         second, third, fourth = CHUNK, 2 * CHUNK, 3 * CHUNK
@@ -425,92 +353,107 @@ def tile_list_visit_risk_burden_kernel(
         load_table(tab2_w, tab2_words[0])
         nc.sync.dma_start(list2[:], offs2)
         load_scales_by_row(nc.sync, tab2_s, tab2_scales)
-        nc.sync.dma_start(list1[:], offs)
-        load_table(tab_w[0], tab_words[0])
         load_wd()
+        load_table(tab_w[0], tab_words[0])
         load_scales_by_row(nc.sync, wd_s_raw, wd_scales)
+        nc.sync.dma_start(list1[:], offs)
         load_wp(0, 0)
         load_wp(0, 1)
         load_table(tab_w[1], tab_words[1])
-        load_time(0, 0, HALF)
+        load_time(0, 0, CHUNK)
+        load_scales(nc.sync, wo_s_raw, wo_scales, WO_ROW, 0)
+        load_time(0, second, CHUNK)
+        load_scales(nc.sync, wo_s_raw, wo_scales, WO_ROW, 1)
         load_wp(1, 0)
+        load_scales(nc.sync, wo_s_raw, wo_scales, WO_ROW, 2)
         load_wp(1, 1)
+        load_scales(nc.sync, wo_s_raw, wo_scales, WO_ROW, 3)
         load_time(1, 0, CHUNK)
         load_wo()
-        load_time(1, CHUNK, CHUNK)
-        load_time(0, HALF, HALF)
-        load_time(1, HALF, HALF)
-        load_scales(nc.gpsimd, tab_s, tab_scales, TAB_ROW)
-        load_scales(nc.gpsimd, wo_s_raw, wo_scales, WO_ROW)
-        load_bias(nc.gpsimd)
+        load_by_slices(bias, bo)
+        load_time(1, second, CHUNK)
+        load_by_slices(weight, cost)
+        load_time(1, third, CHUNK)
+        load_time(0, third, CHUNK)
+        load_time(1, fourth, CHUNK)
+        load_time(0, fourth, CHUNK)
+        for q in range(4):
+            load_scales(nc.gpsimd, tab_s, tab_scales, TAB_ROW, q)
+
         gather(v2_w, tab2_w, list2, 0, S)
         gather(v2_s, tab2_s, list2, 0, S)
-        deal_wd()
+        deal(nc.vector, wd_w[:].bitcast(U16), wd_raw[:].bitcast(U16), 8)
+        deal(nc.vector, wd_s[:], wd_s_raw[:], 16)
         gather(v_w[0], tab_w[0], list1, 0, S)
         gather(v_s, tab_s, list1, 0, S)
-        deal(wo_s[:], wo_s_raw[:], 16)
         round_wp(0, 0, on_scalar)
         quantize_wp(0, 0)
         round_wp(0, 1, on_scalar)
         quantize_wp(0, 1)
-        park_plain(0, wp_raw[0][1][:, 0 : PACK * CHUNK])
-        park_plain(second, wp_raw[0][1][:, PACK * CHUNK :])
-        park_b(0, third, wp_raw[0][0][:, 0 : PACK * CHUNK], "b")
-        park_b(0, fourth, wp_raw[0][0][:, PACK * CHUNK :], "b")
-        for c in range(3):
-            pass_a(0, c * NARROW, 0)
-        gather(v_w[1], tab_w[1], list1, 0, HALF)
+        park_b(0, third, rooms[2][:], (0, 1))
+        park_b(0, fourth, rooms[3][:], (2, 3))
+        park_b(0, 0, rooms[0][:], (4, 5))
+        park_b(0, second, rooms[1][:], (6, 7))
+        for b in range(4):
+            pass_a(0, third + b // 2 * CHUNK, 0, b, 2 * (b % 2), 2)
+        park_b(1, third, wp_raw[0][1][:, 0 : PACK * CHUNK], (4, 5))
+        park_b(1, fourth, wp_raw[0][1][:, PACK * CHUNK :], (6, 7))
         gather(v_w[1], tab_w[1], list1, HALF, HALF)
-        for j0 in range(0, HALF, NARROW):
-            a_times_plain(j0)
-        for j0 in range(HALF, S, NARROW):
-            a_times_parked(0, j0)
-        plain_times_time(0, 2)
-        plain_times_time(second, 2)
+        for b in range(4):
+            a_times_parked(0, third + b // 2 * CHUNK, b % 2, b)
+        for c in range(4):
+            pass_a(0, c * NARROW, 0, 4 + c, 0, PACK)
+        gather(v_w[1], tab_w[1], list1, 0, HALF)
+        parked_times_time(0, 0, 64)
+        parked_times_time(0, second, 64)
+        for c in range(4):
+            h_by_a(0, c * NARROW, 4 + c)
         round_wp(1, 0, on_scalar)
         round_wp(1, 1, on_scalar)
-        round_h(0, on_scalar)
-        round_h(second, on_scalar)
         quantize_wp(1, 0)
-        times_b(1, 0, 0)
-        times_b(1, 0, 1)
-        for c in range(3):
-            pass_a(1, c * NARROW, 0)
+        b_times_time(1, 0, 0, rooms[0][:], 0)
+        b_times_time(1, 0, 1, rooms[0][:], 1)
+        pass_a(1, 0, 0, 2, 0, PACK)
+        pass_a(1, NARROW, 0, 3, 0, PACK)
+        pass_a(1, second, 0, 6, 0, PACK)
+        pass_a(1, second + NARROW, 0, 7, 0, PACK)
         quantize_wp(1, 1)
-        deal_wo()
-        times_a(1, 0)
-        times_a(1, NARROW)
-        times_b(1, second, 0)
-        quantize_h(0, 0, HALF)
-        make_risk(0, CHUNK)
+        deal_wo(nc.vector)
+        deal(nc.vector, wo_s[:], wo_s_raw[:], 16)
+        h_by_a(1, 0, 2)
+        h_by_a(1, NARROW, 3)
+        b_times_time(1, second, 0, rooms[1][:], 4)
+        quantize_h(0, HALF)
+        make_risk(0, CHUNK, (0, 1))
         make_y(0, weigh_on_scalar)
         round_y(0, on_scalar)
-        times_b(1, second, 1)
-        times_a(1, second)
-        times_a(1, second + NARROW)
-        finish_wide(third)
-        quantize_h(0, second, HALF)
-        make_risk(second, CHUNK)
+        b_times_time(1, second, 1, rooms[1][:], 5)
+        h_by_a(1, second, 6)
+        h_by_a(1, second + NARROW, 7)
+        parked_times_time(1, third, 64)
+        parked_times_time(1, fourth, 64)
+        h_by_time(0, third, CHUNK)
+        quantize_h(second, HALF)
+        make_risk(second, CHUNK, (4, 5))
         make_y(second, weigh_on_scalar)
-        times_b(1, third, 0)
-        times_b(1, third, 1)
-        times_a(1, third)
-        times_a(1, third + NARROW)
-        times_b(1, fourth, 0)
+        pass_a(1, third, 0, 2, 0, PACK)
+        h_by_a(1, third, 2)
+        pass_a(1, third + NARROW, 0, 3, 0, PACK)
+        h_by_a(1, third + NARROW, 3)
+        h_by_time(0, first, NARROW)
+        quantize_h(third, HALF)
+        make_y_by_pairs(third, (0, 1))
+        pass_a(1, first, 0, 6, 0, PACK)
+        h_by_a(1, first, 6)
+        h_by_time(0, last, NARROW)
+        quantize_h(first, CHUNK)
+        make_risk(first, NARROW, (2, 3))
+        pass_a(1, last, 0, 7, 0, PACK)
+        h_by_a(1, last, 7)
         quantize_y(0, CHUNK)
         store_words(0, CHUNK, nc.sync)
-        quantize_h(0, third, HALF)
-        make_y_by_pairs(third)
-        times_b(1, fourth, 1)
-        rings["z"] = rings["z"] + rings["b"][0:2]
-        finish_h(0, first, nc.vector, NARROW)
-        times_a(1, first)
-        finish_h(0, last, nc.vector, NARROW)
-        quantize_h(0, first, CHUNK)
-        make_risk(first, NARROW)
-        times_a(1, last)
-        quantize_h(0, last, CHUNK)
-        make_risk(last, NARROW)
+        quantize_h(last, CHUNK)
+        make_risk(last, NARROW, (4, 5))
         round_y(second, on_vector)
         quantize_y(second, CHUNK)
         store_words(second, CHUNK, nc.sync)
@@ -524,4 +467,4 @@ def tile_list_visit_risk_burden_kernel(
         quantize_y(first, NARROW)
         quantize_y(last, NARROW)
         store_words(first, CHUNK, nc.sync)
-        store_scales([nc.scalar] * 4)
+        store_scales(nc.scalar)

@@ -205,21 +205,27 @@ def tile_list_visit_risk_burden_kernel(
 
         def park_plain(g, j0, room, banks):
             plain[g, j0] = room.rearrange("p (t n) -> p t n", t=PACK)
-            partial[g, j0] = in_pairs(plain[g, j0])
             for pair in range(2):
                 product_b(g, j0, pair, banks[pair])
                 nc.scalar.copy(out=plain[g, j0][:, 2 * pair : 2 * pair + 2, :], in_=slices(banks[pair], 2))
 
+        def plain_part(g, j0, width):
+            c0 = j0 % CHUNK
+            return plain[g, j0 - c0][:, :, c0 : c0 + width]
+
         def plain_times_time(g, j0, step):
-            for t0 in range(0, PACK, step):
-                rows = plain[g, j0][:, t0 : t0 + step, :]
-                nc.gpsimd.tensor_tensor(rows, rows, factors(g, j0, CHUNK)[:, t0 : t0 + step, :], MULT)
+            for c0 in range(j0, j0 + CHUNK, step):
+                nc.gpsimd.tensor_tensor(plain_part(g, c0, step), plain_part(g, c0, step), factors(g, c0, step), MULT)
+
+        def in_fours(rows):
+            return rows.rearrange("p t (n e) -> p n t e", e=4)
+
+        def woven(flat):
+            return flat.rearrange("p (n e t) -> p n t e", e=4, t=PACK)
 
         def h_by_a_plain(g, j0, b):
             pass_a(g, j0, 1, b, 0, PACK)
-            nc.vector.tensor_tensor(
-                h_of(g, j0, NARROW).rearrange("p (n e t) -> p n t e", e=2, t=PACK),
-                part(g, j0, NARROW), in_pairs(slices(b, PACK)), MULT)
+            nc.vector.tensor_tensor(woven(h_of(g, j0, NARROW)), in_fours(plain_part(g, j0, NARROW)), in_fours(slices(b, PACK)), MULT)
 
         def pass_a(g, j0, a, b, t0, count):
             width = HALF // count
@@ -239,8 +245,8 @@ def tile_list_visit_risk_burden_kernel(
 
         def a_times_parked(g, j0, pair, b):
             pass_a(g, j0, 1, b, 2 * pair, 2)
-            rows = partial[g, j0][:, :, 2 * pair : 2 * pair + 2, :]
-            nc.vector.tensor_tensor(rows, rows, in_pairs(slices(b, 2)), MULT)
+            rows = plain[g, j0][:, 2 * pair : 2 * pair + 2, :]
+            nc.vector.tensor_tensor(rows, rows, slices(b, 2), MULT)
 
         def h_by_a(g, j0, b):
             pass_a(g, j0, 1, b, 0, PACK)
@@ -252,9 +258,7 @@ def tile_list_visit_risk_burden_kernel(
             )
 
         def h_by_time(g, j0, width):
-            nc.vector.tensor_tensor(
-                h_of(g, j0, width).rearrange("p (n e t) -> p n t e", e=2, t=PACK),
-                part(g, j0, width), in_pairs(factors(g, j0, width)), MULT)
+            nc.vector.tensor_tensor(woven(h_of(g, j0, width)), in_fours(plain_part(g, j0, width)), in_fours(factors(g, j0, width)), MULT)
 
         def quantize_h(j0, width, g=0):
             w0 = h_at[g, j0][2]
@@ -327,9 +331,9 @@ def tile_list_visit_risk_burden_kernel(
         def weigh_and_round(j0):
             width = risk[j0].shape[2]
             nc.vector.tensor_tensor(
-                y_bf[:, PACK * j0 : PACK * (j0 + width)].rearrange("p (n e t) -> p n t e", e=2, t=PACK),
-                risk[j0].rearrange("p t (n e) -> p n t e", e=2),
-                weight[:].unsqueeze(1).unsqueeze(3).to_broadcast([P, width // 2, PACK, 2]),
+                woven(y_bf[:, PACK * j0 : PACK * (j0 + width)]),
+                in_fours(risk[j0]),
+                weight[:].unsqueeze(1).unsqueeze(3).to_broadcast([P, width // 4, PACK, 4]),
                 MULT,
             )
 
@@ -390,24 +394,24 @@ def tile_list_visit_risk_burden_kernel(
         quantize_wp(0, 0)
         round_wp(0, 1, on_scalar)
         quantize_wp(0, 1)
-        park_b(0, third, rooms[2][:], (0, 1))
-        park_b(0, fourth, rooms[3][:], (2, 3))
-        park_b(0, 0, rooms[0][:], (4, 5))
-        park_b(0, second, rooms[1][:], (6, 7))
+        park_plain(0, third, rooms[2][:], (0, 1))
+        park_plain(0, fourth, rooms[3][:], (2, 3))
+        park_plain(0, 0, rooms[0][:], (4, 5))
+        park_plain(0, second, rooms[1][:], (6, 7))
         for b in range(4):
             pass_a(0, third + b // 2 * CHUNK, 0, b, 2 * (b % 2), 2)
-        park_b(1, third, wp_raw[0][1][:, 0 : PACK * CHUNK], (4, 5))
-        park_b(1, fourth, wp_raw[0][1][:, PACK * CHUNK :], (6, 7))
+        park_plain(1, third, wp_raw[0][1][:, 0 : PACK * CHUNK], (4, 5))
+        park_plain(1, fourth, wp_raw[0][1][:, PACK * CHUNK :], (6, 7))
         gather(v_w[1], tab_w[1], list1, HALF, HALF)
         for b in range(4):
             a_times_parked(0, third + b // 2 * CHUNK, b % 2, b)
         for c in range(4):
             pass_a(0, c * NARROW, 0, 4 + c, 0, PACK)
         gather(v_w[1], tab_w[1], list1, 0, HALF)
-        parked_times_time(0, 0, 64)
-        parked_times_time(0, second, 64)
+        plain_times_time(0, 0, NARROW)
+        plain_times_time(0, second, NARROW)
         for c in range(4):
-            h_by_a(0, c * NARROW, 4 + c)
+            h_by_a_plain(0, c * NARROW, 4 + c)
         round_wp(1, 0, on_scalar)
         round_wp(1, 1, on_scalar)
         quantize_wp(1, 0)
@@ -430,26 +434,26 @@ def tile_list_visit_risk_burden_kernel(
         b_times_time(1, second, 1, rooms[1][:], 5)
         h_by_a(1, second, 6)
         h_by_a(1, second + NARROW, 7)
-        parked_times_time(1, third, 64)
-        parked_times_time(1, fourth, 64)
+        plain_times_time(1, third, 64)
+        plain_times_time(1, fourth, 64)
         h_by_time(0, third, CHUNK)
         quantize_h(second, HALF)
         make_risk(second, CHUNK, (4, 5))
         make_y(second, weigh_on_scalar)
         pass_a(1, third, 0, 2, 0, PACK)
-        h_by_a(1, third, 2)
+        h_by_a_plain(1, third, 2)
         pass_a(1, third + NARROW, 0, 3, 0, PACK)
-        h_by_a(1, third + NARROW, 3)
+        h_by_a_plain(1, third + NARROW, 3)
         h_by_time(0, first, NARROW)
         quantize_h(third, HALF)
         make_y_by_pairs(third, (0, 1))
         pass_a(1, first, 0, 6, 0, PACK)
-        h_by_a(1, first, 6)
+        h_by_a_plain(1, first, 6)
         h_by_time(0, last, NARROW)
         quantize_h(first, CHUNK)
         make_risk(first, NARROW, (2, 3))
         pass_a(1, last, 0, 7, 0, PACK)
-        h_by_a(1, last, 7)
+        h_by_a_plain(1, last, 7)
         quantize_y(0, CHUNK)
         store_words(0, CHUNK, nc.sync)
         quantize_h(last, CHUNK)

@@ -378,8 +378,8 @@ def tile_list_visit_risk_burden_kernel(
         load_time(1, second, CHUNK)
         load_by_slices(weight, cost)
         load_time(1, third, CHUNK)
-        load_time(0, third, CHUNK)
         load_time(1, fourth, CHUNK)
+        load_time(0, third, CHUNK)
         load_time(0, fourth, CHUNK)
         for q in range(4):
             load_scales(nc.gpsimd, tab_s, tab_scales, TAB_ROW, q)
@@ -436,14 +436,14 @@ def tile_list_visit_risk_burden_kernel(
         h_by_a(1, second + NARROW, 7)
         plain_times_time(1, third, 64)
         plain_times_time(1, fourth, 64)
-        h_by_time(0, third, CHUNK)
+        pass_a(1, third, 0, 2, 0, PACK)
+        h_by_a_plain(1, third, 2)
         quantize_h(second, HALF)
         make_risk(second, CHUNK, (4, 5))
         make_y(second, weigh_on_scalar)
-        pass_a(1, third, 0, 2, 0, PACK)
-        h_by_a_plain(1, third, 2)
         pass_a(1, third + NARROW, 0, 3, 0, PACK)
         h_by_a_plain(1, third + NARROW, 3)
+        h_by_time(0, third, CHUNK)
         h_by_time(0, first, NARROW)
         quantize_h(third, HALF)
         make_y_by_pairs(third, (0, 1))

@@ -14,7 +14,6 @@ U8 = mybir.dt.uint8
 FP8X4 = mybir.dt.float8_e4m3fn_x4
 FP4X4 = mybir.dt.float4_e2m1fn_x4
 MULT = mybir.AluOpType.mult
-ADD = mybir.AluOpType.add
 SIGMOID = mybir.ActivationFunctionType.Sigmoid
 COPY = mybir.ActivationFunctionType.Copy
 
@@ -56,11 +55,13 @@ def tile_list_visit_risk_burden_kernel(
         wd_s = held("wd_s", [P, H], U8)
         wo_s_raw = held("wo_s_raw", [P, N], U8)
         wo_s = held("wo_s", [P, N], U8)
-        wo_raw = held("wo_raw", [P, 2, N], I32)
-        wo_w = held("wo_w", [P, 2, N], I32)
+        wo_raw = held("wo_raw", [P, 2 * N], U32)
+        wo_w = held("wo_w", [P, 2 * N], U32)
         wp_raw = [[held("wp_raw%d%d" % (g, a), [P, PACK * PASS], F32) for a in range(2)] for g in range(2)]
         wp_w = [[held("wp_w%d%d" % (g, a), [P, PASS], U32) for a in range(2)] for g in range(2)]
         wp_s = [[held("wp_s%d%d" % (g, a), [P, PASS], U8) for a in range(2)] for g in range(2)]
+        rounded = [held("rounded%d" % a, [P, PACK * PASS], BF16) for a in range(2)]
+        h_bf = held("h_bf", [P, 2 * PACK * S], BF16)
         h_w = held("h_w", [P, 2 * S], U32)
         h_s = held("h_s", [P, 2 * S], U8)
         y_bf = held("y_bf", [P, PACK * S], BF16)
@@ -68,38 +69,15 @@ def tile_list_visit_risk_burden_kernel(
         y_s = held("y_s", [P, S], U8)
         bias = held("bias", [P, PACK], F32)
         weight = held("weight", [P, PACK], F32)
-        h_half = [wp_raw[0][0][:, i * PACK * CHUNK : (i + 1) * PACK * CHUNK].bitcast(BF16) for i in range(2)]
-        h_half.append(held("h_half2", [P, PACK * HALF], BF16))
-        rooms = [held("room%d" % i, [P, PACK * CHUNK], F32) for i in range(4)]
-
         bank = [psum.tile([P, HALF], F32, name="bank%d" % i) for i in range(8)]
-        rings = {}
-        rings["rounded"] = [held("rounded%d" % i, [P, PACK * PASS], BF16) for i in range(2)]
-        rings["risk"] = [held("risk%d" % i, [P, PACK * CHUNK], F32) for i in range(3)]
-        rings["y"] = [held("y%d" % i, [P, PACK * CHUNK], F32) for i in range(4)]
 
-        def take(name):
-            ring = rings[name]
-            ring.append(ring.pop(0))
-            return ring[-1]
-
+        second, third, fourth = CHUNK, 2 * CHUNK, 3 * CHUNK
+        last = S - NARROW
+        runs = {0: CHUNK, second: CHUNK, third: CHUNK, fourth: NARROW, last: NARROW}
         time_f = {}
         partial = {}
-        plain = {}
-        rounded = {}
         risk = {}
         y = {}
-        opened = set()
-
-        h_at = {}
-        for g in range(2):
-            for c in range(2):
-                for k in range(3):
-                    h_at[g, k * CHUNK + c * NARROW] = (k, g * CHUNK + c * NARROW, k * HALF + g * CHUNK + c * NARROW)
-                h_at[g, 3 * CHUNK + c * NARROW] = (0, c * CHUNK + g * NARROW, 3 * HALF + c * CHUNK + g * NARROW)
-
-        for plane in (tab_s, tab2_s, wd_s_raw, wo_s_raw):
-            nc.vector.memset(plane[:].bitcast(I32), 0)
 
         def words(dram):
             return dram.rearrange("p n t -> p (n t)").bitcast(I32)
@@ -117,12 +95,11 @@ def tile_list_visit_risk_burden_kernel(
             tile = held("time%d_%d" % (g, j0), [P, PACK, width], F32)
             rows = tv[g * PASS : (g + 1) * PASS, j0 : j0 + width]
             nc.sync.dma_start(out=tile[:], in_=rows.rearrange("(p t) j -> p t j", t=PACK))
-            for c0 in range(0, width, NARROW):
+            for c0 in range(0, width, 64):
                 time_f[g, j0 + c0] = (tile, c0)
 
         def factors(g, j0, width):
-            tile, c0 = time_f[g, j0 - j0 % NARROW]
-            c0 = c0 + j0 % NARROW
+            tile, c0 = time_f[g, j0]
             return tile[:, :, c0 : c0 + width]
 
         def load_wp(g, a):
@@ -136,46 +113,42 @@ def tile_list_visit_risk_burden_kernel(
             nc.sync.dma_start(out=wd_raw[:].bitcast(I32), in_=wd_words[0].bitcast(I32))
 
         def load_wo():
-            nc.sync.dma_start(out=wo_raw[:], in_=wo_words.rearrange("a p n t -> p a (n t)").bitcast(I32))
+            nc.sync.dma_start(out=wo_raw[:].bitcast(I32).rearrange("p (a n) -> p a n", a=2),
+                              in_=wo_words.rearrange("a p n t -> p a (n t)").bitcast(I32))
 
-        def load_by_slices(tile, vector):
-            nc.sync.dma_start(out=tile[:], in_=vector.rearrange("(p t) -> p t", t=PACK))
+        def load_by_slices(queue, tile, vector):
+            queue.dma_start(out=tile[:], in_=vector.rearrange("(p t) -> p t", t=PACK))
 
-        def deal(engine, dst, src, run):
-            engine.tensor_copy(
+        def deal(copy, dst, src, run):
+            copy(
                 out=dst.rearrange("p (g t b m) -> p g b t m", t=PACK, b=P // run, m=run),
                 in_=src.rearrange("p (g b m t) -> p g b t m", t=PACK, b=P // run, m=run),
             )
-
-        def deal_wo(engine):
-            deal(engine, wo_w[:].rearrange("p a n -> p (a n)"), wo_raw[:].rearrange("p a n -> p (a n)"), 4)
 
         def gather(dst, window, entries, first, count):
             nc.vector.tensor_copy(dst[:, first : first + count], window[:].indirect(entries[:, first // 16 : (first + count) // 16]))
 
         def round_wp(g, a, copy, m0=0, m1=P):
-            if (g, a) not in rounded:
-                rounded[g, a] = take("rounded")
             copy(
-                out=rounded[g, a][:].rearrange("p (t m i) -> p m i t", t=PACK, i=PACK)[:, m0:m1, :, :],
+                out=rounded[a][:].rearrange("p (t m i) -> p m i t", t=PACK, i=PACK)[:, m0:m1, :, :],
                 in_=wp_raw[g][a][:].rearrange("p (i m t) -> p m i t", i=PACK, t=PACK)[:, m0:m1, :, :],
             )
 
         def quantize_wp(g, a):
-            nc.vector.quantize_mx(out=wp_w[g][a][:].bitcast(FP8X4), scales=wp_s[g][a][:], in_=rounded[g, a][:])
-
-        def paired(flat):
-            return flat.rearrange("p (n t e) -> p n t e", t=PACK, e=2)
-
-        def in_pairs(rows):
-            return rows.rearrange("p t (n e) -> p n t e", e=2)
+            nc.vector.quantize_mx(out=wp_w[g][a][:].bitcast(FP8X4), scales=wp_s[g][a][:], in_=rounded[a][:])
 
         def slices(b, count):
             return bank[b][:].rearrange("p (t n) -> p t n", t=count)
 
+        def in_fours(rows):
+            return rows.rearrange("p t (n e) -> p n t e", e=4)
+
+        def woven(flat):
+            return flat.rearrange("p (n e t) -> p n t e", e=4, t=PACK)
+
         def part(g, j0, width):
             c0 = j0 % CHUNK
-            return partial[g, j0 - c0][:, c0 // 2 : (c0 + width) // 2, :, :]
+            return partial[g, j0 - c0][:, :, c0 : c0 + width]
 
         def product_b(g, j0, pair, b):
             for u in range(2):
@@ -186,46 +159,22 @@ def tile_list_visit_risk_burden_kernel(
                     rhs=v2_w[:, j0 : j0 + CHUNK].bitcast(FP8X4), rhs_scale=v2_s[:, j0 : j0 + CHUNK],
                     start=True, stop=True,
                 )
-            return in_pairs(slices(b, 2))
 
-        def park_b(g, j0, room, banks):
-            partial[g, j0] = paired(room)
-            for pair in range(2):
-                nc.scalar.copy(out=partial[g, j0][:, :, 2 * pair : 2 * pair + 2, :], in_=product_b(g, j0, pair, banks[pair]))
+        def b_times_time(g, j0, pair, b):
+            partial[g, j0] = factors(g, j0, CHUNK)
+            rows = partial[g, j0][:, 2 * pair : 2 * pair + 2, :]
+            product_b(g, j0, pair, b)
+            nc.vector.tensor_tensor(rows, rows, slices(b, 2), MULT)
 
-        def b_times_time(g, j0, pair, room, b):
-            partial[g, j0] = paired(room)
-            rows = slice(2 * pair, 2 * pair + 2)
-            nc.vector.tensor_tensor(partial[g, j0][:, :, rows, :], in_pairs(factors(g, j0, CHUNK)[:, rows, :]),
-                                    product_b(g, j0, pair, b), MULT)
-
-        def parked_times_time(g, j0, step):
-            for c0 in range(j0, j0 + CHUNK, step):
-                nc.gpsimd.tensor_tensor(part(g, c0, step), part(g, c0, step), in_pairs(factors(g, c0, step)), MULT)
-
-        def park_plain(g, j0, room, banks):
-            plain[g, j0] = room.rearrange("p (t n) -> p t n", t=PACK)
+        def park_b(g, j0, banks):
+            partial[g, j0] = held("parked%d_%d" % (g, j0), [P, PACK, CHUNK], F32)[:]
             for pair in range(2):
                 product_b(g, j0, pair, banks[pair])
-                nc.scalar.copy(out=plain[g, j0][:, 2 * pair : 2 * pair + 2, :], in_=slices(banks[pair], 2))
+                nc.scalar.copy(out=partial[g, j0][:, 2 * pair : 2 * pair + 2, :], in_=slices(banks[pair], 2))
 
-        def plain_part(g, j0, width):
-            c0 = j0 % CHUNK
-            return plain[g, j0 - c0][:, :, c0 : c0 + width]
-
-        def plain_times_time(g, j0, step):
-            for c0 in range(j0, j0 + CHUNK, step):
-                nc.gpsimd.tensor_tensor(plain_part(g, c0, step), plain_part(g, c0, step), factors(g, c0, step), MULT)
-
-        def in_fours(rows):
-            return rows.rearrange("p t (n e) -> p n t e", e=4)
-
-        def woven(flat):
-            return flat.rearrange("p (n e t) -> p n t e", e=4, t=PACK)
-
-        def h_by_a_plain(g, j0, b):
-            pass_a(g, j0, 1, b, 0, PACK)
-            nc.vector.tensor_tensor(woven(h_of(g, j0, NARROW)), in_fours(plain_part(g, j0, NARROW)), in_fours(slices(b, PACK)), MULT)
+        def parked_times_time(engine, g, j0, width, step):
+            for c0 in range(j0, j0 + width, step):
+                engine.tensor_tensor(part(g, c0, step), part(g, c0, step), factors(g, c0, step), MULT)
 
         def pass_a(g, j0, a, b, t0, count):
             width = HALF // count
@@ -239,63 +188,58 @@ def tile_list_visit_risk_burden_kernel(
                     start=(a == 0 and u == 0), stop=(a == 1 and u == count - 1),
                 )
 
-        def h_of(g, j0, width):
-            i, c0, w0 = h_at[g, j0]
-            return h_half[i][:, PACK * c0 : PACK * (c0 + width)]
+        def h_at(g, j0):
+            start = max(r for r in runs if r <= j0)
+            return 2 * start + g * runs[start] + j0 - start
 
-        def a_times_parked(g, j0, pair, b):
-            pass_a(g, j0, 1, b, 2 * pair, 2)
-            rows = plain[g, j0][:, 2 * pair : 2 * pair + 2, :]
-            nc.vector.tensor_tensor(rows, rows, slices(b, 2), MULT)
+        def h_of(g, j0, width):
+            w0 = h_at(g, j0)
+            return h_bf[:, PACK * w0 : PACK * (w0 + width)]
 
         def h_by_a(g, j0, b):
             pass_a(g, j0, 1, b, 0, PACK)
-            nc.vector.tensor_tensor(
-                h_of(g, j0, NARROW).rearrange("p (n e t) -> p n e t", e=2, t=PACK),
-                part(g, j0, NARROW).rearrange("p n t e -> p n e t"),
-                slices(b, PACK).rearrange("p t (n e) -> p n e t", e=2),
-                MULT,
-            )
+            nc.vector.tensor_tensor(woven(h_of(g, j0, NARROW)), in_fours(part(g, j0, NARROW)), in_fours(slices(b, PACK)), MULT)
+
+        def a_times_parked(g, j0, pair, b):
+            pass_a(g, j0, 1, b, 2 * pair, 2)
+            rows = partial[g, j0][:, 2 * pair : 2 * pair + 2, :]
+            nc.vector.tensor_tensor(rows, rows, slices(b, 2), MULT)
 
         def h_by_time(g, j0, width):
-            nc.vector.tensor_tensor(woven(h_of(g, j0, width)), in_fours(plain_part(g, j0, width)), in_fours(factors(g, j0, width)), MULT)
+            nc.vector.tensor_tensor(woven(h_of(g, j0, width)), in_fours(part(g, j0, width)), in_fours(factors(g, j0, width)), MULT)
 
-        def quantize_h(j0, width, g=0):
-            w0 = h_at[g, j0][2]
-            nc.vector.quantize_mx(out=h_w[:, w0 : w0 + width].bitcast(FP8X4), scales=h_s[:, w0 : w0 + width],
-                                  in_=h_of(g, j0, width))
+        def quantize_h(g, j0, count):
+            w0 = h_at(g, j0)
+            nc.vector.quantize_mx(out=h_w[:, w0 : w0 + count].bitcast(FP8X4), scales=h_s[:, w0 : w0 + count],
+                                  in_=h_of(g, j0, count))
 
-        def pass_z(j0, width, t0, b, g):
+        def pass_z(j0, pair, b, g, start):
+            width = runs[j0]
             z = bank[b][:, 0 : 2 * width].rearrange("p (u n) -> p u n", u=2)
-            w0 = h_at[g, j0][2]
+            w0 = h_at(g, j0)
             for u in range(2):
-                t = t0 + u
+                t = 2 * pair + u
                 nc.tensor.matmul_mx(
                     out=z[:, u, :],
-                    lhsT=wo_w[:, g, P * t : P * (t + 1)].bitcast(FP8X4),
+                    lhsT=wo_w[:, N * g + P * t : N * g + P * (t + 1)].bitcast(FP8X4),
                     lhsT_scale=wo_s[WO_ROW + 4 * g : P, P * t : P * (t + 1)],
                     rhs=h_w[:, w0 : w0 + width].bitcast(FP8X4), rhs_scale=h_s[:, w0 : w0 + width],
-                    start=(g == 0 and u == 0), stop=(g == 1 and u == 1),
+                    start=(start and u == 0), stop=(not start and u == 1),
                 )
             return z
 
-        def open_z(j0, width, banks):
-            for pair in range(2):
-                pass_z(j0, width, 2 * pair, banks[pair], 0)
-            opened.add(j0)
+        def room(raw, j0):
+            c0 = PACK * (j0 % HALF)
+            return raw[j0 // HALF][:, c0 : c0 + PACK * runs[j0]].rearrange("p (t n) -> p t n", t=PACK)
 
-        def product_z(j0, width, t0, b):
-            if j0 not in opened:
-                pass_z(j0, width, t0, b, 0)
-            z = pass_z(j0, width, t0, b, 1)
+        def make_risk(j0, pair, b, g):
+            risk[j0] = room(wp_raw[1], j0)
+            y[j0] = room(wp_raw[0], j0)
+            pass_z(j0, pair, b, 1 - g, True)
+            z = pass_z(j0, pair, b, g, False)
             for u in range(2):
-                t = t0 + u
+                t = 2 * pair + u
                 nc.scalar.activation(risk[j0][:, t, :], z[:, u, :], SIGMOID, bias=bias[:, t : t + 1])
-
-        def make_risk(j0, width, banks):
-            risk[j0] = take("risk")[:, 0 : PACK * width].rearrange("p (t n) -> p t n", t=PACK)
-            for pair in range(2):
-                product_z(j0, width, 2 * pair, banks[pair])
 
         def weigh_on_scalar(dst, src, t):
             nc.scalar.activation(dst, src, COPY, scale=weight[:, t : t + 1])
@@ -303,33 +247,19 @@ def tile_list_visit_risk_burden_kernel(
         def weigh_on_vector(dst, src, t):
             nc.vector.tensor_scalar(dst, src, weight[:, t : t + 1], None, MULT)
 
-        def rows_of_out(j0, width):
-            return out_0[:, j0 : j0 + width].rearrange("(p t) j -> p t j", t=PACK)
-
-        def make_y_by_pairs(j0, banks):
-            risk[j0] = take("risk")[:].rearrange("p (t n) -> p t n", t=PACK)
-            y[j0] = take("y")[:].rearrange("p (t n) -> p t n", t=PACK)
-            for pair in range(2):
-                t0 = 2 * pair
-                product_z(j0, CHUNK, t0, banks[pair])
-                for t in range(t0, t0 + 2):
-                    weigh_on_scalar(y[j0][:, t, :], risk[j0][:, t, :], t)
-                nc.sync.dma_start(out=rows_of_out(j0, CHUNK)[:, t0 : t0 + 2, :], in_=y[j0][:, t0 : t0 + 2, :])
-
-        def make_y(j0, weigh):
-            width = risk[j0].shape[2]
-            y[j0] = take("y")[:, 0 : PACK * width].rearrange("p (t n) -> p t n", t=PACK)
-            for t in range(PACK):
+        def make_y(j0, weigh, t0=0, t1=PACK):
+            for t in range(t0, t1):
                 weigh(y[j0][:, t, :], risk[j0][:, t, :], t)
-            nc.sync.dma_start(out=rows_of_out(j0, width), in_=y[j0])
+
+        def store_y(queue, j0, t0=0, t1=PACK):
+            rows = out_0[:, j0 : j0 + runs[j0]].rearrange("(p t) j -> p t j", t=PACK)
+            queue.dma_start(out=rows[:, t0:t1, :], in_=y[j0][:, t0:t1, :])
 
         def round_y(j0, copy):
-            width = y[j0].shape[2]
-            copy(out=y_bf[:, PACK * j0 : PACK * (j0 + width)].rearrange("p (n e t) -> p n t e", e=4, t=PACK),
-                 in_=y[j0].rearrange("p t (n e) -> p n t e", e=4))
+            copy(out=woven(y_bf[:, PACK * j0 : PACK * (j0 + runs[j0])]), in_=in_fours(y[j0]))
 
         def weigh_and_round(j0):
-            width = risk[j0].shape[2]
+            width = runs[j0]
             nc.vector.tensor_tensor(
                 woven(y_bf[:, PACK * j0 : PACK * (j0 + width)]),
                 in_fours(risk[j0]),
@@ -342,7 +272,7 @@ def tile_list_visit_risk_burden_kernel(
             nc.vector.quantize_mx(out=y_w[:, cols].bitcast(FP8X4), scales=y_s[:, cols],
                                   in_=y_bf[:, PACK * j0 : PACK * (j0 + width)])
 
-        def store_words(j0, width, queue):
+        def store_words(queue, j0, width):
             cols = slice(j0, j0 + width)
             queue.dma_start(out=words(out_1[0])[:, cols], in_=y_w[:, cols].bitcast(I32))
 
@@ -351,8 +281,9 @@ def tile_list_visit_risk_burden_kernel(
                 queue.dma_start(out=out_2[0, r:16:4, :].bitcast(I32), in_=y_s[r:P:32, :].bitcast(I32))
 
         on_scalar, on_vector = nc.scalar.copy, nc.vector.tensor_copy
-        second, third, fourth = CHUNK, 2 * CHUNK, 3 * CHUNK
-        first, last = S - 2 * NARROW, S - NARROW
+
+        for plane in (tab_s, tab2_s, wd_s_raw, wo_s_raw):
+            nc.vector.memset(plane[:].bitcast(I32), 0)
 
         load_table(tab2_w, tab2_words[0])
         nc.sync.dma_start(list2[:], offs2)
@@ -362,113 +293,119 @@ def tile_list_visit_risk_burden_kernel(
         load_scales_by_row(nc.sync, wd_s_raw, wd_scales)
         nc.sync.dma_start(list1[:], offs)
         load_wp(0, 0)
+        load_time(0, 0, HALF)
         load_wp(0, 1)
+        for q in range(4):
+            load_scales(nc.sync, wo_s_raw, wo_scales, WO_ROW, q)
         load_table(tab_w[1], tab_words[1])
-        load_time(0, 0, CHUNK)
-        load_scales(nc.sync, wo_s_raw, wo_scales, WO_ROW, 0)
-        load_time(0, second, CHUNK)
-        load_scales(nc.sync, wo_s_raw, wo_scales, WO_ROW, 1)
         load_wp(1, 0)
-        load_scales(nc.sync, wo_s_raw, wo_scales, WO_ROW, 2)
         load_wp(1, 1)
-        load_scales(nc.sync, wo_s_raw, wo_scales, WO_ROW, 3)
         load_time(1, 0, CHUNK)
         load_wo()
-        load_by_slices(bias, bo)
+        load_by_slices(nc.sync, bias, bo)
+        load_by_slices(nc.sync, weight, cost)
         load_time(1, second, CHUNK)
-        load_by_slices(weight, cost)
         load_time(1, third, CHUNK)
-        load_time(1, fourth, CHUNK)
         load_time(0, third, CHUNK)
+        load_time(1, fourth, CHUNK)
         load_time(0, fourth, CHUNK)
         for q in range(4):
             load_scales(nc.gpsimd, tab_s, tab_scales, TAB_ROW, q)
 
         gather(v2_w, tab2_w, list2, 0, S)
         gather(v2_s, tab2_s, list2, 0, S)
-        deal(nc.vector, wd_w[:].bitcast(U16), wd_raw[:].bitcast(U16), 8)
-        deal(nc.vector, wd_s[:], wd_s_raw[:], 16)
+        deal(on_scalar, wd_w[:].bitcast(U16), wd_raw[:].bitcast(U16), 8)
+        deal(on_vector, wd_s[:], wd_s_raw[:], 16)
         gather(v_w[0], tab_w[0], list1, 0, S)
         gather(v_s, tab_s, list1, 0, S)
+        deal(on_vector, wo_s[:], wo_s_raw[:], 16)
         round_wp(0, 0, on_scalar)
         quantize_wp(0, 0)
+        for b in range(4):
+            b_times_time(0, b // 2 * CHUNK, b % 2, b)
+        park_b(0, third, (4, 5))
+        park_b(0, fourth, (6, 7))
         round_wp(0, 1, on_scalar)
         quantize_wp(0, 1)
-        park_plain(0, third, rooms[2][:], (0, 1))
-        park_plain(0, fourth, rooms[3][:], (2, 3))
-        park_plain(0, 0, rooms[0][:], (4, 5))
-        park_plain(0, second, rooms[1][:], (6, 7))
-        for b in range(4):
-            pass_a(0, third + b // 2 * CHUNK, 0, b, 2 * (b % 2), 2)
-        park_plain(1, third, wp_raw[0][1][:, 0 : PACK * CHUNK], (4, 5))
-        park_plain(1, fourth, wp_raw[0][1][:, PACK * CHUNK :], (6, 7))
-        gather(v_w[1], tab_w[1], list1, HALF, HALF)
-        for b in range(4):
-            a_times_parked(0, third + b // 2 * CHUNK, b % 2, b)
+        park_b(1, 0, (4, 5))
+        park_b(1, second, (6, 7))
         for c in range(4):
-            pass_a(0, c * NARROW, 0, 4 + c, 0, PACK)
+            pass_a(0, c * NARROW, 0, c, 0, PACK)
+        park_b(1, third, (4, 5))
+        park_b(1, fourth, (6, 7))
         gather(v_w[1], tab_w[1], list1, 0, HALF)
-        plain_times_time(0, 0, NARROW)
-        plain_times_time(0, second, NARROW)
+        gather(v_w[1], tab_w[1], list1, HALF, HALF)
         for c in range(4):
-            h_by_a_plain(0, c * NARROW, 4 + c)
+            h_by_a(0, c * NARROW, c)
         round_wp(1, 0, on_scalar)
-        round_wp(1, 1, on_scalar)
         quantize_wp(1, 0)
-        b_times_time(1, 0, 0, rooms[0][:], 0)
-        b_times_time(1, 0, 1, rooms[0][:], 1)
-        pass_a(1, 0, 0, 2, 0, PACK)
-        pass_a(1, NARROW, 0, 3, 0, PACK)
-        pass_a(1, second, 0, 6, 0, PACK)
-        pass_a(1, second + NARROW, 0, 7, 0, PACK)
+        for b in range(4):
+            pass_a(0, third + b // 2 * CHUNK, 0, 4 + b, 2 * (b % 2), 2)
+            a_times_parked(0, third + b // 2 * CHUNK, b % 2, 4 + b)
+        for c in range(4):
+            pass_a(1, c * NARROW, 0, c, 0, PACK)
+        round_wp(1, 1, on_scalar)
+        quantize_h(0, 0, CHUNK)
         quantize_wp(1, 1)
-        deal_wo(nc.vector)
-        deal(nc.vector, wo_s[:], wo_s_raw[:], 16)
-        h_by_a(1, 0, 2)
-        h_by_a(1, NARROW, 3)
-        b_times_time(1, second, 0, rooms[1][:], 4)
-        quantize_h(0, HALF)
-        make_risk(0, CHUNK, (0, 1))
+        deal(on_scalar, wo_w[:], wo_raw[:], 4)
+        parked_times_time(nc.vector, 1, 0, CHUNK, CHUNK)
+        h_by_a(1, 0, 0)
+        h_by_a(1, NARROW, 1)
+        quantize_h(0, second, CHUNK)
+        quantize_h(1, 0, CHUNK)
+        make_risk(0, 0, 4, 1)
+        make_risk(0, 1, 5, 1)
         make_y(0, weigh_on_scalar)
-        round_y(0, on_scalar)
-        b_times_time(1, second, 1, rooms[1][:], 5)
-        h_by_a(1, second, 6)
-        h_by_a(1, second + NARROW, 7)
-        plain_times_time(1, third, 64)
-        plain_times_time(1, fourth, 64)
-        pass_a(1, third, 0, 2, 0, PACK)
-        h_by_a_plain(1, third, 2)
-        quantize_h(second, HALF)
-        make_risk(second, CHUNK, (4, 5))
+        store_y(nc.sync, 0)
+        parked_times_time(nc.vector, 1, second, CHUNK, CHUNK)
+        h_by_a(1, second, 2)
+        h_by_a(1, second + NARROW, 3)
+        parked_times_time(nc.vector, 1, third, CHUNK, CHUNK)
+        quantize_h(1, second, CHUNK)
+        make_risk(second, 0, 6, 1)
+        make_risk(second, 1, 7, 1)
         make_y(second, weigh_on_scalar)
-        pass_a(1, third + NARROW, 0, 3, 0, PACK)
-        h_by_a_plain(1, third + NARROW, 3)
+        store_y(nc.sync, second)
+        round_y(0, on_scalar)
+        for c in range(2):
+            pass_a(1, third + c * NARROW, 0, c, 0, PACK)
+            h_by_a(1, third + c * NARROW, c)
         h_by_time(0, third, CHUNK)
-        h_by_time(0, first, NARROW)
-        quantize_h(third, HALF)
-        make_y_by_pairs(third, (0, 1))
-        pass_a(1, first, 0, 6, 0, PACK)
-        h_by_a_plain(1, first, 6)
+        quantize_h(1, third, CHUNK)
+        parked_times_time(nc.vector, 1, fourth, NARROW, NARROW)
+        quantize_h(0, third, CHUNK)
+        make_risk(third, 0, 2, 0)
+        make_y(third, weigh_on_scalar, 0, 2)
+        store_y(nc.sync, third, 0, 2)
+        make_risk(third, 1, 3, 0)
+        make_y(third, weigh_on_scalar, 2, 4)
+        store_y(nc.sync, third, 2, 4)
+        pass_a(1, fourth, 0, 0, 0, PACK)
+        h_by_a(1, fourth, 0)
+        h_by_time(0, fourth, NARROW)
+        parked_times_time(nc.vector, 1, last, NARROW, NARROW)
+        quantize_h(0, fourth, CHUNK)
+        make_risk(fourth, 0, 4, 1)
+        make_risk(fourth, 1, 5, 1)
+        pass_a(1, last, 0, 1, 0, PACK)
+        h_by_a(1, last, 1)
         h_by_time(0, last, NARROW)
-        quantize_h(first, CHUNK)
-        make_risk(first, NARROW, (2, 3))
-        pass_a(1, last, 0, 7, 0, PACK)
-        h_by_a_plain(1, last, 7)
         quantize_y(0, CHUNK)
-        store_words(0, CHUNK, nc.sync)
-        quantize_h(last, CHUNK)
-        make_risk(last, NARROW, (4, 5))
+        store_words(nc.sync, 0, CHUNK)
+        quantize_h(0, last, CHUNK)
+        make_risk(last, 0, 6, 1)
+        make_risk(last, 1, 7, 1)
         round_y(second, on_vector)
-        quantize_y(second, CHUNK)
-        store_words(second, CHUNK, nc.sync)
         round_y(third, on_vector)
-        make_y(first, weigh_on_vector)
-        round_y(first, on_vector)
+        quantize_y(second, CHUNK)
+        make_y(fourth, weigh_on_scalar)
+        store_y(nc.sync, fourth)
         make_y(last, weigh_on_scalar)
+        store_y(nc.sync, last)
         quantize_y(third, CHUNK)
-        store_words(third, CHUNK, nc.sync)
+        store_words(nc.sync, second, HALF)
+        weigh_and_round(fourth)
         weigh_and_round(last)
-        quantize_y(first, NARROW)
-        quantize_y(last, NARROW)
-        store_words(first, CHUNK, nc.sync)
+        quantize_y(fourth, CHUNK)
+        store_words(nc.sync, fourth, CHUNK)
         store_scales(nc.scalar)

@@ -60,7 +60,8 @@ def tile_list_visit_risk_burden_kernel(
         wp_raw = [[held("wp_raw%d%d" % (g, a), [P, PACK * PASS], F32) for a in range(2)] for g in range(2)]
         wp_w = [[held("wp_w%d%d" % (g, a), [P, PASS], U32) for a in range(2)] for g in range(2)]
         wp_s = [[held("wp_s%d%d" % (g, a), [P, PASS], U8) for a in range(2)] for g in range(2)]
-        rounded = [held("rounded%d" % a, [P, PACK * PASS], BF16) for a in range(2)]
+        shared = held("shared", [P, 2 * PACK * CHUNK], F32)
+        rounded = [held("rounded0", [P, PACK * PASS], BF16)[:], shared[:, 2 * CHUNK : 6 * CHUNK].bitcast(BF16)]
         h_bf = held("h_bf", [P, 2 * PACK * S], BF16)
         h_w = held("h_w", [P, 2 * S], U32)
         h_s = held("h_s", [P, 2 * S], U8)
@@ -74,6 +75,7 @@ def tile_list_visit_risk_burden_kernel(
         second, third, fourth = CHUNK, 2 * CHUNK, 3 * CHUNK
         last = S - NARROW
         runs = {0: CHUNK, second: CHUNK, third: CHUNK, fourth: NARROW, last: NARROW}
+        spans = {0: CHUNK, second: CHUNK, third: CHUNK, fourth: NARROW, last: NARROW}
         time_f = {}
         partial = {}
         risk = {}
@@ -130,12 +132,12 @@ def tile_list_visit_risk_burden_kernel(
 
         def round_wp(g, a, copy, m0=0, m1=P):
             copy(
-                out=rounded[a][:].rearrange("p (t m i) -> p m i t", t=PACK, i=PACK)[:, m0:m1, :, :],
+                out=rounded[a].rearrange("p (t m i) -> p m i t", t=PACK, i=PACK)[:, m0:m1, :, :],
                 in_=wp_raw[g][a][:].rearrange("p (i m t) -> p m i t", i=PACK, t=PACK)[:, m0:m1, :, :],
             )
 
         def quantize_wp(g, a):
-            nc.vector.quantize_mx(out=wp_w[g][a][:].bitcast(FP8X4), scales=wp_s[g][a][:], in_=rounded[a][:])
+            nc.vector.quantize_mx(out=wp_w[g][a][:].bitcast(FP8X4), scales=wp_s[g][a][:], in_=rounded[a])
 
         def slices(b, count):
             return bank[b][:].rearrange("p (t n) -> p t n", t=count)
@@ -160,11 +162,14 @@ def tile_list_visit_risk_burden_kernel(
                     start=True, stop=True,
                 )
 
-        def b_times_time(g, j0, pair, b):
-            partial[g, j0] = factors(g, j0, CHUNK)
-            rows = partial[g, j0][:, 2 * pair : 2 * pair + 2, :]
+        def by_slices(flat):
+            return flat.rearrange("p (t n) -> p t n", t=PACK)
+
+        def b_times_time(g, j0, pair, b, room):
+            partial[g, j0] = room
+            rows = slice(2 * pair, 2 * pair + 2)
             product_b(g, j0, pair, b)
-            nc.vector.tensor_tensor(rows, rows, slices(b, 2), MULT)
+            nc.vector.tensor_tensor(room[:, rows, :], factors(g, j0, CHUNK)[:, rows, :], slices(b, 2), MULT)
 
         def park_b(g, j0, banks):
             partial[g, j0] = held("parked%d_%d" % (g, j0), [P, PACK, CHUNK], F32)[:]
@@ -172,9 +177,12 @@ def tile_list_visit_risk_burden_kernel(
                 product_b(g, j0, pair, banks[pair])
                 nc.scalar.copy(out=partial[g, j0][:, 2 * pair : 2 * pair + 2, :], in_=slices(banks[pair], 2))
 
-        def parked_times_time(engine, g, j0, width, step):
-            for c0 in range(j0, j0 + width, step):
-                engine.tensor_tensor(part(g, c0, step), part(g, c0, step), factors(g, c0, step), MULT)
+        def parked_times_time(g, j0, step, room):
+            parked = partial[g, j0]
+            partial[g, j0] = room
+            for c0 in range(0, CHUNK, step):
+                cols = slice(c0, c0 + step)
+                nc.gpsimd.tensor_tensor(room[:, :, cols], parked[:, :, cols], factors(g, j0 + c0, step), MULT)
 
         def pass_a(g, j0, a, b, t0, count):
             width = HALF // count
@@ -189,8 +197,8 @@ def tile_list_visit_risk_burden_kernel(
                 )
 
         def h_at(g, j0):
-            start = max(r for r in runs if r <= j0)
-            return 2 * start + g * runs[start] + j0 - start
+            start = max(r for r in spans if r <= j0)
+            return 2 * start + g * spans[start] + j0 - start
 
         def h_of(g, j0, width):
             w0 = h_at(g, j0)
@@ -293,118 +301,123 @@ def tile_list_visit_risk_burden_kernel(
         load_scales_by_row(nc.sync, wd_s_raw, wd_scales)
         nc.sync.dma_start(list1[:], offs)
         load_wp(0, 0)
-        load_time(0, 0, HALF)
         load_wp(0, 1)
-        for q in range(4):
-            load_scales(nc.sync, wo_s_raw, wo_scales, WO_ROW, q)
         load_table(tab_w[1], tab_words[1])
+        load_time(0, 0, CHUNK)
+        load_scales(nc.sync, wo_s_raw, wo_scales, WO_ROW, 0)
+        load_time(0, second, CHUNK)
+        load_scales(nc.sync, wo_s_raw, wo_scales, WO_ROW, 1)
         load_wp(1, 0)
+        load_scales(nc.sync, wo_s_raw, wo_scales, WO_ROW, 2)
         load_wp(1, 1)
+        load_scales(nc.sync, wo_s_raw, wo_scales, WO_ROW, 3)
         load_time(1, 0, CHUNK)
+        load_time(1, third, CHUNK)
         load_wo()
         load_by_slices(nc.sync, bias, bo)
-        load_by_slices(nc.sync, weight, cost)
         load_time(1, second, CHUNK)
-        load_time(1, third, CHUNK)
-        load_time(0, third, CHUNK)
+        load_by_slices(nc.sync, weight, cost)
         load_time(1, fourth, CHUNK)
+        load_time(0, third, CHUNK)
         load_time(0, fourth, CHUNK)
         for q in range(4):
             load_scales(nc.gpsimd, tab_s, tab_scales, TAB_ROW, q)
 
         gather(v2_w, tab2_w, list2, 0, S)
         gather(v2_s, tab2_s, list2, 0, S)
-        deal(on_scalar, wd_w[:].bitcast(U16), wd_raw[:].bitcast(U16), 8)
+        deal(on_vector, wd_w[:].bitcast(U16), wd_raw[:].bitcast(U16), 8)
         deal(on_vector, wd_s[:], wd_s_raw[:], 16)
         gather(v_w[0], tab_w[0], list1, 0, S)
         gather(v_s, tab_s, list1, 0, S)
-        deal(on_vector, wo_s[:], wo_s_raw[:], 16)
         round_wp(0, 0, on_scalar)
         quantize_wp(0, 0)
-        for b in range(4):
-            b_times_time(0, b // 2 * CHUNK, b % 2, b)
-        park_b(0, third, (4, 5))
-        park_b(0, fourth, (6, 7))
         round_wp(0, 1, on_scalar)
         quantize_wp(0, 1)
-        park_b(1, 0, (4, 5))
-        park_b(1, second, (6, 7))
-        for c in range(4):
-            pass_a(0, c * NARROW, 0, c, 0, PACK)
+        park_b(0, third, (0, 1))
+        park_b(0, fourth, (2, 3))
+        park_b(0, 0, (4, 5))
+        park_b(0, second, (6, 7))
+        for b in range(4):
+            pass_a(0, third + b // 2 * CHUNK, 0, b, 2 * (b % 2), 2)
         park_b(1, third, (4, 5))
         park_b(1, fourth, (6, 7))
-        gather(v_w[1], tab_w[1], list1, 0, HALF)
         gather(v_w[1], tab_w[1], list1, HALF, HALF)
-        for c in range(4):
-            h_by_a(0, c * NARROW, c)
-        round_wp(1, 0, on_scalar)
-        quantize_wp(1, 0)
         for b in range(4):
-            pass_a(0, third + b // 2 * CHUNK, 0, 4 + b, 2 * (b % 2), 2)
-            a_times_parked(0, third + b // 2 * CHUNK, b % 2, 4 + b)
+            a_times_parked(0, third + b // 2 * CHUNK, b % 2, b)
         for c in range(4):
-            pass_a(1, c * NARROW, 0, c, 0, PACK)
+            pass_a(0, c * NARROW, 0, 4 + c, 0, PACK)
+        gather(v_w[1], tab_w[1], list1, 0, HALF)
+        parked_times_time(0, 0, NARROW, partial[0, 0])
+        parked_times_time(0, second, NARROW, partial[0, second])
+        for c in range(4):
+            h_by_a(0, c * NARROW, 4 + c)
+        round_wp(1, 0, on_scalar)
         round_wp(1, 1, on_scalar)
+        quantize_wp(1, 0)
+        deal(on_vector, wo_s[:], wo_s_raw[:], 16)
         quantize_h(0, 0, CHUNK)
+        b_times_time(1, 0, 0, 0, by_slices(shared[:, 0 : PACK * CHUNK]))
+        pass_a(1, 0, 0, 2, 0, PACK)
+        pass_a(1, NARROW, 0, 3, 0, PACK)
+        pass_a(1, second, 0, 6, 0, PACK)
+        pass_a(1, second + NARROW, 0, 7, 0, PACK)
         quantize_wp(1, 1)
+        b_times_time(1, 0, 1, 1, by_slices(shared[:, 0 : PACK * CHUNK]))
         deal(on_scalar, wo_w[:], wo_raw[:], 4)
-        parked_times_time(nc.vector, 1, 0, CHUNK, CHUNK)
-        h_by_a(1, 0, 0)
-        h_by_a(1, NARROW, 1)
-        quantize_h(0, second, CHUNK)
+        parked_times_time(1, third, NARROW, by_slices(shared[:, PACK * CHUNK :]))
+        parked_times_time(1, fourth, 64, partial[1, fourth])
+        h_by_a(1, 0, 2)
+        h_by_a(1, NARROW, 3)
+        b_times_time(1, second, 0, 4, factors(1, second, CHUNK))
         quantize_h(1, 0, CHUNK)
-        make_risk(0, 0, 4, 1)
-        make_risk(0, 1, 5, 1)
+        make_risk(0, 0, 0, 1)
+        make_risk(0, 1, 1, 1)
         make_y(0, weigh_on_scalar)
         store_y(nc.sync, 0)
-        parked_times_time(nc.vector, 1, second, CHUNK, CHUNK)
-        h_by_a(1, second, 2)
-        h_by_a(1, second + NARROW, 3)
-        parked_times_time(nc.vector, 1, third, CHUNK, CHUNK)
-        quantize_h(1, second, CHUNK)
-        make_risk(second, 0, 6, 1)
-        make_risk(second, 1, 7, 1)
+        round_y(0, on_scalar)
+        b_times_time(1, second, 1, 5, factors(1, second, CHUNK))
+        h_by_a(1, second, 6)
+        h_by_a(1, second + NARROW, 7)
+        pass_a(1, third, 0, 2, 0, PACK)
+        h_by_a(1, third, 2)
+        quantize_h(0, second, HALF)
+        make_risk(second, 0, 4, 1)
+        make_risk(second, 1, 5, 1)
         make_y(second, weigh_on_scalar)
         store_y(nc.sync, second)
-        round_y(0, on_scalar)
-        for c in range(2):
-            pass_a(1, third + c * NARROW, 0, c, 0, PACK)
-            h_by_a(1, third + c * NARROW, c)
+        pass_a(1, third + NARROW, 0, 3, 0, PACK)
+        h_by_a(1, third + NARROW, 3)
         h_by_time(0, third, CHUNK)
-        quantize_h(1, third, CHUNK)
-        parked_times_time(nc.vector, 1, fourth, NARROW, NARROW)
-        quantize_h(0, third, CHUNK)
-        make_risk(third, 0, 2, 0)
+        pass_a(1, fourth, 0, 6, 0, PACK)
+        h_by_a(1, fourth, 6)
+        quantize_h(0, third, HALF)
+        make_risk(third, 0, 0, 1)
         make_y(third, weigh_on_scalar, 0, 2)
         store_y(nc.sync, third, 0, 2)
-        make_risk(third, 1, 3, 0)
+        make_risk(third, 1, 1, 1)
         make_y(third, weigh_on_scalar, 2, 4)
         store_y(nc.sync, third, 2, 4)
-        pass_a(1, fourth, 0, 0, 0, PACK)
-        h_by_a(1, fourth, 0)
         h_by_time(0, fourth, NARROW)
-        parked_times_time(nc.vector, 1, last, NARROW, NARROW)
+        pass_a(1, last, 0, 7, 0, PACK)
+        h_by_a(1, last, 7)
         quantize_h(0, fourth, CHUNK)
-        make_risk(fourth, 0, 4, 1)
-        make_risk(fourth, 1, 5, 1)
-        pass_a(1, last, 0, 1, 0, PACK)
-        h_by_a(1, last, 1)
+        make_risk(fourth, 0, 2, 1)
+        make_risk(fourth, 1, 3, 1)
         h_by_time(0, last, NARROW)
         quantize_y(0, CHUNK)
         store_words(nc.sync, 0, CHUNK)
         quantize_h(0, last, CHUNK)
-        make_risk(last, 0, 6, 1)
-        make_risk(last, 1, 7, 1)
+        make_risk(last, 0, 4, 1)
+        make_risk(last, 1, 5, 1)
         round_y(second, on_vector)
         round_y(third, on_vector)
-        quantize_y(second, CHUNK)
+        weigh_and_round(fourth)
         make_y(fourth, weigh_on_scalar)
         store_y(nc.sync, fourth)
         make_y(last, weigh_on_scalar)
         store_y(nc.sync, last)
-        quantize_y(third, CHUNK)
+        quantize_y(second, HALF)
         store_words(nc.sync, second, HALF)
-        weigh_and_round(fourth)
         weigh_and_round(last)
         quantize_y(fourth, CHUNK)
         store_words(nc.sync, fourth, CHUNK)

@@ -62,7 +62,6 @@ def tile_list_visit_risk_burden_kernel(
         wp_s = [[held("wp_s%d%d" % (g, a), [P, PASS], U8) for a in range(2)] for g in range(2)]
         shared = held("shared", [P, 2 * PACK * CHUNK], F32)
         rounded = [held("rounded0", [P, PACK * PASS], BF16)[:], shared[:, 2 * CHUNK : 6 * CHUNK].bitcast(BF16)]
-        h_bf = held("h_bf", [P, 2 * PACK * S], BF16)
         h_w = held("h_w", [P, 2 * S], U32)
         h_s = held("h_s", [P, 2 * S], U8)
         y_bf = held("y_bf", [P, PACK * S], BF16)
@@ -78,8 +77,6 @@ def tile_list_visit_risk_burden_kernel(
         spans = {0: CHUNK, second: CHUNK, third: CHUNK, fourth: NARROW, last: NARROW}
         time_f = {}
         partial = {}
-        risk = {}
-        y = {}
 
         def words(dram):
             return dram.rearrange("p n t -> p (n t)").bitcast(I32)
@@ -171,8 +168,14 @@ def tile_list_visit_risk_burden_kernel(
             product_b(g, j0, pair, b)
             nc.vector.tensor_tensor(room[:, rows, :], factors(g, j0, CHUNK)[:, rows, :], slices(b, 2), MULT)
 
-        def park_b(g, j0, banks):
-            partial[g, j0] = held("parked%d_%d" % (g, j0), [P, PACK, CHUNK], F32)[:]
+        def new_room(g, j0):
+            return held("parked%d_%d" % (g, j0), [P, PACK, CHUNK], F32)[:]
+
+        def half_of(tile, k):
+            return by_slices(tile[:, k * PACK * CHUNK : (k + 1) * PACK * CHUNK])
+
+        def park_b(g, j0, banks, room):
+            partial[g, j0] = room
             for pair in range(2):
                 product_b(g, j0, pair, banks[pair])
                 nc.scalar.copy(out=partial[g, j0][:, 2 * pair : 2 * pair + 2, :], in_=slices(banks[pair], 2))
@@ -201,8 +204,11 @@ def tile_list_visit_risk_burden_kernel(
             return 2 * start + g * spans[start] + j0 - start
 
         def h_of(g, j0, width):
-            w0 = h_at(g, j0)
-            return h_bf[:, PACK * w0 : PACK * (w0 + width)]
+            w0 = h_at(g, j0) % HALF
+            return h_bf[j0 // CHUNK][:, PACK * w0 : PACK * (w0 + width)]
+
+        def bytes_of_factors(g, j0):
+            return factors(g, j0, CHUNK).rearrange("p t n -> p (t n)").bitcast(BF16)
 
         def h_by_a(g, j0, b):
             pass_a(g, j0, 1, b, 0, PACK)
@@ -236,18 +242,22 @@ def tile_list_visit_risk_burden_kernel(
                 )
             return z
 
-        def room(raw, j0):
-            c0 = PACK * (j0 % HALF)
-            return raw[j0 // HALF][:, c0 : c0 + PACK * runs[j0]].rearrange("p (t n) -> p t n", t=PACK)
+        def columns(raw, j0, width):
+            c0 = j0 % CHUNK
+            return half_of(raw[j0 // HALF], j0 % HALF // CHUNK)[:, :, c0 : c0 + width]
+
+        def risk(j0, width):
+            return columns(wp_raw[1], j0, width)
+
+        def y(j0, width):
+            return columns(wp_raw[0], j0, width)
 
         def make_risk(j0, pair, b, g):
-            risk[j0] = room(wp_raw[1], j0)
-            y[j0] = room(wp_raw[0], j0)
             pass_z(j0, pair, b, 1 - g, True)
             z = pass_z(j0, pair, b, g, False)
             for u in range(2):
                 t = 2 * pair + u
-                nc.scalar.activation(risk[j0][:, t, :], z[:, u, :], SIGMOID, bias=bias[:, t : t + 1])
+                nc.scalar.activation(risk(j0, runs[j0])[:, t, :], z[:, u, :], SIGMOID, bias=bias[:, t : t + 1])
 
         def weigh_on_scalar(dst, src, t):
             nc.scalar.activation(dst, src, COPY, scale=weight[:, t : t + 1])
@@ -255,22 +265,21 @@ def tile_list_visit_risk_burden_kernel(
         def weigh_on_vector(dst, src, t):
             nc.vector.tensor_scalar(dst, src, weight[:, t : t + 1], None, MULT)
 
-        def make_y(j0, weigh, t0=0, t1=PACK):
+        def make_y(j0, width, weigh, t0=0, t1=PACK):
             for t in range(t0, t1):
-                weigh(y[j0][:, t, :], risk[j0][:, t, :], t)
+                weigh(y(j0, width)[:, t, :], risk(j0, width)[:, t, :], t)
 
-        def store_y(queue, j0, t0=0, t1=PACK):
-            rows = out_0[:, j0 : j0 + runs[j0]].rearrange("(p t) j -> p t j", t=PACK)
-            queue.dma_start(out=rows[:, t0:t1, :], in_=y[j0][:, t0:t1, :])
+        def store_y(j0, width, t0=0, t1=PACK):
+            rows = out_0[:, j0 : j0 + width].rearrange("(p t) j -> p t j", t=PACK)
+            nc.sync.dma_start(out=rows[:, t0:t1, :], in_=y(j0, width)[:, t0:t1, :])
 
-        def round_y(j0, copy):
-            copy(out=woven(y_bf[:, PACK * j0 : PACK * (j0 + runs[j0])]), in_=in_fours(y[j0]))
+        def round_y(j0, width, copy):
+            copy(out=woven(y_bf[:, PACK * j0 : PACK * (j0 + width)]), in_=in_fours(y(j0, width)))
 
-        def weigh_and_round(j0):
-            width = runs[j0]
+        def weigh_and_round(j0, width):
             nc.vector.tensor_tensor(
                 woven(y_bf[:, PACK * j0 : PACK * (j0 + width)]),
-                in_fours(risk[j0]),
+                in_fours(risk(j0, width)),
                 weight[:].unsqueeze(1).unsqueeze(3).to_broadcast([P, width // 4, PACK, 4]),
                 MULT,
             )
@@ -322,6 +331,7 @@ def tile_list_visit_risk_burden_kernel(
         load_time(0, fourth, CHUNK)
         for q in range(4):
             load_scales(nc.gpsimd, tab_s, tab_scales, TAB_ROW, q)
+        h_bf = [held("h_bf%d" % k, [P, 2 * PACK * CHUNK], BF16)[:] for k in range(4)]
 
         gather(v2_w, tab2_w, list2, 0, S)
         gather(v2_s, tab2_s, list2, 0, S)
@@ -333,14 +343,14 @@ def tile_list_visit_risk_burden_kernel(
         quantize_wp(0, 0)
         round_wp(0, 1, on_scalar)
         quantize_wp(0, 1)
-        park_b(0, third, (0, 1))
-        park_b(0, fourth, (2, 3))
-        park_b(0, 0, (4, 5))
-        park_b(0, second, (6, 7))
+        park_b(0, third, (0, 1), new_room(0, third))
+        park_b(0, fourth, (2, 3), new_room(0, fourth))
+        park_b(0, 0, (4, 5), new_room(0, 0))
+        park_b(0, second, (6, 7), new_room(0, second))
         for b in range(4):
             pass_a(0, third + b // 2 * CHUNK, 0, b, 2 * (b % 2), 2)
-        park_b(1, third, (4, 5))
-        park_b(1, fourth, (6, 7))
+        park_b(1, third, (4, 5), new_room(1, third))
+        park_b(1, fourth, (6, 7), new_room(1, fourth))
         gather(v_w[1], tab_w[1], list1, HALF, HALF)
         for b in range(4):
             a_times_parked(0, third + b // 2 * CHUNK, b % 2, b)
@@ -372,9 +382,9 @@ def tile_list_visit_risk_burden_kernel(
         quantize_h(1, 0, CHUNK)
         make_risk(0, 0, 0, 1)
         make_risk(0, 1, 1, 1)
-        make_y(0, weigh_on_scalar)
-        store_y(nc.sync, 0)
-        round_y(0, on_scalar)
+        make_y(0, CHUNK, weigh_on_scalar)
+        store_y(0, CHUNK)
+        round_y(0, CHUNK, on_scalar)
         b_times_time(1, second, 1, 5, factors(1, second, CHUNK))
         h_by_a(1, second, 6)
         h_by_a(1, second + NARROW, 7)
@@ -383,8 +393,8 @@ def tile_list_visit_risk_burden_kernel(
         quantize_h(0, second, HALF)
         make_risk(second, 0, 4, 1)
         make_risk(second, 1, 5, 1)
-        make_y(second, weigh_on_scalar)
-        store_y(nc.sync, second)
+        make_y(second, CHUNK, weigh_on_scalar)
+        store_y(second, CHUNK)
         pass_a(1, third + NARROW, 0, 3, 0, PACK)
         h_by_a(1, third + NARROW, 3)
         h_by_time(0, third, CHUNK)
@@ -392,11 +402,9 @@ def tile_list_visit_risk_burden_kernel(
         h_by_a(1, fourth, 6)
         quantize_h(0, third, HALF)
         make_risk(third, 0, 0, 1)
-        make_y(third, weigh_on_scalar, 0, 2)
-        store_y(nc.sync, third, 0, 2)
+        make_y(third, CHUNK, weigh_on_scalar, 0, 2)
+        store_y(third, CHUNK, 0, 2)
         make_risk(third, 1, 1, 1)
-        make_y(third, weigh_on_scalar, 2, 4)
-        store_y(nc.sync, third, 2, 4)
         h_by_time(0, fourth, NARROW)
         pass_a(1, last, 0, 7, 0, PACK)
         h_by_a(1, last, 7)
@@ -409,16 +417,18 @@ def tile_list_visit_risk_burden_kernel(
         quantize_h(0, last, CHUNK)
         make_risk(last, 0, 4, 1)
         make_risk(last, 1, 5, 1)
-        round_y(second, on_vector)
-        round_y(third, on_vector)
-        weigh_and_round(fourth)
-        make_y(fourth, weigh_on_scalar)
-        store_y(nc.sync, fourth)
-        make_y(last, weigh_on_scalar)
-        store_y(nc.sync, last)
+        make_y(third, CHUNK, weigh_on_vector, 2, 4)
+        store_y(third, CHUNK, 2, 4)
+        round_y(second, CHUNK, on_vector)
+        round_y(third, CHUNK, on_vector)
+        weigh_and_round(fourth, NARROW)
+        make_y(fourth, NARROW, weigh_on_scalar)
+        store_y(fourth, NARROW)
+        make_y(last, NARROW, weigh_on_scalar)
+        store_y(last, NARROW)
         quantize_y(second, HALF)
         store_words(nc.sync, second, HALF)
-        weigh_and_round(last)
+        weigh_and_round(last, NARROW)
         quantize_y(fourth, CHUNK)
         store_words(nc.sync, fourth, CHUNK)
         store_scales(nc.scalar)

@@ -57,11 +57,15 @@ def tile_list_visit_risk_burden_kernel(
         wo_s = held("wo_s", [P, N], U8)
         wo_raw = held("wo_raw", [P, 2 * N], U32)
         wo_w = held("wo_w", [P, 2 * N], U32)
-        wp_raw = [[held("wp_raw%d%d" % (g, a), [P, PACK * PASS], F32) for a in range(2)] for g in range(2)]
+        late = held("late", [P, 2 * CHUNK + PACK * PASS], F32)
+        wp_raw = [
+            [held("wp_raw00", [P, PACK * PASS], F32)[:], held("wp_raw01", [P, PACK * PASS], F32)[:]],
+            [held("wp_raw10", [P, PACK * PASS], F32)[:], late[:, 2 * CHUNK :]],
+        ]
         wp_w = [[held("wp_w%d%d" % (g, a), [P, PASS], U32) for a in range(2)] for g in range(2)]
         wp_s = [[held("wp_s%d%d" % (g, a), [P, PASS], U8) for a in range(2)] for g in range(2)]
-        shared = held("shared", [P, 2 * PACK * CHUNK], F32)
-        rounded = [held("rounded0", [P, PACK * PASS], BF16)[:], shared[:, 2 * CHUNK : 6 * CHUNK].bitcast(BF16)]
+        shared = held("shared", [P, PACK * CHUNK], F32)
+        rounded = [held("rounded0", [P, PACK * PASS], BF16)[:], shared[:].bitcast(BF16)]
         h_w = held("h_w", [P, 2 * S], U32)
         h_s = held("h_s", [P, 2 * S], U8)
         y_bf = held("y_bf", [P, PACK * S], BF16)
@@ -103,7 +107,7 @@ def tile_list_visit_risk_burden_kernel(
 
         def load_wp(g, a):
             rows = wp[a * PASS : (a + 1) * PASS, g * PASS : (g + 1) * PASS]
-            nc.sync.dma_start(out=wp_raw[g][a][:].rearrange("p (i c) -> p i c", i=PACK), in_=rows.rearrange("(p i) c -> p i c", i=PACK))
+            nc.sync.dma_start(out=wp_raw[g][a].rearrange("p (i c) -> p i c", i=PACK), in_=rows.rearrange("(p i) c -> p i c", i=PACK))
 
         def load_table(tile, dram):
             nc.sync.dma_start(out=tile[:].bitcast(I32), in_=words(dram))
@@ -130,7 +134,7 @@ def tile_list_visit_risk_burden_kernel(
         def round_wp(g, a, copy, m0=0, m1=P):
             copy(
                 out=rounded[a].rearrange("p (t m i) -> p m i t", t=PACK, i=PACK)[:, m0:m1, :, :],
-                in_=wp_raw[g][a][:].rearrange("p (i m t) -> p m i t", i=PACK, t=PACK)[:, m0:m1, :, :],
+                in_=wp_raw[g][a].rearrange("p (i m t) -> p m i t", i=PACK, t=PACK)[:, m0:m1, :, :],
             )
 
         def quantize_wp(g, a):
@@ -366,20 +370,20 @@ def tile_list_visit_risk_burden_kernel(
         quantize_wp(1, 0)
         deal(on_vector, wo_s[:], wo_s_raw[:], 16)
         quantize_h(0, 0, CHUNK)
-        b_times_time(1, 0, 0, 0, by_slices(shared[:, 0 : PACK * CHUNK]))
+        b_times_time(1, 0, 0, 0, by_slices(late[:, 0 : PACK * CHUNK]))
         pass_a(1, 0, 0, 2, 0, PACK)
         pass_a(1, NARROW, 0, 3, 0, PACK)
         pass_a(1, second, 0, 6, 0, PACK)
         pass_a(1, second + NARROW, 0, 7, 0, PACK)
         quantize_wp(1, 1)
-        b_times_time(1, 0, 1, 1, by_slices(shared[:, 0 : PACK * CHUNK]))
+        b_times_time(1, 0, 1, 1, by_slices(late[:, 0 : PACK * CHUNK]))
         deal(on_scalar, wo_w[:], wo_raw[:], 4)
-        parked_times_time(1, third, NARROW, by_slices(shared[:, PACK * CHUNK :]))
-        parked_times_time(1, fourth, 64, partial[1, fourth])
+        parked_times_time(1, third, NARROW, by_slices(shared[:]))
         h_by_a(1, 0, 2)
         h_by_a(1, NARROW, 3)
         b_times_time(1, second, 0, 4, factors(1, second, CHUNK))
         quantize_h(1, 0, CHUNK)
+        parked_times_time(1, fourth, NARROW, by_slices(h_bf[0].bitcast(F32)))
         make_risk(0, 0, 0, 1)
         make_risk(0, 1, 1, 1)
         make_y(0, CHUNK, weigh_on_scalar)

@@ -374,7 +374,6 @@ def tile_list_visit_risk_burden_kernel(
         pass_a(1, 0, 0, 2, 0, PACK)
         pass_a(1, NARROW, 0, 3, 0, PACK)
         pass_a(1, second, 0, 6, 0, PACK)
-        pass_a(1, second + NARROW, 0, 7, 0, PACK)
         quantize_wp(1, 1)
         b_times_time(1, 0, 1, 1, by_slices(late[:, 0 : PACK * CHUNK]))
         deal(on_scalar, wo_w[:], wo_raw[:], 4)
@@ -385,13 +384,14 @@ def tile_list_visit_risk_burden_kernel(
         quantize_h(1, 0, CHUNK)
         parked_times_time(1, fourth, NARROW, by_slices(h_bf[0].bitcast(F32)))
         make_risk(0, 0, 0, 1)
-        make_risk(0, 1, 1, 1)
+        make_risk(0, 1, 7, 1)
         make_y(0, CHUNK, weigh_on_scalar)
         store_y(0, CHUNK)
         round_y(0, CHUNK, on_scalar)
         b_times_time(1, second, 1, 5, factors(1, second, CHUNK))
         h_by_a(1, second, 6)
-        h_by_a(1, second + NARROW, 7)
+        pass_a(1, second + NARROW, 0, 1, 0, PACK)
+        h_by_a(1, second + NARROW, 1)
         pass_a(1, third, 0, 2, 0, PACK)
         h_by_a(1, third, 2)
         quantize_h(0, second, HALF)
@@ -426,10 +426,10 @@ def tile_list_visit_risk_burden_kernel(
         round_y(second, CHUNK, on_vector)
         round_y(third, CHUNK, on_vector)
         weigh_and_round(fourth, NARROW)
-        make_y(fourth, NARROW, weigh_on_scalar)
-        store_y(fourth, NARROW)
-        make_y(last, NARROW, weigh_on_scalar)
-        store_y(last, NARROW)
+        make_y(fourth, CHUNK, weigh_on_scalar, 0, 2)
+        store_y(fourth, CHUNK, 0, 2)
+        make_y(fourth, CHUNK, weigh_on_scalar, 2, 4)
+        store_y(fourth, CHUNK, 2, 4)
         quantize_y(second, HALF)
         store_words(nc.sync, second, HALF)
         weigh_and_round(last, NARROW)

from contextlib import ExitStack

import concourse.mybir as mybir

K, K2, H, N, T, T2, S = 1024, 512, 1024, 512, 4096, 2048, 1024
FLOPS = 2 * S * (K * H + K2 * H + H * N)

F32 = mybir.dt.float32
BF16 = mybir.dt.bfloat16
I32 = mybir.dt.int32
U32 = mybir.dt.uint32
U16 = mybir.dt.uint16
U8 = mybir.dt.uint8
FP8X4 = mybir.dt.float8_e4m3fn_x4
FP4X4 = mybir.dt.float4_e2m1fn_x4
MULT = mybir.AluOpType.mult
SIGMOID = mybir.ActivationFunctionType.Sigmoid
COPY = mybir.ActivationFunctionType.Copy

P = 128
PACK = 4
PASS = P * PACK
HALF = 512
NARROW = 128
CHUNK = 256
TAB_ROW = 8
WO_ROW = 4


def tile_list_visit_risk_burden_kernel(
    tc, tab_words, tab_scales, tab2_words, tab2_scales, offs, offs2, wp, wd_words, wd_scales,
    tv, wo_words, wo_scales, bo, cost, out_0, out_1, out_2,
):
    nc = tc.nc
    with ExitStack() as ctx:
        keep = ctx.enter_context(tc.tile_pool(name="keep", bufs=1))
        psum = ctx.enter_context(tc.psum_pool(name="psum", bufs=1))

        def held(name, shape, dtype):
            return keep.tile(shape, dtype, name=name, align_bytes=64)

        list1 = held("list1", [P, S // 16], U16)
        list2 = held("list2", [P, S // 16], U16)
        tab_w = [held("tab_w%d" % a, [P, T], U32) for a in range(2)]
        tab_s = held("tab_s", [P, T], U8)
        tab2_w = held("tab2_w", [P, T2], U32)
        tab2_s = held("tab2_s", [P, T2], U8)
        v_w = [held("v_w%d" % a, [P, S], U32) for a in range(2)]
        v_s = held("v_s", [P, S], U8)
        v2_w = held("v2_w", [P, S], U32)
        v2_s = held("v2_s", [P, S], U8)
        wd_raw = held("wd_raw", [P, 2 * H], U8)
        wd_w = held("wd_w", [P, 2 * H], U8)
        wd_s_raw = held("wd_s_raw", [P, H], U8)
        wd_s = held("wd_s", [P, H], U8)
        wo_s_raw = held("wo_s_raw", [P, N], U8)
        wo_s = held("wo_s", [P, N], U8)
        wo_raw = held("wo_raw", [P, 2 * N], U32)
        wo_w = held("wo_w", [P, 2 * N], U32)
        late = held("late", [P, 2 * CHUNK + PACK * PASS], F32)
        wp_raw = [
            [held("wp_raw00", [P, PACK * PASS], F32)[:], held("wp_raw01", [P, PACK * PASS], F32)[:]],
            [held("wp_raw10", [P, PACK * PASS], F32)[:], late[:, 2 * CHUNK :]],
        ]
        wp_w = [[held("wp_w%d%d" % (g, a), [P, PASS], U32) for a in range(2)] for g in range(2)]
        wp_s = [[held("wp_s%d%d" % (g, a), [P, PASS], U8) for a in range(2)] for g in range(2)]
        shared = held("shared", [P, PACK * CHUNK], F32)
        rounded = [held("rounded0", [P, PACK * PASS], BF16)[:], shared[:].bitcast(BF16)]
        h_w = held("h_w", [P, 2 * S], U32)
        h_s = held("h_s", [P, 2 * S], U8)
        y_bf = held("y_bf", [P, PACK * S], BF16)
        y_w = held("y_w", [P, S], U32)
        y_s = held("y_s", [P, S], U8)
        bias = held("bias", [P, PACK], F32)
        weight = held("weight", [P, PACK], F32)
        bank = [psum.tile([P, HALF], F32, name="bank%d" % i) for i in range(8)]

        second, third, fourth = CHUNK, 2 * CHUNK, 3 * CHUNK
        last = S - NARROW
        runs = {0: CHUNK, second: CHUNK, third: CHUNK, fourth: NARROW, last: NARROW}
        spans = {0: CHUNK, second: CHUNK, third: CHUNK, fourth: NARROW, last: NARROW}
        time_f = {}
        partial = {}

        def words(dram):
            return dram.rearrange("p n t -> p (n t)").bitcast(I32)

        def load_scales(queue, plane, scales, row, q):
            first = 32 * q + row
            queue.dma_start(out=plane[first : first + 4 * scales.shape[0], :].bitcast(I32),
                            in_=scales[:, 4 * q : 4 * q + 4, :].bitcast(I32))

        def load_scales_by_row(queue, plane, scales):
            for r in range(4):
                queue.dma_start(out=plane[r:P:32, :].bitcast(I32), in_=scales[0, r:16:4, :].bitcast(I32))

        def load_time(g, j0, width):
            tile = held("time%d_%d" % (g, j0), [P, PACK, width], F32)
            rows = tv[g * PASS : (g + 1) * PASS, j0 : j0 + width]
            nc.sync.dma_start(out=tile[:], in_=rows.rearrange("(p t) j -> p t j", t=PACK))
            for c0 in range(0, width, 64):
                time_f[g, j0 + c0] = (tile, c0)

        def factors(g, j0, width):
            tile, c0 = time_f[g, j0]
            return tile[:, :, c0 : c0 + width]

        def load_wp(g, a):
            rows = wp[a * PASS : (a + 1) * PASS, g * PASS : (g + 1) * PASS]
            nc.sync.dma_start(out=wp_raw[g][a].rearrange("p (i c) -> p i c", i=PACK), in_=rows.rearrange("(p i) c -> p i c", i=PACK))

        def load_table(tile, dram):
            nc.sync.dma_start(out=tile[:].bitcast(I32), in_=words(dram))

        def load_wd():
            nc.sync.dma_start(out=wd_raw[:].bitcast(I32), in_=wd_words[0].bitcast(I32))

        def load_wo():
            nc.sync.dma_start(out=wo_raw[:].bitcast(I32).rearrange("p (a n) -> p a n", a=2),
                              in_=wo_words.rearrange("a p n t -> p a (n t)").bitcast(I32))

        def load_by_slices(queue, tile, vector):
            queue.dma_start(out=tile[:], in_=vector.rearrange("(p t) -> p t", t=PACK))

        def deal(copy, dst, src, run):
            copy(
                out=dst.rearrange("p (g t b m) -> p g b t m", t=PACK, b=P // run, m=run),
                in_=src.rearrange("p (g b m t) -> p g b t m", t=PACK, b=P // run, m=run),
            )

        def gather(dst, window, entries, first, count):
            nc.vector.tensor_copy(dst[:, first : first + count], window[:].indirect(entries[:, first // 16 : (first + count) // 16]))

        def round_wp(g, a, copy, m0=0, m1=P):
            copy(
                out=rounded[a].rearrange("p (t m i) -> p m i t", t=PACK, i=PACK)[:, m0:m1, :, :],
                in_=wp_raw[g][a].rearrange("p (i m t) -> p m i t", i=PACK, t=PACK)[:, m0:m1, :, :],
            )

        def quantize_wp(g, a):
            nc.vector.quantize_mx(out=wp_w[g][a][:].bitcast(FP8X4), scales=wp_s[g][a][:], in_=rounded[a])

        def slices(b, count):
            return bank[b][:].rearrange("p (t n) -> p t n", t=count)

        def in_fours(rows):
            return rows.rearrange("p t (n e) -> p n t e", e=4)

        def woven(flat):
            return flat.rearrange("p (n e t) -> p n t e", e=4, t=PACK)

        def part(g, j0, width):
            c0 = j0 % CHUNK
            return partial[g, j0 - c0][:, :, c0 : c0 + width]

        def product_b(g, j0, pair, b):
            for u in range(2):
                s = PACK * g + 2 * pair + u
                nc.tensor.matmul_mx(
                    out=slices(b, 2)[:, u, :],
                    lhsT=wd_w[:, 2 * P * s : 2 * P * (s + 1)].bitcast(FP4X4), lhsT_scale=wd_s[:, P * s : P * (s + 1)],
                    rhs=v2_w[:, j0 : j0 + CHUNK].bitcast(FP8X4), rhs_scale=v2_s[:, j0 : j0 + CHUNK],
                    start=True, stop=True,
                )

        def by_slices(flat):
            return flat.rearrange("p (t n) -> p t n", t=PACK)

        def b_times_time(g, j0, pair, b, room):
            partial[g, j0] = room
            rows = slice(2 * pair, 2 * pair + 2)
            product_b(g, j0, pair, b)
            nc.vector.tensor_tensor(room[:, rows, :], factors(g, j0, CHUNK)[:, rows, :], slices(b, 2), MULT)

        def new_room(g, j0):
            return held("parked%d_%d" % (g, j0), [P, PACK, CHUNK], F32)[:]

        def half_of(tile, k):
            return by_slices(tile[:, k * PACK * CHUNK : (k + 1) * PACK * CHUNK])

        def park_b(g, j0, banks, room):
            partial[g, j0] = room
            for pair in range(2):
                product_b(g, j0, pair, banks[pair])
                nc.scalar.copy(out=partial[g, j0][:, 2 * pair : 2 * pair + 2, :], in_=slices(banks[pair], 2))

        def parked_times_time(g, j0, step, room):
            parked = partial[g, j0]
            partial[g, j0] = room
            for c0 in range(0, CHUNK, step):
                cols = slice(c0, c0 + step)
                nc.gpsimd.tensor_tensor(room[:, :, cols], parked[:, :, cols], factors(g, j0 + c0, step), MULT)

        def pass_a(g, j0, a, b, t0, count):
            width = HALF // count
            for u in range(count):
                t = t0 + u
                nc.tensor.matmul_mx(
                    out=slices(b, count)[:, u, :],
                    lhsT=wp_w[g][a][:, P * t : P * (t + 1)].bitcast(FP8X4), lhsT_scale=wp_s[g][a][:, P * t : P * (t + 1)],
                    rhs=v_w[a][:, j0 : j0 + width].bitcast(FP8X4),
                    rhs_scale=v_s[TAB_ROW + 4 * a : P, j0 : j0 + width],
                    start=(a == 0 and u == 0), stop=(a == 1 and u == count - 1),
                )

        def h_at(g, j0):
            start = max(r for r in spans if r <= j0)
            return 2 * start + g * spans[start] + j0 - start

        def h_of(g, j0, width):
            w0 = h_at(g, j0) % HALF
            return h_bf[j0 // CHUNK][:, PACK * w0 : PACK * (w0 + width)]

        def bytes_of_factors(g, j0):
            return factors(g, j0, CHUNK).rearrange("p t n -> p (t n)").bitcast(BF16)

        def h_by_a(g, j0, b):
            pass_a(g, j0, 1, b, 0, PACK)
            nc.vector.tensor_tensor(woven(h_of(g, j0, NARROW)), in_fours(part(g, j0, NARROW)), in_fours(slices(b, PACK)), MULT)

        def a_times_parked(g, j0, pair, b):
            pass_a(g, j0, 1, b, 2 * pair, 2)
            rows = partial[g, j0][:, 2 * pair : 2 * pair + 2, :]
            nc.vector.tensor_tensor(rows, rows, slices(b, 2), MULT)

        def h_by_time(g, j0, width):
            nc.vector.tensor_tensor(woven(h_of(g, j0, width)), in_fours(part(g, j0, width)), in_fours(factors(g, j0, width)), MULT)

        def quantize_h(g, j0, count):
            w0 = h_at(g, j0)
            nc.vector.quantize_mx(out=h_w[:, w0 : w0 + count].bitcast(FP8X4), scales=h_s[:, w0 : w0 + count],
                                  in_=h_of(g, j0, count))

        def pass_z(j0, pair, b, g, start):
            width = runs[j0]
            z = bank[b][:, 0 : 2 * width].rearrange("p (u n) -> p u n", u=2)
            w0 = h_at(g, j0)
            for u in range(2):
                t = 2 * pair + u
                nc.tensor.matmul_mx(
                    out=z[:, u, :],
                    lhsT=wo_w[:, N * g + P * t : N * g + P * (t + 1)].bitcast(FP8X4),
                    lhsT_scale=wo_s[WO_ROW + 4 * g : P, P * t : P * (t + 1)],
                    rhs=h_w[:, w0 : w0 + width].bitcast(FP8X4), rhs_scale=h_s[:, w0 : w0 + width],
                    start=(start and u == 0), stop=(not start and u == 1),
                )
            return z

        def columns(raw, j0, width):
            c0 = j0 % CHUNK
            return half_of(raw[j0 // HALF], j0 % HALF // CHUNK)[:, :, c0 : c0 + width]

        def risk(j0, width):
            return columns(wp_raw[1], j0, width)

        def y(j0, width):
            return columns(wp_raw[0], j0, width)

        def make_risk(j0, pair, b, g):
            pass_z(j0, pair, b, 1 - g, True)
            z = pass_z(j0, pair, b, g, False)
            for u in range(2):
                t = 2 * pair + u
                nc.scalar.activation(risk(j0, runs[j0])[:, t, :], z[:, u, :], SIGMOID, bias=bias[:, t : t + 1])

        def weigh_on_scalar(dst, src, t):
            nc.scalar.activation(dst, src, COPY, scale=weight[:, t : t + 1])

        def weigh_on_vector(dst, src, t):
            nc.vector.tensor_scalar(dst, src, weight[:, t : t + 1], None, MULT)

        def make_y(j0, width, weigh, t0=0, t1=PACK):
            for t in range(t0, t1):
                weigh(y(j0, width)[:, t, :], risk(j0, width)[:, t, :], t)

        def store_y(j0, width, t0=0, t1=PACK):
            rows = out_0[:, j0 : j0 + width].rearrange("(p t) j -> p t j", t=PACK)
            nc.sync.dma_start(out=rows[:, t0:t1, :], in_=y(j0, width)[:, t0:t1, :])

        def round_y(j0, width, copy):
            copy(out=woven(y_bf[:, PACK * j0 : PACK * (j0 + width)]), in_=in_fours(y(j0, width)))

        def weigh_and_round(j0, width):
            nc.vector.tensor_tensor(
                woven(y_bf[:, PACK * j0 : PACK * (j0 + width)]),
                in_fours(risk(j0, width)),
                weight[:].unsqueeze(1).unsqueeze(3).to_broadcast([P, width // 4, PACK, 4]),
                MULT,
            )

        def quantize_y(j0, width):
            cols = slice(j0, j0 + width)
            nc.vector.quantize_mx(out=y_w[:, cols].bitcast(FP8X4), scales=y_s[:, cols],
                                  in_=y_bf[:, PACK * j0 : PACK * (j0 + width)])

        def store_words(queue, j0, width):
            cols = slice(j0, j0 + width)
            queue.dma_start(out=words(out_1[0])[:, cols], in_=y_w[:, cols].bitcast(I32))

        def store_scales(queue):
            for r in range(4):
                queue.dma_start(out=out_2[0, r:16:4, :].bitcast(I32), in_=y_s[r:P:32, :].bitcast(I32))

        on_scalar, on_vector = nc.scalar.copy, nc.vector.tensor_copy

        for plane in (tab_s, tab2_s, wd_s_raw, wo_s_raw):
            nc.vector.memset(plane[:].bitcast(I32), 0)

        load_table(tab2_w, tab2_words[0])
        nc.sync.dma_start(list2[:], offs2)
        load_scales_by_row(nc.sync, tab2_s, tab2_scales)
        load_wd()
        load_table(tab_w[0], tab_words[0])
        load_scales_by_row(nc.sync, wd_s_raw, wd_scales)
        nc.sync.dma_start(list1[:], offs)
        load_wp(0, 0)
        load_wp(0, 1)
        load_table(tab_w[1], tab_words[1])
        load_time(0, 0, CHUNK)
        load_scales(nc.sync, wo_s_raw, wo_scales, WO_ROW, 0)
        load_time(0, second, CHUNK)
        load_scales(nc.sync, wo_s_raw, wo_scales, WO_ROW, 1)
        load_wp(1, 0)
        load_scales(nc.sync, wo_s_raw, wo_scales, WO_ROW, 2)
        load_wp(1, 1)
        load_scales(nc.sync, wo_s_raw, wo_scales, WO_ROW, 3)
        load_time(1, 0, CHUNK)
        load_time(1, third, CHUNK)
        load_wo()
        load_by_slices(nc.sync, bias, bo)
        load_time(1, second, CHUNK)
        load_by_slices(nc.sync, weight, cost)
        load_time(1, fourth, CHUNK)
        load_time(0, third, CHUNK)
        load_time(0, fourth, CHUNK)
        for q in range(4):
            load_scales(nc.gpsimd, tab_s, tab_scales, TAB_ROW, q)
        h_bf = [held("h_bf%d" % k, [P, 2 * PACK * CHUNK], BF16)[:] for k in range(4)]

        gather(v2_w, tab2_w, list2, 0, S)
        gather(v2_s, tab2_s, list2, 0, S)
        deal(on_vector, wd_w[:].bitcast(U16), wd_raw[:].bitcast(U16), 8)
        deal(on_vector, wd_s[:], wd_s_raw[:], 16)
        gather(v_w[0], tab_w[0], list1, 0, S)
        gather(v_s, tab_s, list1, 0, S)
        round_wp(0, 0, on_scalar)
        quantize_wp(0, 0)
        round_wp(0, 1, on_scalar)
        quantize_wp(0, 1)
        park_b(0, third, (0, 1), new_room(0, third))
        park_b(0, fourth, (2, 3), new_room(0, fourth))
        park_b(0, 0, (4, 5), new_room(0, 0))
        park_b(0, second, (6, 7), new_room(0, second))
        for b in range(4):
            pass_a(0, third + b // 2 * CHUNK, 0, b, 2 * (b % 2), 2)
        park_b(1, third, (4, 5), new_room(1, third))
        park_b(1, fourth, (6, 7), new_room(1, fourth))
        gather(v_w[1], tab_w[1], list1, HALF, HALF)
        for b in range(4):
            a_times_parked(0, third + b // 2 * CHUNK, b % 2, b)
        for c in range(4):
            pass_a(0, c * NARROW, 0, 4 + c, 0, PACK)
        gather(v_w[1], tab_w[1], list1, 0, HALF)
        parked_times_time(0, 0, NARROW, partial[0, 0])
        parked_times_time(0, second, NARROW, partial[0, second])
        for c in range(4):
            h_by_a(0, c * NARROW, 4 + c)
        round_wp(1, 0, on_scalar)
        round_wp(1, 1, on_scalar)
        quantize_wp(1, 0)
        deal(on_vector, wo_s[:], wo_s_raw[:], 16)
        quantize_h(0, 0, CHUNK)
        b_times_time(1, 0, 0, 0, by_slices(late[:, 0 : PACK * CHUNK]))
        pass_a(1, 0, 0, 2, 0, PACK)
        pass_a(1, NARROW, 0, 3, 0, PACK)
        pass_a(1, second, 0, 6, 0, PACK)
        quantize_wp(1, 1)
        b_times_time(1, 0, 1, 1, by_slices(late[:, 0 : PACK * CHUNK]))
        deal(on_scalar, wo_w[:], wo_raw[:], 4)
        parked_times_time(1, third, NARROW, by_slices(shared[:]))
        h_by_a(1, 0, 2)
        h_by_a(1, NARROW, 3)
        b_times_time(1, second, 0, 4, factors(1, second, CHUNK))
        quantize_h(1, 0, CHUNK)
        parked_times_time(1, fourth, NARROW, by_slices(h_bf[0].bitcast(F32)))
        make_risk(0, 0, 0, 1)
        make_risk(0, 1, 7, 1)
        make_y(0, CHUNK, weigh_on_scalar)
        store_y(0, CHUNK)
        round_y(0, CHUNK, on_scalar)
        b_times_time(1, second, 1, 5, factors(1, second, CHUNK))
        h_by_a(1, second, 6)
        pass_a(1, second + NARROW, 0, 1, 0, PACK)
        h_by_a(1, second + NARROW, 1)
        pass_a(1, third, 0, 2, 0, PACK)
        h_by_a(1, third, 2)
        quantize_h(0, second, HALF)
        make_risk(second, 0, 4, 1)
        make_risk(second, 1, 5, 1)
        make_y(second, CHUNK, weigh_on_scalar)
        store_y(second, CHUNK)
        pass_a(1, third + NARROW, 0, 3, 0, PACK)
        h_by_a(1, third + NARROW, 3)
        h_by_time(0, third, CHUNK)
        pass_a(1, fourth, 0, 6, 0, PACK)
        h_by_a(1, fourth, 6)
        quantize_h(0, third, HALF)
        make_risk(third, 0, 0, 1)
        make_y(third, CHUNK, weigh_on_scalar, 0, 2)
        store_y(third, CHUNK, 0, 2)
        make_risk(third, 1, 1, 1)
        h_by_time(0, fourth, NARROW)
        pass_a(1, last, 0, 7, 0, PACK)
        h_by_a(1, last, 7)
        quantize_h(0, fourth, CHUNK)
        make_risk(fourth, 0, 2, 1)
        make_risk(fourth, 1, 3, 1)
        h_by_time(0, last, NARROW)
        quantize_y(0, CHUNK)
        store_words(nc.sync, 0, CHUNK)
        quantize_h(0, last, CHUNK)
        make_risk(last, 0, 4, 1)
        make_risk(last, 1, 5, 1)
        make_y(third, CHUNK, weigh_on_vector, 2, 4)
        store_y(third, CHUNK, 2, 4)
        round_y(second, CHUNK, on_vector)
        round_y(third, CHUNK, on_vector)
        weigh_and_round(fourth, NARROW)
        make_y(fourth, CHUNK, weigh_on_scalar, 0, 2)
        store_y(fourth, CHUNK, 0, 2)
        make_y(fourth, CHUNK, weigh_on_scalar, 2, 4)
        store_y(fourth, CHUNK, 2, 4)
        quantize_y(second, HALF)
        store_words(nc.sync, second, HALF)
        weigh_and_round(last, NARROW)
        quantize_y(fourth, CHUNK)
        store_words(nc.sync, fourth, CHUNK)
        store_scales(nc.scalar)
